import numpy as np
import ml_dtypes


def mxq(x, axis, fmt="e4m3"):
    dtype, down = {"e4m3": (ml_dtypes.float8_e4m3fn, 7), "e5m2": (ml_dtypes.float8_e5m2, 14)}[fmt]
    v = np.moveaxis(np.asarray(x, np.float32).astype(ml_dtypes.bfloat16).astype(np.float64), axis, -1)
    blocks = v.reshape(v.shape[:-1] + (-1, 32))
    amax = np.abs(blocks).max(-1, keepdims=True)
    byte = np.maximum(np.where(amax > 0, np.frexp(amax)[1] - 1 + 127, 0) - down, 1)
    scale = np.exp2(byte - 127.0)
    codes = (blocks / scale).astype(np.float32).astype(dtype).astype(np.float64)
    return np.moveaxis((codes * scale).reshape(v.shape), -1, axis)


WIDE = False


def mx_kscale(k):
    if not WIDE:
        return np.ones(k)
    levels = np.array([10, -10, 5, -5, 0])
    if k % 512:
        return np.exp2(np.random.permutation(np.resize(levels, k // 32))).repeat(32)
    a = np.empty((k // 512, 16))
    for p in range(k // 512):
        a[p, :8] = np.random.permutation(np.resize(levels, 8))
        for g in range(8):
            far = levels[np.abs(levels - a[p, g]) >= 10]
            a[p, g + 8] = far[np.random.randint(len(far))]
    return np.exp2(a.ravel()).repeat(32)


def f64(x):
    return np.asarray(x).astype(np.float64)


def striped(idx):
    return np.tile(np.asarray(idx).reshape(-1, 16).T, (8, 1)).astype(np.uint16)


def unstriped(offs):
    return offs[:16].T.reshape(-1).astype(np.int64)


E2M1 = np.array([0.0, 0.5, 1.0, 1.5, 2.0, 3.0, 4.0, 6.0, -0.0, -0.5, -1.0, -1.5, -2.0, -3.0, -4.0, -6.0])


def pack_weight(w, fmt):
    k, n = w.shape
    w = f64(np.asarray(w, np.float32).astype(ml_dtypes.bfloat16)).reshape(k // 32, 32, n)
    amax = np.abs(w).max(1)
    if fmt == "e4m3":
        byte = np.frexp(amax)[1] - 1 + 127 - 7
    else:
        mant, ex = np.frexp(amax / 6.0)
        byte = np.where(mant > 0.5, ex, ex - 1) + 127
    byte = np.clip(np.where(amax > 0, byte, 1), 1, 254)
    scaled = (w * np.exp2(127.0 - byte)[:, None, :]).reshape(k, n).astype(np.float32)
    by_word = np.ascontiguousarray(scaled.reshape(k // 512, 128, 4, n).transpose(0, 1, 3, 2))
    if fmt == "e4m3":
        words = by_word.astype(ml_dtypes.float8_e4m3fn).view(np.uint8)
    else:
        c = by_word.astype(ml_dtypes.float4_e2m1fn).view(np.uint8) & 0xF
        words = (c[..., 0::2] | (c[..., 1::2] << 4)).reshape(k // 512, 128, 2 * n)
    return np.ascontiguousarray(words), np.ascontiguousarray(byte.astype(np.uint8).reshape(k // 512, 16, n))


def unpack_weight(words, scales, fmt):
    g, _, n = scales.shape
    words = np.ascontiguousarray(words).reshape(g, 128, n, -1)
    if fmt == "e4m3":
        vals = words.view(ml_dtypes.float8_e4m3fn).astype(np.float64)
    else:
        nib = np.empty((g, 128, n, 4), np.uint8)
        nib[..., 0::2] = words & 0xF
        nib[..., 1::2] = words >> 4
        vals = E2M1[nib]
    vals = vals * np.repeat(np.exp2(scales.astype(np.float64) - 127.0), 8, axis=1)[..., None]
    return vals.transpose(0, 1, 3, 2).reshape(g * 512, n)


D, T, U, Q, V, I = 512, 1024, 512, 256, 2048, 512


def setup_inputs():
    n = np.random.standard_normal
    idx = np.random.permutation(T)[:Q]
    idx2 = np.random.randint(0, U, Q)
    idx3 = np.random.permutation(V)[:I]
    fd = mx_kscale(D)
    trep = pack_weight(n((D, V)) / fd[:, None], "e2m1")
    timp = pack_weight(n((D, V)) / fd[:, None], "e2m1")
    return {
        "hre": (n((D, T)) * 0.1 * fd[:, None]).astype(np.float32),
        "him": (n((D, T)) * 0.1 * fd[:, None]).astype(np.float32),
        "rre": (n((D, U)) * 0.6).astype(np.float32),
        "rim": (n((D, U)) * 0.6).astype(np.float32),
        "tre_words": trep[0],
        "tre_scales": trep[1],
        "tim_words": timp[0],
        "tim_scales": timp[1],
        "offs": striped(idx),
        "offs2": striped(idx2),
        "offs3": striped(idx3),
    }


def reference(hre, him, rre, rim, tre_words, tre_scales, tim_words, tim_scales, offs, offs2, offs3):
    idx = unstriped(offs)
    idx2 = unstriped(offs2)
    idx3 = unstriped(offs3)
    treu = unpack_weight(tre_words, tre_scales, "e2m1")
    timu = unpack_weight(tim_words, tim_scales, "e2m1")
    x = f64(hre)[:, idx] * f64(rre)[:, idx2] - f64(him)[:, idx] * f64(rim)[:, idx2]
    z = f64(hre)[:, idx] * f64(rim)[:, idx2] + f64(him)[:, idx] * f64(rre)[:, idx2]
    xq = mxq(x, 0, "e4m3")
    treidx3g = treu[:, idx3]
    zq = mxq(z, 0, "e4m3")
    timidx3g = timu[:, idx3]
    y = xq.T @ treidx3g + zq.T @ timidx3g
    return y

@@ -1,0 +1,134 @@
+from contextlib import ExitStack
+
+import concourse.mybir as mybir
+from concourse.masks import make_identity
+
+D, T, U, Q, V, I = 512, 1024, 512, 256, 2048, 512
+FLOPS = 2 * 2 * D * Q * I
+
+F32 = mybir.dt.float32
+BF16 = mybir.dt.bfloat16
+I32 = mybir.dt.int32
+U32 = mybir.dt.uint32
+U16 = mybir.dt.uint16
+U8 = mybir.dt.uint8
+FP8X4 = mybir.dt.float8_e4m3fn_x4
+FP4X4 = mybir.dt.float4_e2m1fn_x4
+MULT = mybir.AluOpType.mult
+
+P = 128
+SLABS = D // P
+QB = Q // P
+
+
+def tile_attend_complexscores_kernel(tc, hre, him, rre, rim, tre_words, tre_scales, tim_words, tim_scales, offs, offs2, offs3, out):
+    nc = tc.nc
+    with ExitStack() as ctx:
+        lists = ctx.enter_context(tc.tile_pool(name="lists", bufs=1))
+        keep = ctx.enter_context(tc.tile_pool(name="keep", bufs=1))
+        psum = ctx.enter_context(tc.psum_pool(name="psum", bufs=1))
+
+        head_list = lists.tile([P, Q // 16], U16, name="head_list")
+        rel_list = lists.tile([P, Q // 16], U16, name="rel_list")
+        tail_list = lists.tile([P, I // 16], U16, name="tail_list")
+
+        ident = keep.tile([P, P], F32, name="ident")
+        make_identity(nc, ident[:])
+
+        scale_pool = [keep.tile([P, V], U8, name="scale_pool%d" % c) for c in range(2)]
+        for c in range(2):
+            nc.gpsimd.memset(scale_pool[c][:].bitcast(I32), 0)
+        word_pool = [keep.tile([P, V], U16, name="word_pool%d" % c) for c in range(2)]
+
+        rel_first = [keep.tile([P, U], F32, name="rel_first%d" % c) for c in range(2)]
+        rel_rest = [keep.tile([P, SLABS - 1, U], F32, name="rel_rest%d" % c) for c in range(2)]
+        head_pool = [[keep.tile([P, T], F32, name="head_pool%d_%d" % (c, j)) for j in range(SLABS)] for c in range(2)]
+
+        rels = (rre, rim)
+        heads = (hre, him)
+        nc.sync.dma_start(rel_list[:], offs2)
+        for c in range(2):
+            nc.sync.dma_start(rel_first[c][:], rels[c][0:P, :])
+        nc.sync.dma_start(head_list[:], offs)
+        for c in range(2):
+            nc.sync.dma_start(head_pool[c][0][:], heads[c][0:P, :])
+        for c in range(2):
+            nc.sync.dma_start(rel_rest[c][:], rels[c][P:D, :].rearrange("(j p) u -> p j u", p=P))
+        nc.sync.dma_start(tail_list[:], offs3)
+        for j in range(1, SLABS):
+            for c in range(2):
+                nc.sync.dma_start(head_pool[c][j][:], heads[c][j * P : (j + 1) * P, :])
+        for c, scales in enumerate((tre_scales, tim_scales)):
+            for r in range(4):
+                nc.sync.dma_start(scale_pool[c][r:P:32, :].bitcast(I32), scales[0, r:16:4, :].bitcast(I32))
+        for c, words in enumerate((tre_words, tim_words)):
+            nc.sync.dma_start(word_pool[c][:].bitcast(I32), words[0].bitcast(I32))
+
+        by_query = [keep.tile([P, 2, 2, P, 2], BF16, name="by_query%d" % b, align_bytes=64) for b in range(QB)]
+
+        for j in range(SLABS):
+            rel = keep.tile([P, 3, Q], F32, name="rel%d" % j)
+            for c in range(2):
+                window = rel_first[c][:] if j == 0 else rel_rest[c][:, j - 1, :]
+                nc.vector.tensor_copy(rel[:, 1 + c, :], window.indirect(rel_list[:]))
+            nc.scalar.mul(rel[:, 0, :], rel[:, 2, :], -1.0)
+            prods = []
+            for c in range(2):
+                head = keep.tile([P, 1, Q], F32, name="head%d_%d" % (c, j))
+                nc.vector.tensor_copy(head[:, 0, :], head_pool[c][j][:].indirect(head_list[:]))
+                prod = keep.tile([P, 2, Q], F32, name="prod%d_%d" % (c, j))
+                nc.vector.tensor_tensor(prod[:], rel[:, 1 - c : 3 - c, :], head[:].to_broadcast([P, 2, Q]), MULT)
+                prods.append(prod)
+            for b in range(QB):
+                sums = psum.tile([P, 2, P], F32, name="sums%d_%d" % (j, b), tag="sums%d" % b, bufs=2)
+                for s in range(2):
+                    for c in range(2):
+                        nc.tensor.matmul(sums[:, s, :], lhsT=prods[c][:, s, b * P : (b + 1) * P], rhs=ident[:], is_transpose=True, start=(c == 0), stop=(c == 1))
+                nc.scalar.copy(
+                    by_query[b][:, :, :, 32 * j : 32 * (j + 1), :].rearrange("q s u p e -> q u s p e"),
+                    sums[:].rearrange("q s (p u e) -> q u s p e", u=2, e=2),
+                )
+
+        tail_scales = []
+        tail_words = []
+        for c in range(2):
+            picked = keep.tile([P, I], U8, name="tail_scales%d" % c, align_bytes=64)
+            nc.vector.tensor_copy(picked[:], scale_pool[c][:].indirect(tail_list[:]))
+            tail_scales.append(picked)
+        for c in range(2):
+            picked = keep.tile([P, I], U16, name="tail_words%d" % c, align_bytes=64)
+            nc.vector.tensor_copy(picked[:], word_pool[c][:].indirect(tail_list[:]))
+            tail_words.append(picked)
+
+        for b in range(QB):
+            pairs = by_query[b][:].rearrange("q s u p e -> q (s u p e)").bitcast(F32)
+            turned = psum.tile([P, 2, 2, P], F32, name="turned%d" % b)
+            for s in range(2):
+                for u in range(2):
+                    lo = (2 * s + u) * P
+                    nc.tensor.transpose(turned[:, s, u, :], pairs[:, lo : lo + P], ident[:])
+            grouped = keep.tile([P, 2 * P * 4], BF16, name="grouped%d" % b, align_bytes=64)
+            nc.scalar.copy(
+                grouped[:].bitcast(F32).rearrange("p (s q u) -> p s q u", s=2, u=2),
+                turned[:].rearrange("p s u q -> p s q u"),
+            )
+            codes = keep.tile([P, 2 * P], U32, name="codes%d" % b, align_bytes=64)
+            plane = keep.tile([P, 2 * P], U8, name="plane%d" % b, align_bytes=64)
+            nc.vector.quantize_mx(out=codes[:].bitcast(FP8X4), scales=plane[:], in_=grouped[:])
+            acc = psum.tile([P, I], F32, name="acc%d" % b)
+            for s in range(2):
+                nc.tensor.matmul_mx(
+                    out=acc[:],
+                    lhsT=codes[:, s * P : (s + 1) * P].bitcast(FP8X4),
+                    lhsT_scale=plane[:, s * P : (s + 1) * P],
+                    rhs=tail_words[s][:].bitcast(FP4X4),
+                    rhs_scale=tail_scales[s][:],
+                    start=(s == 0),
+                    stop=(s == 1),
+                )
+            result = keep.tile([P, I], F32, name="result%d" % b)
+            if b == 0:
+                nc.scalar.copy(result[:], acc[:])
+            else:
+                nc.vector.tensor_copy(result[:], acc[:])
+            nc.sync.dma_start(out[b * P : (b + 1) * P, :], result[:])

@@ -32,103 +32,107 @@ def tile_attend_complexscores_kernel(tc, hre, him, rre, rim, tre_words, tre_scal
         rel_list = lists.tile([P, Q // 16], U16, name="rel_list")
         tail_list = lists.tile([P, I // 16], U16, name="tail_list")
 
+        scale_pool = [keep.tile([P, V], U8, name="scale_pool%d" % c) for c in range(2)]
+        for c in range(2):
+            nc.vector.memset(scale_pool[c][:].bitcast(I32), 0)
+        tail_plane = keep.tile([P, 2 * I], U8, name="tail_plane", align_bytes=64)
+        nc.gpsimd.memset(tail_plane[:].bitcast(I32), 0)
         ident = keep.tile([P, P], F32, name="ident")
         make_identity(nc, ident[:])
 
-        scale_pool = [keep.tile([P, V], U8, name="scale_pool%d" % c) for c in range(2)]
-        for c in range(2):
-            nc.gpsimd.memset(scale_pool[c][:].bitcast(I32), 0)
         word_pool = [keep.tile([P, V], U16, name="word_pool%d" % c) for c in range(2)]
-
-        rel_first = [keep.tile([P, U], F32, name="rel_first%d" % c) for c in range(2)]
-        rel_rest = [keep.tile([P, SLABS - 1, U], F32, name="rel_rest%d" % c) for c in range(2)]
+        rel_pool = [[keep.tile([P, U], F32, name="rel_pool%d_%d" % (c, j)) for j in range(SLABS)] for c in range(2)]
         head_pool = [[keep.tile([P, T], F32, name="head_pool%d_%d" % (c, j)) for j in range(SLABS)] for c in range(2)]
 
-        rels = (rre, rim)
-        heads = (hre, him)
         nc.sync.dma_start(rel_list[:], offs2)
-        for c in range(2):
-            nc.sync.dma_start(rel_first[c][:], rels[c][0:P, :])
-        nc.sync.dma_start(head_list[:], offs)
-        for c in range(2):
-            nc.sync.dma_start(head_pool[c][0][:], heads[c][0:P, :])
-        for c in range(2):
-            nc.sync.dma_start(rel_rest[c][:], rels[c][P:D, :].rearrange("(j p) u -> p j u", p=P))
-        nc.sync.dma_start(tail_list[:], offs3)
-        for j in range(1, SLABS):
-            for c in range(2):
-                nc.sync.dma_start(head_pool[c][j][:], heads[c][j * P : (j + 1) * P, :])
-        for c, scales in enumerate((tre_scales, tim_scales)):
-            for r in range(4):
-                nc.sync.dma_start(scale_pool[c][r:P:32, :].bitcast(I32), scales[0, r:16:4, :].bitcast(I32))
+        for j in range(SLABS):
+            rows = slice(j * P, (j + 1) * P)
+            for c, table in enumerate((rre, rim)):
+                nc.sync.dma_start(rel_pool[c][j][:], table[rows, :])
+            if j == 0:
+                nc.sync.dma_start(tail_list[:], offs3)
+                nc.sync.dma_start(scale_pool[0][0:P:8, :].bitcast(I32), tre_scales[0].bitcast(I32))
+                nc.sync.dma_start(head_list[:], offs)
+            for c, table in enumerate((hre, him)):
+                nc.sync.dma_start(head_pool[c][j][:], table[rows, :])
+            if j == 0:
+                nc.sync.dma_start(scale_pool[1][0:P:8, :].bitcast(I32), tim_scales[0].bitcast(I32))
         for c, words in enumerate((tre_words, tim_words)):
             nc.sync.dma_start(word_pool[c][:].bitcast(I32), words[0].bitcast(I32))
 
-        by_query = [keep.tile([P, 2, 2, P, 2], BF16, name="by_query%d" % b, align_bytes=64) for b in range(QB)]
+        units = [(b, s) for s in range(2) for b in range(QB)]
+        by_query = {(b, s): keep.tile([P, 2, P, 2], BF16, name="by_query%d_%d" % (b, s), tag="by_query%d_%d" % (b, s), align_bytes=64) for b, s in units}
 
         for j in range(SLABS):
             rel = keep.tile([P, 3, Q], F32, name="rel%d" % j)
             for c in range(2):
-                window = rel_first[c][:] if j == 0 else rel_rest[c][:, j - 1, :]
-                nc.vector.tensor_copy(rel[:, 1 + c, :], window.indirect(rel_list[:]))
+                nc.vector.tensor_copy(rel[:, 1 + c, :], rel_pool[c][j][:].indirect(rel_list[:]))
             nc.scalar.mul(rel[:, 0, :], rel[:, 2, :], -1.0)
             prods = []
             for c in range(2):
                 head = keep.tile([P, 1, Q], F32, name="head%d_%d" % (c, j))
                 nc.vector.tensor_copy(head[:, 0, :], head_pool[c][j][:].indirect(head_list[:]))
-                prod = keep.tile([P, 2, Q], F32, name="prod%d_%d" % (c, j))
-                nc.vector.tensor_tensor(prod[:], rel[:, 1 - c : 3 - c, :], head[:].to_broadcast([P, 2, Q]), MULT)
-                prods.append(prod)
-            for b in range(QB):
-                sums = psum.tile([P, 2, P], F32, name="sums%d_%d" % (j, b), tag="sums%d" % b, bufs=2)
-                for s in range(2):
-                    for c in range(2):
-                        nc.tensor.matmul(sums[:, s, :], lhsT=prods[c][:, s, b * P : (b + 1) * P], rhs=ident[:], is_transpose=True, start=(c == 0), stop=(c == 1))
+                if (j, c) == (SLABS - 1, 1):
+                    prod = [keep.tile([P, 2, P], F32, name="prod%d_%d_%d" % (c, j, b)) for b in range(QB)]
+                    prods.append(prod)
+                    for b in range(QB):
+                        cols = slice(b * P, (b + 1) * P)
+                        nc.vector.tensor_tensor(prod[b][:], rel[:, 0:2, cols], head[:, :, cols].to_broadcast([P, 2, P]), MULT)
+                else:
+                    whole = keep.tile([P, 2, Q], F32, name="whole%d_%d" % (c, j))
+                    nc.gpsimd.tensor_tensor(whole[:], rel[:, 1 - c : 3 - c, :], head[:].to_broadcast([P, 2, Q]), MULT)
+                    prods.append([whole[:, :, b * P : (b + 1) * P] for b in range(QB)])
+            sums = {}
+            for c in range(2):
+                for b in range(QB):
+                    for s in range(2):
+                        if c == 0:
+                            sums[b, s] = psum.tile([P, P], F32, name="sums%d_%d_%d" % (j, b, s), tag="bank%d" % (2 * s + b))
+                        nc.tensor.matmul(sums[b, s][:], lhsT=prods[c][b][:, s, :], rhs=ident[:], is_transpose=True, start=(c == 0), stop=(c == 1))
+            for b, s in units:
                 nc.scalar.copy(
-                    by_query[b][:, :, :, 32 * j : 32 * (j + 1), :].rearrange("q s u p e -> q u s p e"),
-                    sums[:].rearrange("q s (p u e) -> q u s p e", u=2, e=2),
+                    by_query[b, s][:, :, 32 * j : 32 * (j + 1), :],
+                    sums[b, s][:].rearrange("q (p u e) -> q u p e", u=2, e=2),
                 )
+            if j == 0:
+                picked = keep.tile([P, 2 * I], U8, name="picked_scales")
+                for c in range(2):
+                    nc.vector.tensor_copy(picked[:, c * I : (c + 1) * I], scale_pool[c][:].indirect(tail_list[:]))
+                for r in range(4):
+                    nc.scalar.dma_start(tail_plane[r:P:32, :].bitcast(I32), picked[8 * r : P : 32, :].bitcast(I32))
 
-        tail_scales = []
         tail_words = []
         for c in range(2):
-            picked = keep.tile([P, I], U8, name="tail_scales%d" % c, align_bytes=64)
-            nc.vector.tensor_copy(picked[:], scale_pool[c][:].indirect(tail_list[:]))
-            tail_scales.append(picked)
-        for c in range(2):
-            picked = keep.tile([P, I], U16, name="tail_words%d" % c, align_bytes=64)
-            nc.vector.tensor_copy(picked[:], word_pool[c][:].indirect(tail_list[:]))
-            tail_words.append(picked)
+            tail_words.append(keep.tile([P, I], U16, name="tail_words%d" % c, align_bytes=64))
+            nc.vector.tensor_copy(tail_words[c][:], word_pool[c][:].indirect(tail_list[:]))
 
-        for b in range(QB):
-            pairs = by_query[b][:].rearrange("q s u p e -> q (s u p e)").bitcast(F32)
-            turned = psum.tile([P, 2, 2, P], F32, name="turned%d" % b)
-            for s in range(2):
-                for u in range(2):
-                    lo = (2 * s + u) * P
-                    nc.tensor.transpose(turned[:, s, u, :], pairs[:, lo : lo + P], ident[:])
-            grouped = keep.tile([P, 2 * P * 4], BF16, name="grouped%d" % b, align_bytes=64)
-            nc.scalar.copy(
-                grouped[:].bitcast(F32).rearrange("p (s q u) -> p s q u", s=2, u=2),
-                turned[:].rearrange("p s u q -> p s q u"),
+        acc = [psum.tile([P, I], F32, name="acc%d" % b, tag="bank%d" % b) for b in range(QB)]
+        grouped = {}
+        for b, s in units:
+            pairs = by_query[b, s][:].rearrange("q u p e -> q (u p e)").bitcast(F32)
+            turned = psum.tile([P, 2, P], F32, name="turned%d_%d" % (b, s))
+            for u in range(2):
+                nc.tensor.transpose(turned[:, u, :], pairs[:, u * P : (u + 1) * P], ident[:])
+            grouped[b, s] = keep.tile([P, P * 4], BF16, name="grouped%d_%d" % (b, s), align_bytes=64)
+            nc.scalar.copy(grouped[b, s][:].bitcast(F32).rearrange("p (q u) -> p q u", u=2), turned[:].rearrange("p u q -> p q u"))
+        for n, (b, s) in enumerate(units):
+            codes = keep.tile([P, P], U32, name="codes%d_%d" % (b, s), tag="by_query%d_%d" % units[-1 - n], align_bytes=64)
+            plane = keep.tile([P, P], U8, name="plane%d_%d" % (b, s), align_bytes=64)
+            nc.vector.quantize_mx(out=codes[:].bitcast(FP8X4), scales=plane[:], in_=grouped[b, s][:])
+            nc.tensor.matmul_mx(
+                out=acc[b][:],
+                lhsT=codes[:].bitcast(FP8X4),
+                lhsT_scale=plane[:],
+                rhs=tail_words[s][:].bitcast(FP4X4),
+                rhs_scale=tail_plane[:, s * I : (s + 1) * I],
+                start=(s == 0),
+                stop=(s == 1),
             )
-            codes = keep.tile([P, 2 * P], U32, name="codes%d" % b, align_bytes=64)
-            plane = keep.tile([P, 2 * P], U8, name="plane%d" % b, align_bytes=64)
-            nc.vector.quantize_mx(out=codes[:].bitcast(FP8X4), scales=plane[:], in_=grouped[:])
-            acc = psum.tile([P, I], F32, name="acc%d" % b)
-            for s in range(2):
-                nc.tensor.matmul_mx(
-                    out=acc[:],
-                    lhsT=codes[:, s * P : (s + 1) * P].bitcast(FP8X4),
-                    lhsT_scale=plane[:, s * P : (s + 1) * P],
-                    rhs=tail_words[s][:].bitcast(FP4X4),
-                    rhs_scale=tail_scales[s][:],
-                    start=(s == 0),
-                    stop=(s == 1),
-                )
-            result = keep.tile([P, I], F32, name="result%d" % b)
-            if b == 0:
-                nc.scalar.copy(result[:], acc[:])
-            else:
-                nc.vector.tensor_copy(result[:], acc[:])
-            nc.sync.dma_start(out[b * P : (b + 1) * P, :], result[:])
+        result = keep.tile([P, I], F32, name="result0")
+        nc.scalar.copy(result[:], acc[0][:])
+        nc.sync.dma_start(out[0:P, :], result[:])
+        for h in range(2):
+            cols = slice(h * I // 2, (h + 1) * I // 2)
+            half = keep.tile([P, I // 2], F32, name="half%d" % h)
+            nc.vector.tensor_copy(half[:], acc[1][:, cols])
+            nc.sync.dma_start(out[P:Q, cols], half[:])

@@ -18,7 +18,15 @@ MULT = mybir.AluOpType.mult
 
 P = 128
 SLABS = D // P
-QB = Q // P
+BLOCKS = Q // P
+PARTS = 2
+PACK = 4
+LIST_GROUP = 16
+QUADRANT = 32
+SCALE_ROWS = D // 32
+SPREAD = P // SCALE_ROWS
+SLAB_WORDS = P // PACK
+MX_ALIGN = 64
 
 
 def tile_attend_complexscores_kernel(tc, hre, him, rre, rim, tre_words, tre_scales, tim_words, tim_scales, offs, offs2, offs3, out):
@@ -28,111 +36,117 @@ def tile_attend_complexscores_kernel(tc, hre, him, rre, rim, tre_words, tre_scal
         keep = ctx.enter_context(tc.tile_pool(name="keep", bufs=1))
         psum = ctx.enter_context(tc.psum_pool(name="psum", bufs=1))
 
-        head_list = lists.tile([P, Q // 16], U16, name="head_list")
-        rel_list = lists.tile([P, Q // 16], U16, name="rel_list")
-        tail_list = lists.tile([P, I // 16], U16, name="tail_list")
+        head_list = lists.tile([P, Q // LIST_GROUP], U16, name="head_list")
+        rel_list = lists.tile([P, Q // LIST_GROUP], U16, name="rel_list")
+        tail_list = lists.tile([P, I // LIST_GROUP], U16, name="tail_list")
 
-        scale_pool = [keep.tile([P, V], U8, name="scale_pool%d" % c) for c in range(2)]
-        for c in range(2):
-            nc.vector.memset(scale_pool[c][:].bitcast(I32), 0)
-        tail_plane = keep.tile([P, 2 * I], U8, name="tail_plane", align_bytes=64)
-        nc.gpsimd.memset(tail_plane[:].bitcast(I32), 0)
+        scale_table = [keep.tile([P, V], U8, name="scale_table%d" % c) for c in range(PARTS)]
+        for c in range(PARTS):
+            nc.vector.memset(scale_table[c][:].bitcast(I32), 0)
+        tail_scales = keep.tile([P, PARTS * I], U8, name="tail_scales", align_bytes=MX_ALIGN)
+        nc.gpsimd.memset(tail_scales[:].bitcast(I32), 0)
         ident = keep.tile([P, P], F32, name="ident")
         make_identity(nc, ident[:])
 
-        word_pool = [keep.tile([P, V], U16, name="word_pool%d" % c) for c in range(2)]
-        rel_pool = [[keep.tile([P, U], F32, name="rel_pool%d_%d" % (c, j)) for j in range(SLABS)] for c in range(2)]
-        head_pool = [[keep.tile([P, T], F32, name="head_pool%d_%d" % (c, j)) for j in range(SLABS)] for c in range(2)]
+        word_table = [keep.tile([P, V], U16, name="word_table%d" % c, tag="word_table%d" % c, align_bytes=MX_ALIGN) for c in range(PARTS)]
+        rel_table = [[keep.tile([P, U], F32, name="rel_table%d_%d" % (c, j)) for j in range(SLABS)] for c in range(PARTS)]
+        head_table = [[keep.tile([P, T], F32, name="head_table%d_%d" % (c, j)) for j in range(SLABS)] for c in range(PARTS)]
 
         nc.sync.dma_start(rel_list[:], offs2)
         for j in range(SLABS):
             rows = slice(j * P, (j + 1) * P)
             for c, table in enumerate((rre, rim)):
-                nc.sync.dma_start(rel_pool[c][j][:], table[rows, :])
+                nc.sync.dma_start(rel_table[c][j][:], table[rows, :])
             if j == 0:
                 nc.sync.dma_start(tail_list[:], offs3)
-                nc.sync.dma_start(scale_pool[0][0:P:8, :].bitcast(I32), tre_scales[0].bitcast(I32))
+                nc.sync.dma_start(scale_table[0][0:P:SPREAD, :].bitcast(I32), tre_scales[0].bitcast(I32))
                 nc.sync.dma_start(head_list[:], offs)
             for c, table in enumerate((hre, him)):
-                nc.sync.dma_start(head_pool[c][j][:], table[rows, :])
+                nc.sync.dma_start(head_table[c][j][:], table[rows, :])
             if j == 0:
-                nc.sync.dma_start(scale_pool[1][0:P:8, :].bitcast(I32), tim_scales[0].bitcast(I32))
-        for c, words in enumerate((tre_words, tim_words)):
-            nc.sync.dma_start(word_pool[c][:].bitcast(I32), words[0].bitcast(I32))
+                nc.sync.dma_start(scale_table[1][0:P:SPREAD, :].bitcast(I32), tim_scales[0].bitcast(I32))
+        for c, table in enumerate((tre_words, tim_words)):
+            nc.sync.dma_start(word_table[c][:].bitcast(I32), table[0].bitcast(I32))
 
-        units = [(b, s) for s in range(2) for b in range(QB)]
-        by_query = {(b, s): keep.tile([P, 2, P, 2], BF16, name="by_query%d_%d" % (b, s), tag="by_query%d_%d" % (b, s), align_bytes=64) for b, s in units}
+        units = [(b, s) for b in range(BLOCKS) for s in range(PARTS)]
+        by_query = {(b, s): keep.tile([P, 2, P, 2], BF16, name="by_query%d_%d" % (b, s), align_bytes=MX_ALIGN) for b, s in units}
 
         for j in range(SLABS):
             rel = keep.tile([P, 3, Q], F32, name="rel%d" % j)
-            for c in range(2):
-                nc.vector.tensor_copy(rel[:, 1 + c, :], rel_pool[c][j][:].indirect(rel_list[:]))
+            for c in range(PARTS):
+                nc.vector.tensor_copy(rel[:, 1 + c, :], rel_table[c][j][:].indirect(rel_list[:]))
             nc.scalar.mul(rel[:, 0, :], rel[:, 2, :], -1.0)
-            prods = []
-            for c in range(2):
+
+            terms = []
+            for c in range(PARTS):
                 head = keep.tile([P, 1, Q], F32, name="head%d_%d" % (c, j))
-                nc.vector.tensor_copy(head[:, 0, :], head_pool[c][j][:].indirect(head_list[:]))
-                if (j, c) == (SLABS - 1, 1):
-                    prod = [keep.tile([P, 2, P], F32, name="prod%d_%d_%d" % (c, j, b)) for b in range(QB)]
-                    prods.append(prod)
-                    for b in range(QB):
-                        cols = slice(b * P, (b + 1) * P)
-                        nc.vector.tensor_tensor(prod[b][:], rel[:, 0:2, cols], head[:, :, cols].to_broadcast([P, 2, P]), MULT)
+                nc.vector.tensor_copy(head[:, 0, :], head_table[c][j][:].indirect(head_list[:]))
+                if (j, c) == (SLABS - 1, PARTS - 1):
+                    terms.append([keep.tile([P, PARTS, P], F32, name="last_term%d" % b) for b in range(BLOCKS)])
+                    for b in range(BLOCKS):
+                        queries = slice(b * P, (b + 1) * P)
+                        nc.vector.tensor_tensor(terms[c][b][:], rel[:, 0:2, queries], head[:, :, queries].to_broadcast([P, PARTS, P]), MULT)
                 else:
-                    whole = keep.tile([P, 2, Q], F32, name="whole%d_%d" % (c, j))
-                    nc.gpsimd.tensor_tensor(whole[:], rel[:, 1 - c : 3 - c, :], head[:].to_broadcast([P, 2, Q]), MULT)
-                    prods.append([whole[:, :, b * P : (b + 1) * P] for b in range(QB)])
+                    term = keep.tile([P, PARTS, Q], F32, name="term%d_%d" % (c, j))
+                    nc.gpsimd.tensor_tensor(term[:], rel[:, 1 - c : 3 - c, :], head[:].to_broadcast([P, PARTS, Q]), MULT)
+                    terms.append([term[:, :, b * P : (b + 1) * P] for b in range(BLOCKS)])
+
             sums = {}
-            for c in range(2):
-                for b in range(QB):
-                    for s in range(2):
+            for b in range(BLOCKS):
+                for c in range(PARTS):
+                    for s in range(PARTS):
                         if c == 0:
-                            sums[b, s] = psum.tile([P, P], F32, name="sums%d_%d_%d" % (j, b, s), tag="bank%d" % (2 * s + b))
-                        nc.tensor.matmul(sums[b, s][:], lhsT=prods[c][b][:, s, :], rhs=ident[:], is_transpose=True, start=(c == 0), stop=(c == 1))
+                            sums[b, s] = psum.tile([P, P], F32, name="sums%d_%d_%d" % (j, b, s), tag="bank%d" % (PARTS * b + s))
+                        nc.tensor.matmul(sums[b, s][:], lhsT=terms[c][b][:, s, :], rhs=ident[:], is_transpose=True, start=(c == 0), stop=(c == PARTS - 1))
             for b, s in units:
                 nc.scalar.copy(
-                    by_query[b, s][:, :, 32 * j : 32 * (j + 1), :],
+                    by_query[b, s][:, :, SLAB_WORDS * j : SLAB_WORDS * (j + 1), :],
                     sums[b, s][:].rearrange("q (p u e) -> q u p e", u=2, e=2),
                 )
+
             if j == 0:
-                picked = keep.tile([P, 2 * I], U8, name="picked_scales")
-                for c in range(2):
-                    nc.vector.tensor_copy(picked[:, c * I : (c + 1) * I], scale_pool[c][:].indirect(tail_list[:]))
-                for r in range(4):
-                    nc.scalar.dma_start(tail_plane[r:P:32, :].bitcast(I32), picked[8 * r : P : 32, :].bitcast(I32))
+                picked_scales = keep.tile([P, PARTS * I], U8, name="picked_scales")
+                for c in range(PARTS):
+                    nc.vector.tensor_copy(picked_scales[:, c * I : (c + 1) * I], scale_table[c][:].indirect(tail_list[:]))
+                for r in range(QUADRANT // SPREAD):
+                    nc.sync.dma_start(tail_scales[r:P:QUADRANT, :].bitcast(I32), picked_scales[SPREAD * r : P : QUADRANT, :].bitcast(I32))
 
         tail_words = []
-        for c in range(2):
-            tail_words.append(keep.tile([P, I], U16, name="tail_words%d" % c, align_bytes=64))
-            nc.vector.tensor_copy(tail_words[c][:], word_pool[c][:].indirect(tail_list[:]))
+        for c in range(PARTS):
+            tail_words.append(keep.tile([P, I], U16, name="tail_words%d" % c, align_bytes=MX_ALIGN))
+            nc.vector.tensor_copy(tail_words[c][:], word_table[c][:].indirect(tail_list[:]))
 
-        acc = [psum.tile([P, I], F32, name="acc%d" % b, tag="bank%d" % b) for b in range(QB)]
+        scores = [psum.tile([P, I], F32, name="scores%d" % b, tag="bank%d" % (len(units) - 1 - b)) for b in range(BLOCKS)]
+
         grouped = {}
         for b, s in units:
             pairs = by_query[b, s][:].rearrange("q u p e -> q (u p e)").bitcast(F32)
             turned = psum.tile([P, 2, P], F32, name="turned%d_%d" % (b, s))
             for u in range(2):
                 nc.tensor.transpose(turned[:, u, :], pairs[:, u * P : (u + 1) * P], ident[:])
-            grouped[b, s] = keep.tile([P, P * 4], BF16, name="grouped%d_%d" % (b, s), align_bytes=64)
+            grouped[b, s] = keep.tile([P, P * PACK], BF16, name="grouped%d_%d" % (b, s), align_bytes=MX_ALIGN)
             nc.scalar.copy(grouped[b, s][:].bitcast(F32).rearrange("p (q u) -> p q u", u=2), turned[:].rearrange("p u q -> p q u"))
+
+        query_codes = keep.tile([P, len(units) * P], U32, name="query_codes", tag="word_table%d" % (PARTS - 1), align_bytes=MX_ALIGN)
         for n, (b, s) in enumerate(units):
-            codes = keep.tile([P, P], U32, name="codes%d_%d" % (b, s), tag="by_query%d_%d" % units[-1 - n], align_bytes=64)
-            plane = keep.tile([P, P], U8, name="plane%d_%d" % (b, s), align_bytes=64)
-            nc.vector.quantize_mx(out=codes[:].bitcast(FP8X4), scales=plane[:], in_=grouped[b, s][:])
+            codes = query_codes[:, n * P : (n + 1) * P]
+            query_scales = keep.tile([P, P], U8, name="query_scales%d_%d" % (b, s), align_bytes=MX_ALIGN)
+            nc.vector.quantize_mx(out=codes.bitcast(FP8X4), scales=query_scales[:], in_=grouped[b, s][:])
             nc.tensor.matmul_mx(
-                out=acc[b][:],
-                lhsT=codes[:].bitcast(FP8X4),
-                lhsT_scale=plane[:],
+                out=scores[b][:],
+                lhsT=codes.bitcast(FP8X4),
+                lhsT_scale=query_scales[:],
                 rhs=tail_words[s][:].bitcast(FP4X4),
-                rhs_scale=tail_plane[:, s * I : (s + 1) * I],
+                rhs_scale=tail_scales[:, s * I : (s + 1) * I],
                 start=(s == 0),
-                stop=(s == 1),
+                stop=(s == PARTS - 1),
             )
-        result = keep.tile([P, I], F32, name="result0")
-        nc.scalar.copy(result[:], acc[0][:])
-        nc.sync.dma_start(out[0:P, :], result[:])
+
+        first_block = keep.tile([P, I], F32, name="first_block")
+        nc.scalar.copy(first_block[:], scores[0][:])
+        nc.sync.dma_start(out[0:P, :], first_block[:])
         for h in range(2):
-            cols = slice(h * I // 2, (h + 1) * I // 2)
-            half = keep.tile([P, I // 2], F32, name="half%d" % h)
-            nc.vector.tensor_copy(half[:], acc[1][:, cols])
-            nc.sync.dma_start(out[P:Q, cols], half[:])
+            candidates = slice(h * I // 2, (h + 1) * I // 2)
+            half_block = keep.tile([P, I // 2], F32, name="half_block%d" % h)
+            nc.vector.tensor_copy(half_block[:], scores[1][:, candidates])
+            nc.sync.dma_start(out[P:Q, candidates], half_block[:])

@@ -17,15 +17,14 @@ FP4X4 = mybir.dt.float4_e2m1fn_x4
 MULT = mybir.AluOpType.mult
 
 P = 128
-SLABS = D // P
 BLOCKS = Q // P
 PARTS = 2
 PACK = 4
+LAST = PACK - 1
 LIST_GROUP = 16
 QUADRANT = 32
 SCALE_ROWS = D // 32
 SPREAD = P // SCALE_ROWS
-SLAB_WORDS = P // PACK
 MX_ALIGN = 64
 
 
@@ -49,62 +48,94 @@ def tile_attend_complexscores_kernel(tc, hre, him, rre, rim, tre_words, tre_scal
         make_identity(nc, ident[:])
 
         word_table = [keep.tile([P, V], U16, name="word_table%d" % c, tag="word_table%d" % c, align_bytes=MX_ALIGN) for c in range(PARTS)]
-        rel_table = [[keep.tile([P, U], F32, name="rel_table%d_%d" % (c, j)) for j in range(SLABS)] for c in range(PARTS)]
-        head_table = [[keep.tile([P, T], F32, name="head_table%d_%d" % (c, j)) for j in range(SLABS)] for c in range(PARTS)]
+        rel_table = [[keep.tile([P, U], F32, name="rel_table%d_%d" % (c, t)) for t in range(PACK)] for c in range(PARTS)]
+        head_table = [[keep.tile([P, T], F32, name="head_table%d_%d" % (c, t)) for t in range(PACK)] for c in range(PARTS)]
 
-        nc.sync.dma_start(rel_list[:], offs2)
-        for j in range(SLABS):
-            rows = slice(j * P, (j + 1) * P)
-            for c, table in enumerate((rre, rim)):
-                nc.sync.dma_start(rel_table[c][j][:], table[rows, :])
-            if j == 0:
+        def load_plane(tiles, tables, c, t):
+            nc.sync.dma_start(tiles[c][t][:], tables[c].rearrange("(p t) w -> t p w", t=PACK)[t])
+
+        rels, heads = (rre, rim), (hre, him)
+        for t in range(PACK):
+            if t == LAST:
+                load_plane(rel_table, rels, 1, t)
+                load_plane(head_table, heads, 0, t)
+                load_plane(rel_table, rels, 0, t)
+                load_plane(head_table, heads, 1, t)
+                continue
+            if t == 0:
+                nc.sync.dma_start(rel_list[:], offs2)
+            load_plane(rel_table, rels, 0, t)
+            load_plane(rel_table, rels, 1, t)
+            if t == 0:
                 nc.sync.dma_start(tail_list[:], offs3)
                 nc.sync.dma_start(scale_table[0][0:P:SPREAD, :].bitcast(I32), tre_scales[0].bitcast(I32))
                 nc.sync.dma_start(head_list[:], offs)
-            for c, table in enumerate((hre, him)):
-                nc.sync.dma_start(head_table[c][j][:], table[rows, :])
-            if j == 0:
+            load_plane(head_table, heads, 0, t)
+            load_plane(head_table, heads, 1, t)
+            if t == 0:
                 nc.sync.dma_start(scale_table[1][0:P:SPREAD, :].bitcast(I32), tim_scales[0].bitcast(I32))
         for c, table in enumerate((tre_words, tim_words)):
             nc.sync.dma_start(word_table[c][:].bitcast(I32), table[0].bitcast(I32))
 
-        units = [(b, s) for b in range(BLOCKS) for s in range(PARTS)]
-        by_query = {(b, s): keep.tile([P, 2, P, 2], BF16, name="by_query%d_%d" % (b, s), align_bytes=MX_ALIGN) for b, s in units}
+        units = [(b, s) for s in range(PARTS) for b in range(BLOCKS)]
+        turned = {(b, s): psum.tile([P, 2, P], F32, name="turned%d_%d" % (b, s)) for b, s in units}
+        pairs = {}
 
-        for j in range(SLABS):
-            rel = keep.tile([P, 3, Q], F32, name="rel%d" % j)
-            for c in range(PARTS):
-                nc.vector.tensor_copy(rel[:, 1 + c, :], rel_table[c][j][:].indirect(rel_list[:]))
-            nc.scalar.mul(rel[:, 0, :], rel[:, 2, :], -1.0)
+        def gather_rel(rel, c, t):
+            nc.vector.tensor_copy(rel[:, 1 + c, :], rel_table[c][t][:].indirect(rel_list[:]))
+            if c == 1:
+                nc.scalar.mul(rel[:, 0, :], rel[:, 2, :], -1.0)
 
-            terms = []
-            for c in range(PARTS):
-                head = keep.tile([P, 1, Q], F32, name="head%d_%d" % (c, j))
-                nc.vector.tensor_copy(head[:, 0, :], head_table[c][j][:].indirect(head_list[:]))
-                if (j, c) == (SLABS - 1, PARTS - 1):
-                    terms.append([keep.tile([P, PARTS, P], F32, name="last_term%d" % b) for b in range(BLOCKS)])
+        for t in range(PACK):
+            u, e = divmod(t, 2)
+            rel = keep.tile([P, 3, Q], F32, name="rel%d" % t)
+            term = {}
+            if t < LAST:
+                for c in range(PARTS):
+                    gather_rel(rel, c, t)
+                for c in range(PARTS):
+                    head = keep.tile([P, 1, Q], F32, name="head%d_%d" % (c, t))
+                    nc.vector.tensor_copy(head[:, 0, :], head_table[c][t][:].indirect(head_list[:]))
+                    both = keep.tile([P, PARTS, Q], F32, name="term%d_%d" % (c, t))
+                    nc.gpsimd.tensor_tensor(both[:], rel[:, 1 - c : 3 - c, :], head[:].to_broadcast([P, PARTS, Q]), MULT)
+                    for b, s in units:
+                        term[c, b, s] = both[:, s, b * P : (b + 1) * P]
+            else:
+                gather_rel(rel, 1, t)
+                head = keep.tile([P, Q], F32, name="head0_%d" % t)
+                nc.vector.tensor_copy(head[:], head_table[0][t][:].indirect(head_list[:]))
+                gather_rel(rel, 0, t)
+                for s in (1, 0):
+                    one = keep.tile([P, Q], F32, name="last_real_term%d" % s)
+                    nc.gpsimd.tensor_tensor(one[:], rel[:, 1 + s, :], head[:], MULT)
                     for b in range(BLOCKS):
-                        queries = slice(b * P, (b + 1) * P)
-                        nc.vector.tensor_tensor(terms[c][b][:], rel[:, 0:2, queries], head[:, :, queries].to_broadcast([P, PARTS, P]), MULT)
-                else:
-                    term = keep.tile([P, PARTS, Q], F32, name="term%d_%d" % (c, j))
-                    nc.gpsimd.tensor_tensor(term[:], rel[:, 1 - c : 3 - c, :], head[:].to_broadcast([P, PARTS, Q]), MULT)
-                    terms.append([term[:, :, b * P : (b + 1) * P] for b in range(BLOCKS)])
+                        term[0, b, s] = one[:, b * P : (b + 1) * P]
+                last_head = keep.tile([P, 1, Q], F32, name="last_head")
+                for b in range(BLOCKS):
+                    columns = slice(b * P // LIST_GROUP, (b + 1) * P // LIST_GROUP)
+                    nc.vector.tensor_copy(last_head[:, 0, b * P : (b + 1) * P], head_table[1][t][:].indirect(head_list[:, columns]))
+                for b in range(BLOCKS):
+                    queries = slice(b * P, (b + 1) * P)
+                    both = keep.tile([P, PARTS, P], F32, name="last_term%d" % b)
+                    nc.vector.tensor_tensor(both[:], rel[:, 0:2, queries], last_head[:, :, queries].to_broadcast([P, PARTS, P]), MULT)
+                    for s in range(PARTS):
+                        term[1, b, s] = both[:, s, :]
 
             sums = {}
-            for b in range(BLOCKS):
-                for c in range(PARTS):
-                    for s in range(PARTS):
-                        if c == 0:
-                            sums[b, s] = psum.tile([P, P], F32, name="sums%d_%d_%d" % (j, b, s), tag="bank%d" % (PARTS * b + s))
-                        nc.tensor.matmul(sums[b, s][:], lhsT=terms[c][b][:, s, :], rhs=ident[:], is_transpose=True, start=(c == 0), stop=(c == PARTS - 1))
+            for c in range(PARTS):
+                for n, (b, s) in enumerate(units):
+                    if c == 0:
+                        sums[b, s] = psum.tile([P, P], F32, name="sums%d_%d_%d" % (t, b, s), tag="bank%d" % n)
+                    nc.tensor.matmul(sums[b, s][:], lhsT=term[c, b, s], rhs=ident[:], is_transpose=True, start=(c == 0), stop=(c == PARTS - 1))
             for b, s in units:
-                nc.scalar.copy(
-                    by_query[b, s][:, :, SLAB_WORDS * j : SLAB_WORDS * (j + 1), :],
-                    sums[b, s][:].rearrange("q (p u e) -> q u p e", u=2, e=2),
-                )
+                if e == 0:
+                    pairs[b, s] = keep.tile([P, P, 2], BF16, name="pairs%d_%d_%d" % (u, b, s))
+                nc.scalar.copy(pairs[b, s][:, :, e], sums[b, s][:])
+                if e == 1:
+                    words = pairs[b, s][:].rearrange("q p e -> q (p e)").bitcast(F32)
+                    nc.tensor.transpose(turned[b, s][:, u, :], words, ident[:])
 
-            if j == 0:
+            if t == 0:
                 picked_scales = keep.tile([P, PARTS * I], U8, name="picked_scales")
                 for c in range(PARTS):
                     nc.vector.tensor_copy(picked_scales[:, c * I : (c + 1) * I], scale_table[c][:].indirect(tail_list[:]))
@@ -118,20 +149,13 @@ def tile_attend_complexscores_kernel(tc, hre, him, rre, rim, tre_words, tre_scal
 
         scores = [psum.tile([P, I], F32, name="scores%d" % b, tag="bank%d" % (len(units) - 1 - b)) for b in range(BLOCKS)]
 
-        grouped = {}
-        for b, s in units:
-            pairs = by_query[b, s][:].rearrange("q u p e -> q (u p e)").bitcast(F32)
-            turned = psum.tile([P, 2, P], F32, name="turned%d_%d" % (b, s))
-            for u in range(2):
-                nc.tensor.transpose(turned[:, u, :], pairs[:, u * P : (u + 1) * P], ident[:])
-            grouped[b, s] = keep.tile([P, P * PACK], BF16, name="grouped%d_%d" % (b, s), align_bytes=MX_ALIGN)
-            nc.scalar.copy(grouped[b, s][:].bitcast(F32).rearrange("p (q u) -> p q u", u=2), turned[:].rearrange("p u q -> p q u"))
-
         query_codes = keep.tile([P, len(units) * P], U32, name="query_codes", tag="word_table%d" % (PARTS - 1), align_bytes=MX_ALIGN)
         for n, (b, s) in enumerate(units):
+            grouped = keep.tile([P, P * PACK], BF16, name="grouped%d_%d" % (b, s), align_bytes=MX_ALIGN)
+            nc.scalar.copy(grouped[:].bitcast(F32).rearrange("p (q u) -> p q u", u=2), turned[b, s][:].rearrange("p u q -> p q u"))
             codes = query_codes[:, n * P : (n + 1) * P]
             query_scales = keep.tile([P, P], U8, name="query_scales%d_%d" % (b, s), align_bytes=MX_ALIGN)
-            nc.vector.quantize_mx(out=codes.bitcast(FP8X4), scales=query_scales[:], in_=grouped[b, s][:])
+            nc.vector.quantize_mx(out=codes.bitcast(FP8X4), scales=query_scales[:], in_=grouped[:])
             nc.tensor.matmul_mx(
                 out=scores[b][:],
                 lhsT=codes.bitcast(FP8X4),

@@ -15,6 +15,7 @@ U8 = mybir.dt.uint8
 FP8X4 = mybir.dt.float8_e4m3fn_x4
 FP4X4 = mybir.dt.float4_e2m1fn_x4
 MULT = mybir.AluOpType.mult
+ADD = mybir.AluOpType.add
 
 P = 128
 BLOCKS = Q // P
@@ -79,61 +80,50 @@ def tile_attend_complexscores_kernel(tc, hre, him, rre, rim, tre_words, tre_scal
 
         units = [(b, s) for s in range(PARTS) for b in range(BLOCKS)]
         turned = {(b, s): psum.tile([P, 2, P], F32, name="turned%d_%d" % (b, s)) for b, s in units}
-        pairs = {}
+        grouped = [keep.tile([P, Q, PACK], BF16, name="grouped%d" % s, tag="grouped%d" % s, align_bytes=MX_ALIGN) for s in range(PARTS)]
 
         def gather_rel(rel, c, t):
             nc.vector.tensor_copy(rel[:, 1 + c, :], rel_table[c][t][:].indirect(rel_list[:]))
             if c == 1:
                 nc.scalar.mul(rel[:, 0, :], rel[:, 2, :], -1.0)
 
-        for t in range(PACK):
+        sums = {}
+        for t in range(LAST):
             u, e = divmod(t, 2)
             rel = keep.tile([P, 3, Q], F32, name="rel%d" % t)
-            term = {}
-            if t < LAST:
-                for c in range(PARTS):
-                    gather_rel(rel, c, t)
-                for c in range(PARTS):
-                    head = keep.tile([P, 1, Q], F32, name="head%d_%d" % (c, t))
-                    nc.vector.tensor_copy(head[:, 0, :], head_table[c][t][:].indirect(head_list[:]))
-                    both = keep.tile([P, PARTS, Q], F32, name="term%d_%d" % (c, t))
-                    nc.gpsimd.tensor_tensor(both[:], rel[:, 1 - c : 3 - c, :], head[:].to_broadcast([P, PARTS, Q]), MULT)
-                    for b, s in units:
-                        term[c, b, s] = both[:, s, b * P : (b + 1) * P]
-            else:
-                gather_rel(rel, 1, t)
-                head = keep.tile([P, Q], F32, name="head0_%d" % t)
-                nc.vector.tensor_copy(head[:], head_table[0][t][:].indirect(head_list[:]))
-                gather_rel(rel, 0, t)
-                for s in (1, 0):
-                    one = keep.tile([P, Q], F32, name="last_real_term%d" % s)
-                    nc.gpsimd.tensor_tensor(one[:], rel[:, 1 + s, :], head[:], MULT)
-                    for b in range(BLOCKS):
-                        term[0, b, s] = one[:, b * P : (b + 1) * P]
-                last_head = keep.tile([P, 1, Q], F32, name="last_head")
-                for b in range(BLOCKS):
-                    columns = slice(b * P // LIST_GROUP, (b + 1) * P // LIST_GROUP)
-                    nc.vector.tensor_copy(last_head[:, 0, b * P : (b + 1) * P], head_table[1][t][:].indirect(head_list[:, columns]))
-                for b in range(BLOCKS):
-                    queries = slice(b * P, (b + 1) * P)
-                    both = keep.tile([P, PARTS, P], F32, name="last_term%d" % b)
-                    nc.vector.tensor_tensor(both[:], rel[:, 0:2, queries], last_head[:, :, queries].to_broadcast([P, PARTS, P]), MULT)
-                    for s in range(PARTS):
-                        term[1, b, s] = both[:, s, :]
-
-            sums = {}
             for c in range(PARTS):
-                for n, (b, s) in enumerate(units):
-                    if c == 0:
-                        sums[b, s] = psum.tile([P, P], F32, name="sums%d_%d_%d" % (t, b, s), tag="bank%d" % n)
-                    nc.tensor.matmul(sums[b, s][:], lhsT=term[c, b, s], rhs=ident[:], is_transpose=True, start=(c == 0), stop=(c == PARTS - 1))
-            for b, s in units:
+                gather_rel(rel, c, t)
+            terms = []
+            for c in range(PARTS):
+                head = keep.tile([P, 1, Q], F32, name="head%d_%d" % (c, t))
+                nc.vector.tensor_copy(head[:, 0, :], head_table[c][t][:].indirect(head_list[:]))
+                terms.append(keep.tile([P, PARTS, Q], F32, name="term%d_%d" % (c, t)))
+                if (t, c) == (LAST - 1, PARTS - 1):
+                    for s in range(PARTS):
+                        nc.gpsimd.tensor_tensor(terms[c][:, s, :], rel[:, s, :], head[:, 0, :], MULT)
+                else:
+                    nc.gpsimd.tensor_tensor(terms[c][:], rel[:, 1 - c : 3 - c, :], head[:].to_broadcast([P, PARTS, Q]), MULT)
+
+            for n, (b, s) in enumerate(units):
                 if e == 0:
-                    pairs[b, s] = keep.tile([P, P, 2], BF16, name="pairs%d_%d_%d" % (u, b, s))
-                nc.scalar.copy(pairs[b, s][:, :, e], sums[b, s][:])
-                if e == 1:
-                    words = pairs[b, s][:].rearrange("q p e -> q (p e)").bitcast(F32)
-                    nc.tensor.transpose(turned[b, s][:, u, :], words, ident[:])
+                    sums[b, s] = psum.tile([P, 2, P], F32, name="sums%d_%d_%d" % (u, b, s), tag="bank%d" % n)
+                nc.tensor.matmul(sums[b, s][:, e, :], lhsT=terms[0][:, s, b * P : (b + 1) * P], rhs=ident[:], is_transpose=True, start=True, stop=False)
+            for s in range(PARTS):
+                for b in range(BLOCKS):
+                    nc.tensor.matmul(sums[b, s][:, e, :], lhsT=terms[1][:, s, b * P : (b + 1) * P], rhs=ident[:], is_transpose=True, start=False, stop=True)
+                if t == 0:
+                    continue
+                for b in range(BLOCKS):
+                    pairs = keep.tile([P, P, 2], BF16, name="pairs%d_%d_%d" % (u, b, s))
+                    if u == 0:
+                        nc.scalar.copy(pairs[:], sums[b, s][:].rearrange("q e p -> q p e"))
+                    else:
+                        nc.scalar.copy(pairs[:], sums[b, s][:, 0:1, :].rearrange("q e p -> q p e").to_broadcast([P, P, 2]))
+                    nc.tensor.transpose(turned[b, s][:, u, :], pairs[:].rearrange("q p e -> q (p e)").bitcast(F32), ident[:])
+                if u == 1:
+                    for b in range(BLOCKS):
+                        words = grouped[s][:, b * P : (b + 1) * P, :].rearrange("p q t -> p (q t)").bitcast(F32)
+                        nc.scalar.copy(words.rearrange("p (q u) -> p q u", u=2), turned[b, s][:].rearrange("p u q -> p q u"))
 
             if t == 0:
                 picked_scales = keep.tile([P, PARTS * I], U8, name="picked_scales")
@@ -142,29 +132,50 @@ def tile_attend_complexscores_kernel(tc, hre, him, rre, rim, tre_words, tre_scal
                 for r in range(QUADRANT // SPREAD):
                     nc.sync.dma_start(tail_scales[r:P:QUADRANT, :].bitcast(I32), picked_scales[SPREAD * r : P : QUADRANT, :].bitcast(I32))
 
-        tail_words = []
-        for c in range(PARTS):
-            tail_words.append(keep.tile([P, I], U16, name="tail_words%d" % c, align_bytes=MX_ALIGN))
-            nc.vector.tensor_copy(tail_words[c][:], word_table[c][:].indirect(tail_list[:]))
+        rel = keep.tile([P, 3, Q], F32, name="rel%d" % LAST)
+        head = [keep.tile([P, Q], F32, name="head%d_%d" % (c, LAST)) for c in range(PARTS)]
+        real_term = [keep.tile([P, Q], F32, name="real_term%d" % s) for s in range(PARTS)]
+        gather_rel(rel, 1, LAST)
+        nc.vector.tensor_copy(head[0][:], head_table[0][LAST][:].indirect(head_list[:]))
+        gather_rel(rel, 0, LAST)
+        for s in (1, 0):
+            nc.gpsimd.tensor_tensor(real_term[s][:], rel[:, 1 + s, :], head[0][:], MULT)
+        for b in range(BLOCKS):
+            columns = slice(b * P // LIST_GROUP, (b + 1) * P // LIST_GROUP)
+            nc.vector.tensor_copy(head[1][:, b * P : (b + 1) * P], head_table[1][LAST][:].indirect(head_list[:, columns]))
 
-        scores = [psum.tile([P, I], F32, name="scores%d" % b, tag="bank%d" % (len(units) - 1 - b)) for b in range(BLOCKS)]
+        scores = [psum.tile([P, I], F32, name="scores%d" % b, tag="bank%d" % b) for b in range(BLOCKS)]
+        for s in range(PARTS):
+            if s == 0:
+                imag_term = keep.tile([P, Q], F32, name="imag_term0")
+                for b in range(BLOCKS):
+                    queries = slice(b * P, (b + 1) * P)
+                    nc.vector.tensor_tensor(imag_term[:, queries], rel[:, s, queries], head[1][:, queries], MULT)
+            else:
+                imag_term = keep.tile([P, Q], F32, name="imag_term1", tag="grouped0", align_bytes=MX_ALIGN)
+                nc.vector.tensor_tensor(imag_term[:], rel[:, s, :], head[1][:], MULT)
+            nc.gpsimd.tensor_tensor(grouped[s][:, :, LAST], real_term[s][:], imag_term[:], ADD)
 
-        query_codes = keep.tile([P, len(units) * P], U32, name="query_codes", tag="word_table%d" % (PARTS - 1), align_bytes=MX_ALIGN)
-        for n, (b, s) in enumerate(units):
-            grouped = keep.tile([P, P * PACK], BF16, name="grouped%d_%d" % (b, s), align_bytes=MX_ALIGN)
-            nc.scalar.copy(grouped[:].bitcast(F32).rearrange("p (q u) -> p q u", u=2), turned[b, s][:].rearrange("p u q -> p q u"))
-            codes = query_codes[:, n * P : (n + 1) * P]
-            query_scales = keep.tile([P, P], U8, name="query_scales%d_%d" % (b, s), align_bytes=MX_ALIGN)
-            nc.vector.quantize_mx(out=codes.bitcast(FP8X4), scales=query_scales[:], in_=grouped[:])
-            nc.tensor.matmul_mx(
-                out=scores[b][:],
-                lhsT=codes.bitcast(FP8X4),
-                lhsT_scale=query_scales[:],
-                rhs=tail_words[s][:].bitcast(FP4X4),
-                rhs_scale=tail_scales[:, s * I : (s + 1) * I],
-                start=(s == 0),
-                stop=(s == PARTS - 1),
-            )
+            tail_words = keep.tile([P, I], U16, name="tail_words%d" % s, align_bytes=MX_ALIGN)
+            nc.vector.tensor_copy(tail_words[:], word_table[s][:].indirect(tail_list[:]))
+
+            codes = keep.tile([P, Q], U32, name="query_codes%d" % s, tag="word_table%d" % s, align_bytes=MX_ALIGN)
+            query_scales = keep.tile([P, Q], U8, name="query_scales%d" % s, align_bytes=MX_ALIGN)
+            width = Q if s == 0 else P
+            for first in range(0, Q, width):
+                queries = slice(first, first + width)
+                nc.vector.quantize_mx(out=codes[:, queries].bitcast(FP8X4), scales=query_scales[:, queries], in_=grouped[s][:, queries, :].rearrange("p q t -> p (q t)"))
+            for b in range(BLOCKS):
+                queries = slice(b * P, (b + 1) * P)
+                nc.tensor.matmul_mx(
+                    out=scores[b][:],
+                    lhsT=codes[:, queries].bitcast(FP8X4),
+                    lhsT_scale=query_scales[:, queries],
+                    rhs=tail_words[:].bitcast(FP4X4),
+                    rhs_scale=tail_scales[:, s * I : (s + 1) * I],
+                    start=(s == 0),
+                    stop=(s == PARTS - 1),
+                )
 
         first_block = keep.tile([P, I], F32, name="first_block")
         nc.scalar.copy(first_block[:], scores[0][:])

@@ -27,6 +27,7 @@ QUADRANT = 32
 SCALE_ROWS = D // 32
 SPREAD = P // SCALE_ROWS
 MX_ALIGN = 64
+HALF = I // 2
 
 
 def tile_attend_complexscores_kernel(tc, hre, him, rre, rim, tre_words, tre_scales, tim_words, tim_scales, offs, offs2, offs3, out):
@@ -73,7 +74,7 @@ def tile_attend_complexscores_kernel(tc, hre, him, rre, rim, tre_words, tre_scal
                 nc.sync.dma_start(head_list[:], offs)
             load_plane(head_table, heads, 0, t)
             load_plane(head_table, heads, 1, t)
-            if t == 0:
+            if t == LAST - 1:
                 nc.sync.dma_start(scale_table[1][0:P:SPREAD, :].bitcast(I32), tim_scales[0].bitcast(I32))
         for c, table in enumerate((tre_words, tim_words)):
             nc.sync.dma_start(word_table[c][:].bitcast(I32), table[0].bitcast(I32))
@@ -81,18 +82,39 @@ def tile_attend_complexscores_kernel(tc, hre, him, rre, rim, tre_words, tre_scal
         units = [(b, s) for s in range(PARTS) for b in range(BLOCKS)]
         turned = {(b, s): psum.tile([P, 2, P], F32, name="turned%d_%d" % (b, s)) for b, s in units}
         grouped = [keep.tile([P, Q, PACK], BF16, name="grouped%d" % s, tag="grouped%d" % s, align_bytes=MX_ALIGN) for s in range(PARTS)]
+        picked_scales = keep.tile([P, PARTS * I], U8, name="picked_scales")
+        sums = {}
 
         def gather_rel(rel, c, t):
             nc.vector.tensor_copy(rel[:, 1 + c, :], rel_table[c][t][:].indirect(rel_list[:]))
             if c == 1:
                 nc.scalar.mul(rel[:, 0, :], rel[:, 2, :], -1.0)
 
-        sums = {}
-        for t in range(LAST):
+        def add_term(b, s, t, term, c):
             u, e = divmod(t, 2)
+            if (c, e) == (0, 0):
+                sums[b, s] = psum.tile([P, 2, P], F32, name="sums%d_%d_%d" % (u, b, s), tag="bank%d" % units.index((b, s)))
+            nc.tensor.matmul(sums[b, s][:, e, :], lhsT=term[:, b * P : (b + 1) * P], rhs=ident[:], is_transpose=True, start=(c == 0), stop=(c == PARTS - 1))
+
+        def turn_back(s, u, summed):
+            for b in range(BLOCKS):
+                pairs = keep.tile([P, P, 2], BF16, name="pairs%d_%d_%d" % (u, b, s))
+                nc.scalar.copy(pairs[:], sums[b, s][:, 0:summed, :].rearrange("q e p -> q p e").to_broadcast([P, P, 2]))
+                nc.tensor.transpose(turned[b, s][:, u, :], pairs[:].rearrange("q p e -> q (p e)").bitcast(F32), ident[:])
+            if u == 1:
+                for b in range(BLOCKS):
+                    words = grouped[s][:, b * P : (b + 1) * P, :].rearrange("p q t -> p (q t)").bitcast(F32)
+                    nc.scalar.copy(words.rearrange("p (q u) -> p q u", u=2), turned[b, s][:].rearrange("p u q -> p q u"))
+
+        def gather_scales(c):
+            nc.vector.tensor_copy(picked_scales[:, c * I : (c + 1) * I], scale_table[c][:].indirect(tail_list[:]))
+
+        for t in range(LAST):
             rel = keep.tile([P, 3, Q], F32, name="rel%d" % t)
             for c in range(PARTS):
                 gather_rel(rel, c, t)
+            if t == 0:
+                gather_scales(0)
             terms = []
             for c in range(PARTS):
                 head = keep.tile([P, 1, Q], F32, name="head%d_%d" % (c, t))
@@ -103,85 +125,85 @@ def tile_attend_complexscores_kernel(tc, hre, him, rre, rim, tre_words, tre_scal
                         nc.gpsimd.tensor_tensor(terms[c][:, s, :], rel[:, s, :], head[:, 0, :], MULT)
                 else:
                     nc.gpsimd.tensor_tensor(terms[c][:], rel[:, 1 - c : 3 - c, :], head[:].to_broadcast([P, PARTS, Q]), MULT)
-
-            for n, (b, s) in enumerate(units):
-                if e == 0:
-                    sums[b, s] = psum.tile([P, 2, P], F32, name="sums%d_%d_%d" % (u, b, s), tag="bank%d" % n)
-                nc.tensor.matmul(sums[b, s][:, e, :], lhsT=terms[0][:, s, b * P : (b + 1) * P], rhs=ident[:], is_transpose=True, start=True, stop=False)
+            for b, s in units:
+                add_term(b, s, t, terms[0][:, s, :], 0)
             for s in range(PARTS):
                 for b in range(BLOCKS):
-                    nc.tensor.matmul(sums[b, s][:, e, :], lhsT=terms[1][:, s, b * P : (b + 1) * P], rhs=ident[:], is_transpose=True, start=False, stop=True)
-                if t == 0:
-                    continue
-                for b in range(BLOCKS):
-                    pairs = keep.tile([P, P, 2], BF16, name="pairs%d_%d_%d" % (u, b, s))
-                    if u == 0:
-                        nc.scalar.copy(pairs[:], sums[b, s][:].rearrange("q e p -> q p e"))
-                    else:
-                        nc.scalar.copy(pairs[:], sums[b, s][:, 0:1, :].rearrange("q e p -> q p e").to_broadcast([P, P, 2]))
-                    nc.tensor.transpose(turned[b, s][:, u, :], pairs[:].rearrange("q p e -> q (p e)").bitcast(F32), ident[:])
-                if u == 1:
-                    for b in range(BLOCKS):
-                        words = grouped[s][:, b * P : (b + 1) * P, :].rearrange("p q t -> p (q t)").bitcast(F32)
-                        nc.scalar.copy(words.rearrange("p (q u) -> p q u", u=2), turned[b, s][:].rearrange("p u q -> p q u"))
+                    add_term(b, s, t, terms[1][:, s, :], 1)
+                if t == 1:
+                    turn_back(s, 0, 2)
+                elif (t, s) == (LAST - 1, 0):
+                    turn_back(s, 1, 1)
 
-            if t == 0:
-                picked_scales = keep.tile([P, PARTS * I], U8, name="picked_scales")
-                for c in range(PARTS):
-                    nc.vector.tensor_copy(picked_scales[:, c * I : (c + 1) * I], scale_table[c][:].indirect(tail_list[:]))
-                for r in range(QUADRANT // SPREAD):
-                    nc.sync.dma_start(tail_scales[r:P:QUADRANT, :].bitcast(I32), picked_scales[SPREAD * r : P : QUADRANT, :].bitcast(I32))
+        gather_scales(1)
+        for r in range(QUADRANT // SPREAD):
+            nc.sync.dma_start(tail_scales[r:P:QUADRANT, :].bitcast(I32), picked_scales[SPREAD * r : P : QUADRANT, :].bitcast(I32))
 
         rel = keep.tile([P, 3, Q], F32, name="rel%d" % LAST)
         head = [keep.tile([P, Q], F32, name="head%d_%d" % (c, LAST)) for c in range(PARTS)]
         real_term = [keep.tile([P, Q], F32, name="real_term%d" % s) for s in range(PARTS)]
+        imag_term = [keep.tile([P, Q], F32, name="imag_term%d" % s) for s in range(PARTS)]
         gather_rel(rel, 1, LAST)
         nc.vector.tensor_copy(head[0][:], head_table[0][LAST][:].indirect(head_list[:]))
         gather_rel(rel, 0, LAST)
         for s in (1, 0):
             nc.gpsimd.tensor_tensor(real_term[s][:], rel[:, 1 + s, :], head[0][:], MULT)
         for b in range(BLOCKS):
+            add_term(b, 1, LAST, real_term[1], 0)
+        for b in range(BLOCKS):
             columns = slice(b * P // LIST_GROUP, (b + 1) * P // LIST_GROUP)
             nc.vector.tensor_copy(head[1][:, b * P : (b + 1) * P], head_table[1][LAST][:].indirect(head_list[:, columns]))
+        for b in range(BLOCKS):
+            queries = slice(b * P, (b + 1) * P)
+            nc.vector.tensor_tensor(imag_term[1][:, queries], rel[:, 1, queries], head[1][:, queries], MULT)
+            add_term(b, 1, LAST, imag_term[1], 1)
+        nc.vector.tensor_tensor(imag_term[0][:], rel[:, 0, :], head[1][:], MULT)
+        nc.gpsimd.tensor_tensor(grouped[0][:, :, LAST], real_term[0][:], imag_term[0][:], ADD)
+        turn_back(1, 1, 2)
 
-        scores = [psum.tile([P, I], F32, name="scores%d" % b, tag="bank%d" % b) for b in range(BLOCKS)]
-        for s in range(PARTS):
-            if s == 0:
-                imag_term = keep.tile([P, Q], F32, name="imag_term0")
-                for b in range(BLOCKS):
-                    queries = slice(b * P, (b + 1) * P)
-                    nc.vector.tensor_tensor(imag_term[:, queries], rel[:, s, queries], head[1][:, queries], MULT)
-            else:
-                imag_term = keep.tile([P, Q], F32, name="imag_term1", tag="grouped0", align_bytes=MX_ALIGN)
-                nc.vector.tensor_tensor(imag_term[:], rel[:, s, :], head[1][:], MULT)
-            nc.gpsimd.tensor_tensor(grouped[s][:, :, LAST], real_term[s][:], imag_term[:], ADD)
+        def gather_words(tile, c, first, count):
+            nc.vector.tensor_copy(tile[:], word_table[c][:].indirect(tail_list[:, first // LIST_GROUP : (first + count) // LIST_GROUP]))
 
-            tail_words = keep.tile([P, I], U16, name="tail_words%d" % s, align_bytes=MX_ALIGN)
-            nc.vector.tensor_copy(tail_words[:], word_table[s][:].indirect(tail_list[:]))
-
-            codes = keep.tile([P, Q], U32, name="query_codes%d" % s, tag="word_table%d" % s, align_bytes=MX_ALIGN)
+        def quantise(s, tag):
+            codes = keep.tile([P, Q], U32, name="query_codes%d" % s, tag=tag, align_bytes=MX_ALIGN)
             query_scales = keep.tile([P, Q], U8, name="query_scales%d" % s, align_bytes=MX_ALIGN)
-            width = Q if s == 0 else P
-            for first in range(0, Q, width):
-                queries = slice(first, first + width)
-                nc.vector.quantize_mx(out=codes[:, queries].bitcast(FP8X4), scales=query_scales[:, queries], in_=grouped[s][:, queries, :].rearrange("p q t -> p (q t)"))
-            for b in range(BLOCKS):
-                queries = slice(b * P, (b + 1) * P)
+            nc.vector.quantize_mx(out=codes[:].bitcast(FP8X4), scales=query_scales[:], in_=grouped[s][:].rearrange("p q t -> p (q t)"))
+            return codes, query_scales
+
+        halves = [(h, b) for h in range(2) for b in range(BLOCKS)]
+        scores = {(h, b): psum.tile([P, HALF], F32, name="scores%d_%d" % (h, b), tag="bank%d" % (len(units) - 1 - n)) for n, (h, b) in enumerate(halves)}
+
+        def multiply(h, b, s, operand, words):
+            codes, query_scales = operand
+            queries = slice(b * P, (b + 1) * P)
+            for k in range(HALF // P):
+                first = s * I + h * HALF + k * P
                 nc.tensor.matmul_mx(
-                    out=scores[b][:],
+                    out=scores[h, b][:, k * P : (k + 1) * P],
                     lhsT=codes[:, queries].bitcast(FP8X4),
                     lhsT_scale=query_scales[:, queries],
-                    rhs=tail_words[:].bitcast(FP4X4),
-                    rhs_scale=tail_scales[:, s * I : (s + 1) * I],
-                    start=(s == 0),
-                    stop=(s == PARTS - 1),
+                    rhs=words[:, k * P : (k + 1) * P].bitcast(FP4X4),
+                    rhs_scale=tail_scales[:, first : first + P],
+                    start=((s, k) == (0, 0)),
+                    stop=((s, k) == (PARTS - 1, HALF // P - 1)),
                 )
 
-        first_block = keep.tile([P, I], F32, name="first_block")
-        nc.scalar.copy(first_block[:], scores[0][:])
-        nc.sync.dma_start(out[0:P, :], first_block[:])
+        real_words = keep.tile([P, I], U16, name="real_words", align_bytes=MX_ALIGN)
+        gather_words(real_words, 0, 0, I)
+        x_operand = quantise(0, "word_table0")
+        for h, b in halves:
+            multiply(h, b, 0, x_operand, real_words[:, h * HALF : (h + 1) * HALF])
+        imag_words = []
         for h in range(2):
-            candidates = slice(h * I // 2, (h + 1) * I // 2)
-            half_block = keep.tile([P, I // 2], F32, name="half_block%d" % h)
-            nc.vector.tensor_copy(half_block[:], scores[1][:, candidates])
-            nc.sync.dma_start(out[P:Q, candidates], half_block[:])
+            imag_words.append(keep.tile([P, HALF], U16, name="imag_words%d" % h, tag="grouped%d" % h, align_bytes=MX_ALIGN))
+            gather_words(imag_words[h], 1, h * HALF, HALF)
+            if h == 0:
+                z_operand = quantise(1, "query_codes1")
+        for h, b in halves:
+            multiply(h, b, 1, z_operand, imag_words[h][:])
+            result = keep.tile([P, HALF], F32, name="result%d_%d" % (h, b))
+            if (h, b) == halves[-1]:
+                nc.vector.tensor_copy(result[:], scores[h, b][:])
+            else:
+                nc.scalar.copy(result[:], scores[h, b][:])
+            nc.sync.dma_start(out[b * P : (b + 1) * P, h * HALF : (h + 1) * HALF], result[:])

@@ -64,18 +64,18 @@ def tile_attend_complexscores_kernel(tc, hre, him, rre, rim, tre_words, tre_scal
                 load_plane(rel_table, rels, 0, t)
                 load_plane(head_table, heads, 1, t)
                 continue
+            load_plane(rel_table, rels, 0, t)
             if t == 0:
                 nc.sync.dma_start(rel_list[:], offs2)
-            load_plane(rel_table, rels, 0, t)
             load_plane(rel_table, rels, 1, t)
             if t == 0:
                 nc.sync.dma_start(tail_list[:], offs3)
                 nc.sync.dma_start(scale_table[0][0:P:SPREAD, :].bitcast(I32), tre_scales[0].bitcast(I32))
                 nc.sync.dma_start(head_list[:], offs)
             load_plane(head_table, heads, 0, t)
-            load_plane(head_table, heads, 1, t)
             if t == LAST - 1:
                 nc.sync.dma_start(scale_table[1][0:P:SPREAD, :].bitcast(I32), tim_scales[0].bitcast(I32))
+            load_plane(head_table, heads, 1, t)
         for c, table in enumerate((tre_words, tim_words)):
             nc.sync.dma_start(word_table[c][:].bitcast(I32), table[0].bitcast(I32))
 
@@ -117,6 +117,8 @@ def tile_attend_complexscores_kernel(tc, hre, him, rre, rim, tre_words, tre_scal
                 gather_scales(0)
             terms = []
             for c in range(PARTS):
+                if (t, c) == (LAST - 1, PARTS - 1):
+                    gather_scales(1)
                 head = keep.tile([P, 1, Q], F32, name="head%d_%d" % (c, t))
                 nc.vector.tensor_copy(head[:, 0, :], head_table[c][t][:].indirect(head_list[:]))
                 terms.append(keep.tile([P, PARTS, Q], F32, name="term%d_%d" % (c, t)))
@@ -135,7 +137,6 @@ def tile_attend_complexscores_kernel(tc, hre, him, rre, rim, tre_words, tre_scal
                 elif (t, s) == (LAST - 1, 0):
                     turn_back(s, 1, 1)
 
-        gather_scales(1)
         for r in range(QUADRANT // SPREAD):
             nc.sync.dma_start(tail_scales[r:P:QUADRANT, :].bitcast(I32), picked_scales[SPREAD * r : P : QUADRANT, :].bitcast(I32))
 
@@ -206,4 +207,5 @@ def tile_attend_complexscores_kernel(tc, hre, him, rre, rim, tre_words, tre_scal
                 nc.vector.tensor_copy(result[:], scores[h, b][:])
             else:
                 nc.scalar.copy(result[:], scores[h, b][:])
-            nc.sync.dma_start(out[b * P : (b + 1) * P, h * HALF : (h + 1) * HALF], result[:])
+            queue = nc.scalar if (h, b) == halves[-2] else nc.sync
+            queue.dma_start(out[b * P : (b + 1) * P, h * HALF : (h + 1) * HALF], result[:])

@@ -50,32 +50,35 @@ def tile_attend_complexscores_kernel(tc, hre, him, rre, rim, tre_words, tre_scal
         make_identity(nc, ident[:])
 
         word_table = [keep.tile([P, V], U16, name="word_table%d" % c, tag="word_table%d" % c, align_bytes=MX_ALIGN) for c in range(PARTS)]
-        rel_table = [[keep.tile([P, U], F32, name="rel_table%d_%d" % (c, t)) for t in range(PACK)] for c in range(PARTS)]
-        head_table = [[keep.tile([P, T], F32, name="head_table%d_%d" % (c, t)) for t in range(PACK)] for c in range(PARTS)]
+        rel_table, head_table = {}, {}
 
-        def load_plane(tiles, tables, c, t):
-            nc.sync.dma_start(tiles[c][t][:], tables[c].rearrange("(p t) w -> t p w", t=PACK)[t])
+        def load_planes(windows, table, c, first, count):
+            width = table.shape[1]
+            tile = keep.tile([P, count, width], F32, name="table%d_%d_%d" % (width, c, first))
+            nc.sync.dma_start(tile[:], table.rearrange("(p t) w -> p t w", t=PACK)[:, first : first + count, :])
+            for n in range(count):
+                windows[c, first + n] = tile[:, n, :]
 
-        rels, heads = (rre, rim), (hre, him)
-        for t in range(PACK):
-            if t == LAST:
-                load_plane(rel_table, rels, 1, t)
-                load_plane(head_table, heads, 0, t)
-                load_plane(rel_table, rels, 0, t)
-                load_plane(head_table, heads, 1, t)
-                continue
-            load_plane(rel_table, rels, 0, t)
-            if t == 0:
-                nc.sync.dma_start(rel_list[:], offs2)
-            load_plane(rel_table, rels, 1, t)
-            if t == 0:
-                nc.sync.dma_start(tail_list[:], offs3)
-                nc.sync.dma_start(scale_table[0][0:P:SPREAD, :].bitcast(I32), tre_scales[0].bitcast(I32))
-                nc.sync.dma_start(head_list[:], offs)
-            load_plane(head_table, heads, 0, t)
-            if t == LAST - 1:
-                nc.sync.dma_start(scale_table[1][0:P:SPREAD, :].bitcast(I32), tim_scales[0].bitcast(I32))
-            load_plane(head_table, heads, 1, t)
+        def load_scales(c, table):
+            nc.sync.dma_start(scale_table[c][0:P:SPREAD, :].bitcast(I32), table[0].bitcast(I32))
+
+        load_planes(rel_table, rre, 0, 0, 2)
+        nc.sync.dma_start(rel_list[:], offs2)
+        nc.sync.dma_start(tail_list[:], offs3)
+        load_scales(0, tre_scales)
+        load_planes(rel_table, rim, 1, 0, 2)
+        nc.sync.dma_start(head_list[:], offs)
+        load_planes(head_table, hre, 0, 0, 2)
+        load_scales(1, tim_scales)
+        load_planes(head_table, him, 1, 0, 2)
+        load_planes(rel_table, rre, 0, 2, 1)
+        load_planes(rel_table, rim, 1, 2, 1)
+        load_planes(head_table, hre, 0, 2, 1)
+        load_planes(head_table, him, 1, 2, 1)
+        load_planes(rel_table, rim, 1, LAST, 1)
+        load_planes(head_table, hre, 0, LAST, 1)
+        load_planes(rel_table, rre, 0, LAST, 1)
+        load_planes(head_table, him, 1, LAST, 1)
         for c, table in enumerate((tre_words, tim_words)):
             nc.sync.dma_start(word_table[c][:].bitcast(I32), table[0].bitcast(I32))
 
@@ -86,7 +89,7 @@ def tile_attend_complexscores_kernel(tc, hre, him, rre, rim, tre_words, tre_scal
         sums = {}
 
         def gather_rel(rel, c, t):
-            nc.vector.tensor_copy(rel[:, 1 + c, :], rel_table[c][t][:].indirect(rel_list[:]))
+            nc.vector.tensor_copy(rel[:, 1 + c, :], rel_table[c, t].indirect(rel_list[:]))
             if c == 1:
                 nc.scalar.mul(rel[:, 0, :], rel[:, 2, :], -1.0)
 
@@ -117,10 +120,10 @@ def tile_attend_complexscores_kernel(tc, hre, him, rre, rim, tre_words, tre_scal
                 gather_scales(0)
             terms = []
             for c in range(PARTS):
-                if (t, c) == (LAST - 1, PARTS - 1):
+                if (t, c) == (0, PARTS - 1):
                     gather_scales(1)
                 head = keep.tile([P, 1, Q], F32, name="head%d_%d" % (c, t))
-                nc.vector.tensor_copy(head[:, 0, :], head_table[c][t][:].indirect(head_list[:]))
+                nc.vector.tensor_copy(head[:, 0, :], head_table[c, t].indirect(head_list[:]))
                 terms.append(keep.tile([P, PARTS, Q], F32, name="term%d_%d" % (c, t)))
                 if (t, c) == (LAST - 1, PARTS - 1):
                     for s in range(PARTS):
@@ -145,7 +148,7 @@ def tile_attend_complexscores_kernel(tc, hre, him, rre, rim, tre_words, tre_scal
         real_term = [keep.tile([P, Q], F32, name="real_term%d" % s) for s in range(PARTS)]
         imag_term = [keep.tile([P, Q], F32, name="imag_term%d" % s) for s in range(PARTS)]
         gather_rel(rel, 1, LAST)
-        nc.vector.tensor_copy(head[0][:], head_table[0][LAST][:].indirect(head_list[:]))
+        nc.vector.tensor_copy(head[0][:], head_table[0, LAST].indirect(head_list[:]))
         gather_rel(rel, 0, LAST)
         for s in (1, 0):
             nc.gpsimd.tensor_tensor(real_term[s][:], rel[:, 1 + s, :], head[0][:], MULT)
@@ -153,7 +156,7 @@ def tile_attend_complexscores_kernel(tc, hre, him, rre, rim, tre_words, tre_scal
             add_term(b, 1, LAST, real_term[1], 0)
         for b in range(BLOCKS):
             columns = slice(b * P // LIST_GROUP, (b + 1) * P // LIST_GROUP)
-            nc.vector.tensor_copy(head[1][:, b * P : (b + 1) * P], head_table[1][LAST][:].indirect(head_list[:, columns]))
+            nc.vector.tensor_copy(head[1][:, b * P : (b + 1) * P], head_table[1, LAST].indirect(head_list[:, columns]))
         for b in range(BLOCKS):
             queries = slice(b * P, (b + 1) * P)
             nc.vector.tensor_tensor(imag_term[1][:, queries], rel[:, 1, queries], head[1][:, queries], MULT)

@@ -66,21 +66,20 @@ def tile_attend_complexscores_kernel(tc, hre, him, rre, rim, tre_words, tre_scal
         nc.sync.dma_start(rel_list[:], offs2)
         nc.sync.dma_start(tail_list[:], offs3)
         load_scales(0, tre_scales)
-        load_planes(rel_table, rim, 1, 0, 2)
         nc.sync.dma_start(head_list[:], offs)
         load_planes(head_table, hre, 0, 0, 2)
-        load_scales(1, tim_scales)
+        load_planes(rel_table, rim, 1, 0, 2)
         load_planes(head_table, him, 1, 0, 2)
         load_planes(rel_table, rre, 0, 2, 1)
         load_planes(rel_table, rim, 1, 2, 1)
         load_planes(head_table, hre, 0, 2, 1)
+        load_scales(1, tim_scales)
         load_planes(head_table, him, 1, 2, 1)
         load_planes(rel_table, rim, 1, LAST, 1)
         load_planes(head_table, hre, 0, LAST, 1)
         load_planes(rel_table, rre, 0, LAST, 1)
         load_planes(head_table, him, 1, LAST, 1)
-        for c, table in enumerate((tre_words, tim_words)):
-            nc.sync.dma_start(word_table[c][:].bitcast(I32), table[0].bitcast(I32))
+        nc.sync.dma_start(word_table[0][:].bitcast(I32), tre_words[0].bitcast(I32))
 
         units = [(b, s) for s in range(PARTS) for b in range(BLOCKS)]
         turned = {(b, s): psum.tile([P, 2, P], F32, name="turned%d_%d" % (b, s)) for b, s in units}
@@ -120,14 +119,14 @@ def tile_attend_complexscores_kernel(tc, hre, him, rre, rim, tre_words, tre_scal
                 gather_scales(0)
             terms = []
             for c in range(PARTS):
-                if (t, c) == (0, PARTS - 1):
+                if (t, c) == (LAST - 1, PARTS - 1):
                     gather_scales(1)
                 head = keep.tile([P, 1, Q], F32, name="head%d_%d" % (c, t))
                 nc.vector.tensor_copy(head[:, 0, :], head_table[c, t].indirect(head_list[:]))
                 terms.append(keep.tile([P, PARTS, Q], F32, name="term%d_%d" % (c, t)))
-                if (t, c) == (LAST - 1, PARTS - 1):
+                if (t, c) in ((0, 0), (1, 0), (LAST - 1, PARTS - 1)):
                     for s in range(PARTS):
-                        nc.gpsimd.tensor_tensor(terms[c][:, s, :], rel[:, s, :], head[:, 0, :], MULT)
+                        nc.gpsimd.tensor_tensor(terms[c][:, s, :], rel[:, 1 - c + s, :], head[:, 0, :], MULT)
                 else:
                     nc.gpsimd.tensor_tensor(terms[c][:], rel[:, 1 - c : 3 - c, :], head[:].to_broadcast([P, PARTS, Q]), MULT)
             for b, s in units:
@@ -142,6 +141,7 @@ def tile_attend_complexscores_kernel(tc, hre, him, rre, rim, tre_words, tre_scal
 
         for r in range(QUADRANT // SPREAD):
             nc.sync.dma_start(tail_scales[r:P:QUADRANT, :].bitcast(I32), picked_scales[SPREAD * r : P : QUADRANT, :].bitcast(I32))
+        nc.sync.dma_start(word_table[1][:].bitcast(I32), tim_words[0].bitcast(I32))
 
         rel = keep.tile([P, 3, Q], F32, name="rel%d" % LAST)
         head = [keep.tile([P, Q], F32, name="head%d_%d" % (c, LAST)) for c in range(PARTS)]

@@ -69,17 +69,18 @@ def tile_attend_complexscores_kernel(tc, hre, him, rre, rim, tre_words, tre_scal
         nc.sync.dma_start(head_list[:], offs)
         load_planes(head_table, hre, 0, 0, 2)
         load_planes(rel_table, rim, 1, 0, 2)
+        load_scales(1, tim_scales)
         load_planes(head_table, him, 1, 0, 2)
         load_planes(rel_table, rre, 0, 2, 1)
         load_planes(rel_table, rim, 1, 2, 1)
         load_planes(head_table, hre, 0, 2, 1)
-        load_scales(1, tim_scales)
         load_planes(head_table, him, 1, 2, 1)
         load_planes(rel_table, rim, 1, LAST, 1)
         load_planes(head_table, hre, 0, LAST, 1)
         load_planes(rel_table, rre, 0, LAST, 1)
         load_planes(head_table, him, 1, LAST, 1)
-        nc.sync.dma_start(word_table[0][:].bitcast(I32), tre_words[0].bitcast(I32))
+        for c, table in enumerate((tre_words, tim_words)):
+            nc.sync.dma_start(word_table[c][:].bitcast(I32), table[0].bitcast(I32))
 
         units = [(b, s) for s in range(PARTS) for b in range(BLOCKS)]
         turned = {(b, s): psum.tile([P, 2, P], F32, name="turned%d_%d" % (b, s)) for b, s in units}
@@ -119,7 +120,7 @@ def tile_attend_complexscores_kernel(tc, hre, him, rre, rim, tre_words, tre_scal
                 gather_scales(0)
             terms = []
             for c in range(PARTS):
-                if (t, c) == (LAST - 1, PARTS - 1):
+                if (t, c) == (0, PARTS - 1):
                     gather_scales(1)
                 head = keep.tile([P, 1, Q], F32, name="head%d_%d" % (c, t))
                 nc.vector.tensor_copy(head[:, 0, :], head_table[c, t].indirect(head_list[:]))
@@ -141,7 +142,6 @@ def tile_attend_complexscores_kernel(tc, hre, him, rre, rim, tre_words, tre_scal
 
         for r in range(QUADRANT // SPREAD):
             nc.sync.dma_start(tail_scales[r:P:QUADRANT, :].bitcast(I32), picked_scales[SPREAD * r : P : QUADRANT, :].bitcast(I32))
-        nc.sync.dma_start(word_table[1][:].bitcast(I32), tim_words[0].bitcast(I32))
 
         rel = keep.tile([P, 3, Q], F32, name="rel%d" % LAST)
         head = [keep.tile([P, Q], F32, name="head%d_%d" % (c, LAST)) for c in range(PARTS)]

@@ -83,7 +83,7 @@ def tile_attend_complexscores_kernel(tc, hre, him, rre, rim, tre_words, tre_scal
             nc.sync.dma_start(word_table[c][:].bitcast(I32), table[0].bitcast(I32))
 
         units = [(b, s) for s in range(PARTS) for b in range(BLOCKS)]
-        turned = {(b, s): psum.tile([P, 2, P], F32, name="turned%d_%d" % (b, s)) for b, s in units}
+        turned = {(b, s): psum.tile([P, 2, P], F32, name="turned%d_%d" % (b, s), tag="bank%d" % (len(units) + n)) for n, (b, s) in enumerate(units)}
         grouped = [keep.tile([P, Q, PACK], BF16, name="grouped%d" % s, tag="grouped%d" % s, align_bytes=MX_ALIGN) for s in range(PARTS)]
         picked_scales = keep.tile([P, PARTS * I], U8, name="picked_scales")
         sums = {}
@@ -174,41 +174,44 @@ def tile_attend_complexscores_kernel(tc, hre, him, rre, rim, tre_words, tre_scal
             nc.vector.quantize_mx(out=codes[:].bitcast(FP8X4), scales=query_scales[:], in_=grouped[s][:].rearrange("p q t -> p (q t)"))
             return codes, query_scales
 
-        halves = [(h, b) for h in range(2) for b in range(BLOCKS)]
-        scores = {(h, b): psum.tile([P, HALF], F32, name="scores%d_%d" % (h, b), tag="bank%d" % (len(units) - 1 - n)) for n, (h, b) in enumerate(halves)}
+        pieces = [(0, HALF, b) for b in range(BLOCKS)] + [(first, P, b) for first in range(HALF, I, P) for b in range(BLOCKS)]
+        banks = [3, 2, 1, 0, 4, 5]
+        scores = {piece: psum.tile([P, piece[1]], F32, name="scores%d" % n, tag="bank%d" % banks[n]) for n, piece in enumerate(pieces)}
 
-        def multiply(h, b, s, operand, words):
+        def multiply(piece, s, operand, words, words_first):
+            first, width, b = piece
             codes, query_scales = operand
             queries = slice(b * P, (b + 1) * P)
-            for k in range(HALF // P):
-                first = s * I + h * HALF + k * P
+            for k in range(0, width, P):
+                column = first + k
                 nc.tensor.matmul_mx(
-                    out=scores[h, b][:, k * P : (k + 1) * P],
+                    out=scores[piece][:, k : k + P],
                     lhsT=codes[:, queries].bitcast(FP8X4),
                     lhsT_scale=query_scales[:, queries],
-                    rhs=words[:, k * P : (k + 1) * P].bitcast(FP4X4),
-                    rhs_scale=tail_scales[:, first : first + P],
+                    rhs=words[:, column - words_first : column - words_first + P].bitcast(FP4X4),
+                    rhs_scale=tail_scales[:, s * I + column : s * I + column + P],
                     start=((s, k) == (0, 0)),
-                    stop=((s, k) == (PARTS - 1, HALF // P - 1)),
+                    stop=((s, k) == (PARTS - 1, width - P)),
                 )
 
         real_words = keep.tile([P, I], U16, name="real_words", align_bytes=MX_ALIGN)
         gather_words(real_words, 0, 0, I)
         x_operand = quantise(0, "word_table0")
-        for h, b in halves:
-            multiply(h, b, 0, x_operand, real_words[:, h * HALF : (h + 1) * HALF])
+        for piece in pieces:
+            multiply(piece, 0, x_operand, real_words, 0)
         imag_words = []
         for h in range(2):
             imag_words.append(keep.tile([P, HALF], U16, name="imag_words%d" % h, tag="grouped%d" % h, align_bytes=MX_ALIGN))
             gather_words(imag_words[h], 1, h * HALF, HALF)
             if h == 0:
                 z_operand = quantise(1, "query_codes1")
-        for h, b in halves:
-            multiply(h, b, 1, z_operand, imag_words[h][:])
-            result = keep.tile([P, HALF], F32, name="result%d_%d" % (h, b))
-            if (h, b) == halves[-1]:
-                nc.vector.tensor_copy(result[:], scores[h, b][:])
-            else:
-                nc.scalar.copy(result[:], scores[h, b][:])
-            queue = nc.scalar if (h, b) == halves[-2] else nc.sync
-            queue.dma_start(out[b * P : (b + 1) * P, h * HALF : (h + 1) * HALF], result[:])
+        results = {(h, b): keep.tile([P, HALF], F32, name="result%d_%d" % (h, b)) for h in range(2) for b in range(BLOCKS)}
+        for piece in pieces:
+            first, width, b = piece
+            h, offset = divmod(first, HALF)
+            multiply(piece, 1, z_operand, imag_words[h], h * HALF)
+            copy = nc.scalar.copy if b == 0 else nc.vector.tensor_copy
+            copy(results[h, b][:, offset : offset + width], scores[piece][:])
+            if offset + width == HALF:
+                queue = nc.scalar if (h, b) == (1, 0) else nc.sync
+                queue.dma_start(out[b * P : (b + 1) * P, h * HALF : (h + 1) * HALF], results[h, b][:])

@@ -84,7 +84,11 @@ def tile_attend_complexscores_kernel(tc, hre, him, rre, rim, tre_words, tre_scal
 
         units = [(b, s) for s in range(PARTS) for b in range(BLOCKS)]
         turned = {(b, s): psum.tile([P, 2, P], F32, name="turned%d_%d" % (b, s), tag="bank%d" % (len(units) + n)) for n, (b, s) in enumerate(units)}
-        grouped = [keep.tile([P, Q, PACK], BF16, name="grouped%d" % s, tag="grouped%d" % s, align_bytes=MX_ALIGN) for s in range(PARTS)]
+        grouped_x = keep.tile([P, Q, PACK], BF16, name="grouped_x", tag="grouped_x", align_bytes=MX_ALIGN)
+        grouped_z = [keep.tile([P, P, PACK], BF16, name="grouped_z%d" % b, tag="grouped_z%d" % b, align_bytes=MX_ALIGN) for b in range(BLOCKS)]
+        grouped = [[grouped_x[:]], [tile[:] for tile in grouped_z]]
+        by_block = {(b, 0): grouped_x[:, b * P : (b + 1) * P, :] for b in range(BLOCKS)}
+        by_block.update({(b, 1): grouped_z[b][:] for b in range(BLOCKS)})
         picked_scales = keep.tile([P, PARTS * I], U8, name="picked_scales")
         sums = {}
 
@@ -106,7 +110,7 @@ def tile_attend_complexscores_kernel(tc, hre, him, rre, rim, tre_words, tre_scal
                 nc.tensor.transpose(turned[b, s][:, u, :], pairs[:].rearrange("q p e -> q (p e)").bitcast(F32), ident[:])
             if u == 1:
                 for b in range(BLOCKS):
-                    words = grouped[s][:, b * P : (b + 1) * P, :].rearrange("p q t -> p (q t)").bitcast(F32)
+                    words = by_block[b, s].rearrange("p q t -> p (q t)").bitcast(F32)
                     nc.scalar.copy(words.rearrange("p (q u) -> p q u", u=2), turned[b, s][:].rearrange("p u q -> p q u"))
 
         def gather_scales(c):
@@ -162,32 +166,34 @@ def tile_attend_complexscores_kernel(tc, hre, him, rre, rim, tre_words, tre_scal
             nc.vector.tensor_tensor(imag_term[1][:, queries], rel[:, 1, queries], head[1][:, queries], MULT)
             add_term(b, 1, LAST, imag_term[1], 1)
         nc.vector.tensor_tensor(imag_term[0][:], rel[:, 0, :], head[1][:], MULT)
-        nc.gpsimd.tensor_tensor(grouped[0][:, :, LAST], real_term[0][:], imag_term[0][:], ADD)
+        nc.gpsimd.tensor_tensor(grouped_x[:, :, LAST], real_term[0][:], imag_term[0][:], ADD)
         turn_back(1, 1, 2)
 
         def gather_words(tile, c, first, count):
             nc.vector.tensor_copy(tile[:], word_table[c][:].indirect(tail_list[:, first // LIST_GROUP : (first + count) // LIST_GROUP]))
 
-        def quantise(s, tag):
-            codes = keep.tile([P, Q], U32, name="query_codes%d" % s, tag=tag, align_bytes=MX_ALIGN)
-            query_scales = keep.tile([P, Q], U8, name="query_scales%d" % s, align_bytes=MX_ALIGN)
-            nc.vector.quantize_mx(out=codes[:].bitcast(FP8X4), scales=query_scales[:], in_=grouped[s][:].rearrange("p q t -> p (q t)"))
-            return codes, query_scales
+        def quantise(s, first, count, tag):
+            codes = keep.tile([P, count], U32, name="query_codes%d_%d" % (s, first), tag=tag, align_bytes=MX_ALIGN)
+            query_scales = keep.tile([P, count], U8, name="query_scales%d_%d" % (s, first), align_bytes=MX_ALIGN)
+            nc.vector.quantize_mx(out=codes[:].bitcast(FP8X4), scales=query_scales[:], in_=grouped[s][first // P].rearrange("p q t -> p (q t)"))
+            for b in range(first // P, (first + count) // P):
+                queries = slice(b * P - first, (b + 1) * P - first)
+                operands[b, s] = codes[:, queries], query_scales[:, queries]
 
-        pieces = [(0, HALF, b) for b in range(BLOCKS)] + [(first, P, b) for first in range(HALF, I, P) for b in range(BLOCKS)]
-        banks = [3, 2, 1, 0, 4, 5]
+        operands = {}
+        pieces = [(0, HALF, 0), (HALF, HALF, 0), (0, HALF, 1), (HALF, P, 1), (HALF + P, P, 1)]
+        banks = [3, 2, 1, 0, 4]
         scores = {piece: psum.tile([P, piece[1]], F32, name="scores%d" % n, tag="bank%d" % banks[n]) for n, piece in enumerate(pieces)}
 
-        def multiply(piece, s, operand, words, words_first):
+        def multiply(piece, s, words, words_first):
             first, width, b = piece
-            codes, query_scales = operand
-            queries = slice(b * P, (b + 1) * P)
+            codes, query_scales = operands[b, s]
             for k in range(0, width, P):
                 column = first + k
                 nc.tensor.matmul_mx(
                     out=scores[piece][:, k : k + P],
-                    lhsT=codes[:, queries].bitcast(FP8X4),
-                    lhsT_scale=query_scales[:, queries],
+                    lhsT=codes.bitcast(FP8X4),
+                    lhsT_scale=query_scales,
                     rhs=words[:, column - words_first : column - words_first + P].bitcast(FP4X4),
                     rhs_scale=tail_scales[:, s * I + column : s * I + column + P],
                     start=((s, k) == (0, 0)),
@@ -196,22 +202,20 @@ def tile_attend_complexscores_kernel(tc, hre, him, rre, rim, tre_words, tre_scal
 
         real_words = keep.tile([P, I], U16, name="real_words", align_bytes=MX_ALIGN)
         gather_words(real_words, 0, 0, I)
-        x_operand = quantise(0, "word_table0")
+        quantise(0, 0, Q, "word_table0")
         for piece in pieces:
-            multiply(piece, 0, x_operand, real_words, 0)
+            multiply(piece, 0, real_words, 0)
         imag_words = []
         for h in range(2):
-            imag_words.append(keep.tile([P, HALF], U16, name="imag_words%d" % h, tag="grouped%d" % h, align_bytes=MX_ALIGN))
+            imag_words.append(keep.tile([P, HALF], U16, name="imag_words%d" % h, tag=("grouped_x", "grouped_z0")[h], align_bytes=MX_ALIGN))
             gather_words(imag_words[h], 1, h * HALF, HALF)
-            if h == 0:
-                z_operand = quantise(1, "query_codes1")
+            quantise(1, h * P, P, ("query_codes_z0", "word_table1")[h])
         results = {(h, b): keep.tile([P, HALF], F32, name="result%d_%d" % (h, b)) for h in range(2) for b in range(BLOCKS)}
-        for piece in pieces:
+        for n, piece in enumerate(pieces):
             first, width, b = piece
             h, offset = divmod(first, HALF)
-            multiply(piece, 1, z_operand, imag_words[h], h * HALF)
-            copy = nc.scalar.copy if b == 0 else nc.vector.tensor_copy
+            multiply(piece, 1, imag_words[h], h * HALF)
+            copy = nc.vector.tensor_copy if n in (2, 4) else nc.scalar.copy
             copy(results[h, b][:, offset : offset + width], scores[piece][:])
             if offset + width == HALF:
-                queue = nc.scalar if (h, b) == (1, 0) else nc.sync
-                queue.dma_start(out[b * P : (b + 1) * P, h * HALF : (h + 1) * HALF], results[h, b][:])
+                nc.sync.dma_start(out[b * P : (b + 1) * P, h * HALF : (h + 1) * HALF], results[h, b][:])

@@ -1,7 +1,6 @@
 from contextlib import ExitStack
 
 import concourse.mybir as mybir
-from concourse.masks import make_identity
 
 D, T, U, Q, V, I = 512, 1024, 512, 256, 2048, 512
 FLOPS = 2 * 2 * D * Q * I
@@ -15,7 +14,8 @@ U8 = mybir.dt.uint8
 FP8X4 = mybir.dt.float8_e4m3fn_x4
 FP4X4 = mybir.dt.float4_e2m1fn_x4
 MULT = mybir.AluOpType.mult
-ADD = mybir.AluOpType.add
+COMBINE = (mybir.AluOpType.subtract, mybir.AluOpType.add)
+COPY = mybir.ActivationFunctionType.Copy
 
 P = 128
 BLOCKS = Q // P
@@ -43,11 +43,9 @@ def tile_attend_complexscores_kernel(tc, hre, him, rre, rim, tre_words, tre_scal
 
         scale_table = [keep.tile([P, V], U8, name="scale_table%d" % c) for c in range(PARTS)]
         for c in range(PARTS):
-            nc.vector.memset(scale_table[c][:].bitcast(I32), 0)
+            nc.gpsimd.memset(scale_table[c][:].bitcast(I32), 0)
         tail_scales = keep.tile([P, PARTS * I], U8, name="tail_scales", align_bytes=MX_ALIGN)
         nc.gpsimd.memset(tail_scales[:].bitcast(I32), 0)
-        ident = keep.tile([P, P], F32, name="ident")
-        make_identity(nc, ident[:])
 
         word_table = [keep.tile([P, V], U16, name="word_table%d" % c, tag="word_table%d" % c, align_bytes=MX_ALIGN) for c in range(PARTS)]
         rel_table, head_table = {}, {}
@@ -58,158 +56,123 @@ def tile_attend_complexscores_kernel(tc, hre, him, rre, rim, tre_words, tre_scal
             nc.sync.dma_start(tile[:], table.rearrange("(p t) w -> p t w", t=PACK)[:, first : first + count, :])
             for n in range(count):
                 windows[c, first + n] = tile[:, n, :]
+            windows[c, first] = tile[:].rearrange("p t w -> p (t w)")
 
         def load_scales(c, table):
             nc.sync.dma_start(scale_table[c][0:P:SPREAD, :].bitcast(I32), table[0].bitcast(I32))
 
-        load_planes(rel_table, rre, 0, 0, 2)
+        load_planes(rel_table, rre, 0, 0, LAST)
         nc.sync.dma_start(rel_list[:], offs2)
         nc.sync.dma_start(tail_list[:], offs3)
         load_scales(0, tre_scales)
+        load_planes(rel_table, rim, 1, 0, LAST)
+        load_scales(1, tim_scales)
         nc.sync.dma_start(head_list[:], offs)
         load_planes(head_table, hre, 0, 0, 2)
-        load_planes(rel_table, rim, 1, 0, 2)
-        load_scales(1, tim_scales)
         load_planes(head_table, him, 1, 0, 2)
-        load_planes(rel_table, rre, 0, 2, 1)
-        load_planes(rel_table, rim, 1, 2, 1)
         load_planes(head_table, hre, 0, 2, 1)
         load_planes(head_table, him, 1, 2, 1)
+        load_planes(rel_table, rre, 0, LAST, 1)
         load_planes(rel_table, rim, 1, LAST, 1)
         load_planes(head_table, hre, 0, LAST, 1)
-        load_planes(rel_table, rre, 0, LAST, 1)
         load_planes(head_table, him, 1, LAST, 1)
         for c, table in enumerate((tre_words, tim_words)):
             nc.sync.dma_start(word_table[c][:].bitcast(I32), table[0].bitcast(I32))
 
-        units = [(b, s) for s in range(PARTS) for b in range(BLOCKS)]
-        turned = {(b, s): psum.tile([P, 2, P], F32, name="turned%d_%d" % (b, s), tag="bank%d" % (len(units) + n)) for n, (b, s) in enumerate(units)}
         grouped_x = keep.tile([P, Q, PACK], BF16, name="grouped_x", tag="grouped_x", align_bytes=MX_ALIGN)
         grouped_z = [keep.tile([P, P, PACK], BF16, name="grouped_z%d" % b, tag="grouped_z%d" % b, align_bytes=MX_ALIGN) for b in range(BLOCKS)]
-        grouped = [[grouped_x[:]], [tile[:] for tile in grouped_z]]
-        by_block = {(b, 0): grouped_x[:, b * P : (b + 1) * P, :] for b in range(BLOCKS)}
-        by_block.update({(b, 1): grouped_z[b][:] for b in range(BLOCKS)})
         picked_scales = keep.tile([P, PARTS * I], U8, name="picked_scales")
-        sums = {}
 
-        def gather_rel(rel, c, t):
-            nc.vector.tensor_copy(rel[:, 1 + c, :], rel_table[c, t].indirect(rel_list[:]))
-            if c == 1:
-                nc.scalar.mul(rel[:, 0, :], rel[:, 2, :], -1.0)
+        rel = [keep.tile([P, PARTS, Q], F32, name="rel%d" % t) for t in range(PACK)]
+        head = {(c, t): keep.tile([P, 1, Q], F32, name="head%d_%d" % (c, t)) for c in range(PARTS) for t in range(PACK)}
+        terms = [keep.tile([P, LAST, PARTS, Q], F32, name="terms%d" % c) for c in range(PARTS)]
+        last_terms = [keep.tile([P, PARTS, Q], F32, name="last_terms%d" % c) for c in range(PARTS)]
 
-        def add_term(b, s, t, term, c):
-            u, e = divmod(t, 2)
-            if (c, e) == (0, 0):
-                sums[b, s] = psum.tile([P, 2, P], F32, name="sums%d_%d_%d" % (u, b, s), tag="bank%d" % units.index((b, s)))
-            nc.tensor.matmul(sums[b, s][:, e, :], lhsT=term[:, b * P : (b + 1) * P], rhs=ident[:], is_transpose=True, start=(c == 0), stop=(c == PARTS - 1))
-
-        def turn_back(s, u, summed):
-            for b in range(BLOCKS):
-                pairs = keep.tile([P, P, 2], BF16, name="pairs%d_%d_%d" % (u, b, s))
-                nc.scalar.copy(pairs[:], sums[b, s][:, 0:summed, :].rearrange("q e p -> q p e").to_broadcast([P, P, 2]))
-                nc.tensor.transpose(turned[b, s][:, u, :], pairs[:].rearrange("q p e -> q (p e)").bitcast(F32), ident[:])
-            if u == 1:
-                for b in range(BLOCKS):
-                    words = by_block[b, s].rearrange("p q t -> p (q t)").bitcast(F32)
-                    nc.scalar.copy(words.rearrange("p (q u) -> p q u", u=2), turned[b, s][:].rearrange("p u q -> p q u"))
-
-        def gather_scales(c):
+        for c in range(PARTS):
+            nc.scalar.activation(rel[0][:, c, :], rel_table[c, 0].indirect(rel_list[:]), COPY)
+            for t in range(1, LAST):
+                nc.vector.tensor_copy(rel[t][:, c, :], rel_table[c, t].indirect(rel_list[:]))
             nc.vector.tensor_copy(picked_scales[:, c * I : (c + 1) * I], scale_table[c][:].indirect(tail_list[:]))
+        for c, t in ((0, 0), (0, 1), (1, 0), (1, 1), (0, 2), (1, 2)):
+            if c == 1 and t != 1:
+                nc.vector.tensor_copy(head[c, t][:, 0, :], head_table[c, t].indirect(head_list[:]))
+            else:
+                nc.scalar.activation(head[c, t][:, 0, :], head_table[c, t].indirect(head_list[:]), COPY)
+            if (c, t) == (1, 2):
+                for r in (1, 0):
+                    nc.vector.tensor_tensor(terms[c][:, t, r, :], rel[t][:, r, :], head[c, t][:, 0, :], MULT)
+            else:
+                engine = nc.gpsimd if (c, t) == (0, 2) else nc.vector
+                engine.tensor_tensor(terms[c][:, t, :, :], rel[t][:], head[c, t][:].to_broadcast([P, PARTS, Q]), MULT)
 
-        for t in range(LAST):
-            rel = keep.tile([P, 3, Q], F32, name="rel%d" % t)
-            for c in range(PARTS):
-                gather_rel(rel, c, t)
-            if t == 0:
-                gather_scales(0)
-            terms = []
-            for c in range(PARTS):
-                if (t, c) == (0, PARTS - 1):
-                    gather_scales(1)
-                head = keep.tile([P, 1, Q], F32, name="head%d_%d" % (c, t))
-                nc.vector.tensor_copy(head[:, 0, :], head_table[c, t].indirect(head_list[:]))
-                terms.append(keep.tile([P, PARTS, Q], F32, name="term%d_%d" % (c, t)))
-                if (t, c) in ((0, 0), (1, 0), (LAST - 1, PARTS - 1)):
-                    for s in range(PARTS):
-                        nc.gpsimd.tensor_tensor(terms[c][:, s, :], rel[:, 1 - c + s, :], head[:, 0, :], MULT)
-                else:
-                    nc.gpsimd.tensor_tensor(terms[c][:], rel[:, 1 - c : 3 - c, :], head[:].to_broadcast([P, PARTS, Q]), MULT)
-            for b, s in units:
-                add_term(b, s, t, terms[0][:, s, :], 0)
-            for s in range(PARTS):
-                for b in range(BLOCKS):
-                    add_term(b, s, t, terms[1][:, s, :], 1)
-                if t == 1:
-                    turn_back(s, 0, 2)
-                elif (t, s) == (LAST - 1, 0):
-                    turn_back(s, 1, 1)
+        def add_first_planes(s, words, queries):
+            nc.vector.tensor_tensor(
+                words.rearrange("p (n i) t -> p n t i", i=2)[:, :, 0:LAST, :],
+                terms[0][:, :, s, queries].rearrange("p t (n i) -> p n t i", i=2),
+                terms[1][:, :, 1 - s, queries].rearrange("p t (n i) -> p n t i", i=2),
+                COMBINE[s],
+            )
+
+        add_first_planes(0, grouped_x[:], slice(0, Q))
+        for b in range(BLOCKS):
+            add_first_planes(1, grouped_z[b][:], slice(b * P, (b + 1) * P))
 
         for r in range(QUADRANT // SPREAD):
             nc.sync.dma_start(tail_scales[r:P:QUADRANT, :].bitcast(I32), picked_scales[SPREAD * r : P : QUADRANT, :].bitcast(I32))
 
-        rel = keep.tile([P, 3, Q], F32, name="rel%d" % LAST)
-        head = [keep.tile([P, Q], F32, name="head%d_%d" % (c, LAST)) for c in range(PARTS)]
-        real_term = [keep.tile([P, Q], F32, name="real_term%d" % s) for s in range(PARTS)]
-        imag_term = [keep.tile([P, Q], F32, name="imag_term%d" % s) for s in range(PARTS)]
-        gather_rel(rel, 1, LAST)
-        nc.vector.tensor_copy(head[0][:], head_table[0, LAST].indirect(head_list[:]))
-        gather_rel(rel, 0, LAST)
-        for s in (1, 0):
-            nc.gpsimd.tensor_tensor(real_term[s][:], rel[:, 1 + s, :], head[0][:], MULT)
-        for b in range(BLOCKS):
-            add_term(b, 1, LAST, real_term[1], 0)
-        for b in range(BLOCKS):
-            columns = slice(b * P // LIST_GROUP, (b + 1) * P // LIST_GROUP)
-            nc.vector.tensor_copy(head[1][:, b * P : (b + 1) * P], head_table[1, LAST].indirect(head_list[:, columns]))
+        for c in range(PARTS):
+            nc.scalar.activation(rel[LAST][:, c, :], rel_table[c, LAST].indirect(rel_list[:]), COPY)
+        nc.scalar.activation(head[0, LAST][:, 0, :], head_table[0, LAST].indirect(head_list[:]), COPY)
+        nc.vector.tensor_tensor(last_terms[0][:], rel[LAST][:], head[0, LAST][:].to_broadcast([P, PARTS, Q]), MULT)
+        columns = P // LIST_GROUP
         for b in range(BLOCKS):
             queries = slice(b * P, (b + 1) * P)
-            nc.vector.tensor_tensor(imag_term[1][:, queries], rel[:, 1, queries], head[1][:, queries], MULT)
-            add_term(b, 1, LAST, imag_term[1], 1)
-        nc.vector.tensor_tensor(imag_term[0][:], rel[:, 0, :], head[1][:], MULT)
-        nc.gpsimd.tensor_tensor(grouped_x[:, :, LAST], real_term[0][:], imag_term[0][:], ADD)
-        turn_back(1, 1, 2)
+            nc.scalar.activation(head[1, LAST][:, 0, queries], head_table[1, LAST].indirect(head_list[:, b * columns : (b + 1) * columns]), COPY)
+            nc.vector.tensor_tensor(last_terms[1][:, :, queries], rel[LAST][:, :, queries], head[1, LAST][:, :, queries].to_broadcast([P, PARTS, P]), MULT)
+        for s in range(PARTS):
+            for b in range(BLOCKS):
+                queries = slice(b * P, (b + 1) * P)
+                words = grouped_z[b][:] if s else grouped_x[:, queries, :]
+                nc.gpsimd.tensor_tensor(words[:, :, LAST], last_terms[0][:, s, queries], last_terms[1][:, 1 - s, queries], COMBINE[s])
 
         def gather_words(tile, c, first, count):
             nc.vector.tensor_copy(tile[:], word_table[c][:].indirect(tail_list[:, first // LIST_GROUP : (first + count) // LIST_GROUP]))
 
-        def quantise(s, first, count, tag):
+        def quantise(s, words, first, count, tag):
             codes = keep.tile([P, count], U32, name="query_codes%d_%d" % (s, first), tag=tag, align_bytes=MX_ALIGN)
             query_scales = keep.tile([P, count], U8, name="query_scales%d_%d" % (s, first), align_bytes=MX_ALIGN)
-            nc.vector.quantize_mx(out=codes[:].bitcast(FP8X4), scales=query_scales[:], in_=grouped[s][first // P].rearrange("p q t -> p (q t)"))
+            nc.vector.quantize_mx(out=codes[:].bitcast(FP8X4), scales=query_scales[:], in_=words.rearrange("p q t -> p (q t)"))
             for b in range(first // P, (first + count) // P):
                 queries = slice(b * P - first, (b + 1) * P - first)
                 operands[b, s] = codes[:, queries], query_scales[:, queries]
 
         operands = {}
         pieces = [(0, HALF, 0), (HALF, HALF, 0), (0, HALF, 1), (HALF, P, 1), (HALF + P, P, 1)]
-        banks = [3, 2, 1, 0, 4]
-        scores = {piece: psum.tile([P, piece[1]], F32, name="scores%d" % n, tag="bank%d" % banks[n]) for n, piece in enumerate(pieces)}
+        scores = {piece: psum.tile([P, piece[1]], F32, name="scores%d" % n) for n, piece in enumerate(pieces)}
 
         def multiply(piece, s, words, words_first):
             first, width, b = piece
             codes, query_scales = operands[b, s]
-            for k in range(0, width, P):
-                column = first + k
-                nc.tensor.matmul_mx(
-                    out=scores[piece][:, k : k + P],
-                    lhsT=codes.bitcast(FP8X4),
-                    lhsT_scale=query_scales,
-                    rhs=words[:, column - words_first : column - words_first + P].bitcast(FP4X4),
-                    rhs_scale=tail_scales[:, s * I + column : s * I + column + P],
-                    start=((s, k) == (0, 0)),
-                    stop=((s, k) == (PARTS - 1, width - P)),
-                )
+            nc.tensor.matmul_mx(
+                out=scores[piece][:],
+                lhsT=codes.bitcast(FP8X4),
+                lhsT_scale=query_scales,
+                rhs=words[:, first - words_first : first - words_first + width].bitcast(FP4X4),
+                rhs_scale=tail_scales[:, s * I + first : s * I + first + width],
+                start=(s == 0),
+                stop=(s == PARTS - 1),
+            )
 
         real_words = keep.tile([P, I], U16, name="real_words", align_bytes=MX_ALIGN)
         gather_words(real_words, 0, 0, I)
-        quantise(0, 0, Q, "word_table0")
+        quantise(0, grouped_x[:], 0, Q, "word_table0")
         for piece in pieces:
             multiply(piece, 0, real_words, 0)
         imag_words = []
         for h in range(2):
             imag_words.append(keep.tile([P, HALF], U16, name="imag_words%d" % h, tag=("grouped_x", "grouped_z0")[h], align_bytes=MX_ALIGN))
             gather_words(imag_words[h], 1, h * HALF, HALF)
-            quantise(1, h * P, P, ("query_codes_z0", "word_table1")[h])
+            quantise(1, grouped_z[h][:], h * P, P, ("query_codes_z0", "word_table1")[h])
         results = {(h, b): keep.tile([P, HALF], F32, name="result%d_%d" % (h, b)) for h in range(2) for b in range(BLOCKS)}
         for n, piece in enumerate(pieces):
             first, width, b = piece

@@ -79,8 +79,8 @@ def tile_attend_complexscores_kernel(tc, hre, him, rre, rim, tre_words, tre_scal
         for c, table in enumerate((tre_words, tim_words)):
             nc.sync.dma_start(word_table[c][:].bitcast(I32), table[0].bitcast(I32))
 
-        grouped_x = keep.tile([P, Q, PACK], BF16, name="grouped_x", tag="grouped_x", align_bytes=MX_ALIGN)
-        grouped_z = [keep.tile([P, P, PACK], BF16, name="grouped_z%d" % b, tag="grouped_z%d" % b, align_bytes=MX_ALIGN) for b in range(BLOCKS)]
+        grouped_x = [keep.tile([P, P, PACK], BF16, name="grouped_x%d" % b, tag="grouped_x%d" % b, align_bytes=MX_ALIGN) for b in range(BLOCKS)]
+        grouped_z = keep.tile([P, Q, PACK], BF16, name="grouped_z", tag="grouped_z", align_bytes=MX_ALIGN)
         picked_scales = keep.tile([P, PARTS * I], U8, name="picked_scales")
 
         rel = [keep.tile([P, PARTS, Q], F32, name="rel%d" % t) for t in range(PACK)]
@@ -113,50 +113,46 @@ def tile_attend_complexscores_kernel(tc, hre, him, rre, rim, tre_words, tre_scal
                 COMBINE[s],
             )
 
-        add_first_planes(0, grouped_x[:], slice(0, Q))
         for b in range(BLOCKS):
-            add_first_planes(1, grouped_z[b][:], slice(b * P, (b + 1) * P))
+            add_first_planes(0, grouped_x[b][:], slice(b * P, (b + 1) * P))
+        add_first_planes(1, grouped_z[:], slice(0, Q))
 
         for r in range(QUADRANT // SPREAD):
             nc.sync.dma_start(tail_scales[r:P:QUADRANT, :].bitcast(I32), picked_scales[SPREAD * r : P : QUADRANT, :].bitcast(I32))
 
         for c in range(PARTS):
             nc.scalar.activation(rel[LAST][:, c, :], rel_table[c, LAST].indirect(rel_list[:]), COPY)
-        nc.scalar.activation(head[0, LAST][:, 0, :], head_table[0, LAST].indirect(head_list[:]), COPY)
-        nc.vector.tensor_tensor(last_terms[0][:], rel[LAST][:], head[0, LAST][:].to_broadcast([P, PARTS, Q]), MULT)
         columns = P // LIST_GROUP
         for b in range(BLOCKS):
             queries = slice(b * P, (b + 1) * P)
-            nc.scalar.activation(head[1, LAST][:, 0, queries], head_table[1, LAST].indirect(head_list[:, b * columns : (b + 1) * columns]), COPY)
-            nc.vector.tensor_tensor(last_terms[1][:, :, queries], rel[LAST][:, :, queries], head[1, LAST][:, :, queries].to_broadcast([P, PARTS, P]), MULT)
-        for s in range(PARTS):
-            for b in range(BLOCKS):
-                queries = slice(b * P, (b + 1) * P)
-                words = grouped_z[b][:] if s else grouped_x[:, queries, :]
-                nc.gpsimd.tensor_tensor(words[:, :, LAST], last_terms[0][:, s, queries], last_terms[1][:, 1 - s, queries], COMBINE[s])
+            nc.scalar.activation(head[0, LAST][:, 0, queries], head_table[0, LAST].indirect(head_list[:, b * columns : (b + 1) * columns]), COPY)
+            nc.vector.tensor_tensor(last_terms[0][:, :, queries], rel[LAST][:, :, queries], head[0, LAST][:, :, queries].to_broadcast([P, PARTS, P]), MULT)
+        nc.vector.tensor_copy(head[1, LAST][:, 0, 0:P], head_table[1, LAST].indirect(head_list[:, 0:columns]))
+        nc.scalar.activation(head[1, LAST][:, 0, P:Q], head_table[1, LAST].indirect(head_list[:, columns : 2 * columns]), COPY)
+        for r in (1, 0):
+            nc.vector.tensor_tensor(last_terms[1][:, r, :], rel[LAST][:, r, :], head[1, LAST][:, 0, :], MULT)
+        last_x = keep.tile([P, Q], BF16, name="last_x")
+        nc.vector.tensor_tensor(last_x[:], last_terms[0][:, 0, :], last_terms[1][:, 1, :], COMBINE[0])
+        for b in range(BLOCKS):
+            nc.scalar.copy(grouped_x[b][:, :, LAST], last_x[:, b * P : (b + 1) * P])
+        nc.gpsimd.tensor_tensor(grouped_z[:, :, LAST], last_terms[0][:, 1, :], last_terms[1][:, 0, :], COMBINE[1])
 
         def gather_words(tile, c, first, count):
             nc.vector.tensor_copy(tile[:], word_table[c][:].indirect(tail_list[:, first // LIST_GROUP : (first + count) // LIST_GROUP]))
 
-        def quantise(s, words, first, count, tag):
-            codes = keep.tile([P, count], U32, name="query_codes%d_%d" % (s, first), tag=tag, align_bytes=MX_ALIGN)
-            query_scales = keep.tile([P, count], U8, name="query_scales%d_%d" % (s, first), align_bytes=MX_ALIGN)
-            nc.vector.quantize_mx(out=codes[:].bitcast(FP8X4), scales=query_scales[:], in_=words.rearrange("p q t -> p (q t)"))
-            for b in range(first // P, (first + count) // P):
-                queries = slice(b * P - first, (b + 1) * P - first)
-                operands[b, s] = codes[:, queries], query_scales[:, queries]
+        def quantise(s, words, queries):
+            nc.vector.quantize_mx(out=codes[s][:, queries].bitcast(FP8X4), scales=query_scales[s][:, queries], in_=words.rearrange("p q t -> p (q t)"))
 
-        operands = {}
-        pieces = [(0, HALF, 0), (HALF, HALF, 0), (0, HALF, 1), (HALF, P, 1), (HALF + P, P, 1)]
+        pieces = [(0, HALF, 0), (0, HALF, 1), (HALF, HALF, 0), (HALF, P, 1), (HALF + P, P, 1)]
         scores = {piece: psum.tile([P, piece[1]], F32, name="scores%d" % n) for n, piece in enumerate(pieces)}
 
         def multiply(piece, s, words, words_first):
             first, width, b = piece
-            codes, query_scales = operands[b, s]
+            queries = slice(b * P, (b + 1) * P)
             nc.tensor.matmul_mx(
                 out=scores[piece][:],
-                lhsT=codes.bitcast(FP8X4),
-                lhsT_scale=query_scales,
+                lhsT=codes[s][:, queries].bitcast(FP8X4),
+                lhsT_scale=query_scales[s][:, queries],
                 rhs=words[:, first - words_first : first - words_first + width].bitcast(FP4X4),
                 rhs_scale=tail_scales[:, s * I + first : s * I + first + width],
                 start=(s == 0),
@@ -165,20 +161,25 @@ def tile_attend_complexscores_kernel(tc, hre, him, rre, rim, tre_words, tre_scal
 
         real_words = keep.tile([P, I], U16, name="real_words", align_bytes=MX_ALIGN)
         gather_words(real_words, 0, 0, I)
-        quantise(0, grouped_x[:], 0, Q, "word_table0")
-        for piece in pieces:
-            multiply(piece, 0, real_words, 0)
-        imag_words = []
-        for h in range(2):
-            imag_words.append(keep.tile([P, HALF], U16, name="imag_words%d" % h, tag=("grouped_x", "grouped_z0")[h], align_bytes=MX_ALIGN))
-            gather_words(imag_words[h], 1, h * HALF, HALF)
-            quantise(1, grouped_z[h][:], h * P, P, ("query_codes_z0", "word_table1")[h])
+        codes = [keep.tile([P, Q], U32, name="codes_x", tag="word_table0", align_bytes=MX_ALIGN)]
+        query_scales = [keep.tile([P, Q], U8, name="query_scales%d" % s, align_bytes=MX_ALIGN) for s in range(PARTS)]
+        for b in range(BLOCKS):
+            quantise(0, grouped_x[b][:], slice(b * P, (b + 1) * P))
+            for piece in pieces:
+                if piece[2] == b:
+                    multiply(piece, 0, real_words, 0)
+        imag_words = [keep.tile([P, HALF], U16, name="imag_words0", tag="grouped_x1", align_bytes=MX_ALIGN)]
+        gather_words(imag_words[0], 1, 0, HALF)
+        codes.append(keep.tile([P, Q], U32, name="codes_z", tag="grouped_x0", align_bytes=MX_ALIGN))
+        quantise(1, grouped_z[:], slice(0, Q))
+        imag_words.append(keep.tile([P, HALF], U16, name="imag_words1", tag="grouped_z", align_bytes=MX_ALIGN))
+        gather_words(imag_words[1], 1, HALF, HALF)
         results = {(h, b): keep.tile([P, HALF], F32, name="result%d_%d" % (h, b)) for h in range(2) for b in range(BLOCKS)}
-        for n, piece in enumerate(pieces):
+        for piece in pieces:
             first, width, b = piece
             h, offset = divmod(first, HALF)
             multiply(piece, 1, imag_words[h], h * HALF)
-            copy = nc.vector.tensor_copy if n in (2, 4) else nc.scalar.copy
+            copy = nc.vector.tensor_copy if b else nc.scalar.copy
             copy(results[h, b][:, offset : offset + width], scores[piece][:])
             if offset + width == HALF:
                 nc.sync.dma_start(out[b * P : (b + 1) * P, h * HALF : (h + 1) * HALF], results[h, b][:])

@@ -61,21 +61,19 @@ def tile_attend_complexscores_kernel(tc, hre, him, rre, rim, tre_words, tre_scal
         def load_scales(c, table):
             nc.sync.dma_start(scale_table[c][0:P:SPREAD, :].bitcast(I32), table[0].bitcast(I32))
 
-        load_planes(rel_table, rre, 0, 0, LAST)
+        load_planes(rel_table, rre, 0, 0, 2)
         nc.sync.dma_start(rel_list[:], offs2)
         nc.sync.dma_start(tail_list[:], offs3)
         load_scales(0, tre_scales)
-        load_planes(rel_table, rim, 1, 0, LAST)
+        load_planes(rel_table, rim, 1, 0, 2)
         load_scales(1, tim_scales)
         nc.sync.dma_start(head_list[:], offs)
-        load_planes(head_table, hre, 0, 0, 2)
-        load_planes(head_table, him, 1, 0, 2)
-        load_planes(head_table, hre, 0, 2, 1)
-        load_planes(head_table, him, 1, 2, 1)
-        load_planes(rel_table, rre, 0, LAST, 1)
-        load_planes(rel_table, rim, 1, LAST, 1)
-        load_planes(head_table, hre, 0, LAST, 1)
-        load_planes(head_table, him, 1, LAST, 1)
+        for t in range(PACK):
+            if t == 2:
+                load_planes(rel_table, rre, 0, 2, 2)
+                load_planes(rel_table, rim, 1, 2, 2)
+            load_planes(head_table, hre, 0, t, 1)
+            load_planes(head_table, him, 1, t, 1)
         for c, table in enumerate((tre_words, tim_words)):
             nc.sync.dma_start(word_table[c][:].bitcast(I32), table[0].bitcast(I32))
 
@@ -85,57 +83,66 @@ def tile_attend_complexscores_kernel(tc, hre, him, rre, rim, tre_words, tre_scal
 
         rel = [keep.tile([P, PARTS, Q], F32, name="rel%d" % t) for t in range(PACK)]
         head = {(c, t): keep.tile([P, 1, Q], F32, name="head%d_%d" % (c, t)) for c in range(PARTS) for t in range(PACK)}
-        terms = [keep.tile([P, LAST, PARTS, Q], F32, name="terms%d" % c) for c in range(PARTS)]
-        last_terms = [keep.tile([P, PARTS, Q], F32, name="last_terms%d" % c) for c in range(PARTS)]
+        terms = {(c, u): keep.tile([P, 2, PARTS, Q], F32, name="terms%d_%d" % (c, u)) for c in range(PARTS) for u in range(2)}
+        last_x = keep.tile([P, 2, Q], BF16, name="last_x")
 
-        for c in range(PARTS):
-            nc.scalar.activation(rel[0][:, c, :], rel_table[c, 0].indirect(rel_list[:]), COPY)
-            for t in range(1, LAST):
-                nc.vector.tensor_copy(rel[t][:, c, :], rel_table[c, t].indirect(rel_list[:]))
-            nc.vector.tensor_copy(picked_scales[:, c * I : (c + 1) * I], scale_table[c][:].indirect(tail_list[:]))
-        for c, t in ((0, 0), (0, 1), (1, 0), (1, 1), (0, 2), (1, 2)):
-            if c == 1 and t != 1:
-                nc.vector.tensor_copy(head[c, t][:, 0, :], head_table[c, t].indirect(head_list[:]))
-            else:
-                nc.scalar.activation(head[c, t][:, 0, :], head_table[c, t].indirect(head_list[:]), COPY)
-            if (c, t) == (1, 2):
-                for r in (1, 0):
-                    nc.vector.tensor_tensor(terms[c][:, t, r, :], rel[t][:, r, :], head[c, t][:, 0, :], MULT)
-            else:
-                engine = nc.gpsimd if (c, t) == (0, 2) else nc.vector
-                engine.tensor_tensor(terms[c][:, t, :, :], rel[t][:], head[c, t][:].to_broadcast([P, PARTS, Q]), MULT)
+        def gather_rel(c, u):
+            nc.scalar.activation(rel[2 * u][:, c, :], rel_table[c, 2 * u].indirect(rel_list[:]), COPY)
+            nc.vector.tensor_copy(rel[2 * u + 1][:, c, :], rel_table[c, 2 * u + 1].indirect(rel_list[:]))
 
-        def add_first_planes(s, words, queries):
-            nc.vector.tensor_tensor(
-                words.rearrange("p (n i) t -> p n t i", i=2)[:, :, 0:LAST, :],
-                terms[0][:, :, s, queries].rearrange("p t (n i) -> p n t i", i=2),
-                terms[1][:, :, 1 - s, queries].rearrange("p t (n i) -> p n t i", i=2),
+        def gather_head(c, t, first, count):
+            window = head_table[c, t].indirect(head_list[:, first // LIST_GROUP : (first + count) // LIST_GROUP])
+            nc.scalar.activation(head[c, t][:, 0, first : first + count], window, COPY)
+
+        def multiply_both(c, t, first, count):
+            queries = slice(first, first + count)
+            nc.vector.tensor_tensor(terms[c, t // 2][:, t % 2, :, queries], rel[t][:, :, queries], head[c, t][:, :, queries].to_broadcast([P, PARTS, count]), MULT)
+
+        def multiply_each(c, t):
+            for r in (1, 0):
+                nc.vector.tensor_tensor(terms[c, t // 2][:, t % 2, r, :], rel[t][:, r, :], head[c, t][:, 0, :], MULT)
+
+        def add_pair(engine, s, u, words, queries):
+            engine.tensor_tensor(
+                words.rearrange("p (n i) t -> p n t i", i=2)[:, :, 2 * u : 2 * u + 2, :],
+                terms[0, u][:, :, s, queries].rearrange("p t (n i) -> p n t i", i=2),
+                terms[1, u][:, :, 1 - s, queries].rearrange("p t (n i) -> p n t i", i=2),
                 COMBINE[s],
             )
 
+        def add_last_x(e, first, count):
+            queries = slice(first, first + count)
+            nc.vector.tensor_tensor(last_x[:, e, queries], terms[0, 1][:, e, 0, queries], terms[1, 1][:, e, 1, queries], COMBINE[0])
+
+        for c in range(PARTS):
+            gather_rel(c, 0)
+            nc.vector.tensor_copy(picked_scales[:, c * I : (c + 1) * I], scale_table[c][:].indirect(tail_list[:]))
+        for t in range(2):
+            for c in range(PARTS):
+                gather_head(c, t, 0, Q)
+                multiply_both(c, t, 0, Q)
         for b in range(BLOCKS):
-            add_first_planes(0, grouped_x[b][:], slice(b * P, (b + 1) * P))
-        add_first_planes(1, grouped_z[:], slice(0, Q))
+            add_pair(nc.vector, 0, 0, grouped_x[b][:], slice(b * P, (b + 1) * P))
+        add_pair(nc.vector, 1, 0, grouped_z[:], slice(0, Q))
+        for c in range(PARTS):
+            gather_rel(c, 1)
 
         for r in range(QUADRANT // SPREAD):
             nc.sync.dma_start(tail_scales[r:P:QUADRANT, :].bitcast(I32), picked_scales[SPREAD * r : P : QUADRANT, :].bitcast(I32))
 
         for c in range(PARTS):
-            nc.scalar.activation(rel[LAST][:, c, :], rel_table[c, LAST].indirect(rel_list[:]), COPY)
-        columns = P // LIST_GROUP
+            gather_head(c, 2, 0, Q)
+        multiply_both(0, 2, 0, Q)
+        multiply_each(1, 2)
+        add_last_x(0, 0, Q)
+        for c in range(PARTS):
+            for b in range(BLOCKS):
+                gather_head(c, LAST, b * P, P)
+                multiply_both(c, LAST, b * P, P)
         for b in range(BLOCKS):
-            queries = slice(b * P, (b + 1) * P)
-            nc.scalar.activation(head[0, LAST][:, 0, queries], head_table[0, LAST].indirect(head_list[:, b * columns : (b + 1) * columns]), COPY)
-            nc.vector.tensor_tensor(last_terms[0][:, :, queries], rel[LAST][:, :, queries], head[0, LAST][:, :, queries].to_broadcast([P, PARTS, P]), MULT)
-        nc.vector.tensor_copy(head[1, LAST][:, 0, 0:P], head_table[1, LAST].indirect(head_list[:, 0:columns]))
-        nc.scalar.activation(head[1, LAST][:, 0, P:Q], head_table[1, LAST].indirect(head_list[:, columns : 2 * columns]), COPY)
-        for r in (1, 0):
-            nc.vector.tensor_tensor(last_terms[1][:, r, :], rel[LAST][:, r, :], head[1, LAST][:, 0, :], MULT)
-        last_x = keep.tile([P, Q], BF16, name="last_x")
-        nc.vector.tensor_tensor(last_x[:], last_terms[0][:, 0, :], last_terms[1][:, 1, :], COMBINE[0])
-        for b in range(BLOCKS):
-            nc.scalar.copy(grouped_x[b][:, :, LAST], last_x[:, b * P : (b + 1) * P])
-        nc.gpsimd.tensor_tensor(grouped_z[:, :, LAST], last_terms[0][:, 1, :], last_terms[1][:, 0, :], COMBINE[1])
+            add_last_x(1, b * P, P)
+            nc.scalar.copy(grouped_x[b][:, :, 2:PACK], last_x[:, :, b * P : (b + 1) * P].rearrange("p e q -> p q e"))
+        add_pair(nc.gpsimd, 1, 1, grouped_z[:], slice(0, Q))
 
         def gather_words(tile, c, first, count):
             nc.vector.tensor_copy(tile[:], word_table[c][:].indirect(tail_list[:, first // LIST_GROUP : (first + count) // LIST_GROUP]))

@@ -1,6 +1,7 @@
 from contextlib import ExitStack
 
 import concourse.mybir as mybir
+from concourse.masks import make_identity
 
 D, T, U, Q, V, I = 512, 1024, 512, 256, 2048, 512
 FLOPS = 2 * 2 * D * Q * I
@@ -46,6 +47,8 @@ def tile_attend_complexscores_kernel(tc, hre, him, rre, rim, tre_words, tre_scal
             nc.gpsimd.memset(scale_table[c][:].bitcast(I32), 0)
         tail_scales = keep.tile([P, PARTS * I], U8, name="tail_scales", align_bytes=MX_ALIGN)
         nc.gpsimd.memset(tail_scales[:].bitcast(I32), 0)
+        ident = keep.tile([P, P], F32, name="ident")
+        make_identity(nc, ident[:])
 
         word_table = [keep.tile([P, V], U16, name="word_table%d" % c, tag="word_table%d" % c, align_bytes=MX_ALIGN) for c in range(PARTS)]
         rel_table, head_table = {}, {}
@@ -79,6 +82,8 @@ def tile_attend_complexscores_kernel(tc, hre, him, rre, rim, tre_words, tre_scal
 
         grouped_x = [keep.tile([P, P, PACK], BF16, name="grouped_x%d" % b, tag="grouped_x%d" % b, align_bytes=MX_ALIGN) for b in range(BLOCKS)]
         grouped_z = keep.tile([P, Q, PACK], BF16, name="grouped_z", tag="grouped_z", align_bytes=MX_ALIGN)
+        sums = psum.tile([P, 2, P], F32, name="sums")
+        turned = psum.tile([P, P], F32, name="turned")
         picked_scales = keep.tile([P, PARTS * I], U8, name="picked_scales")
 
         rel = [keep.tile([P, PARTS, Q], F32, name="rel%d" % t) for t in range(PACK)]
@@ -98,9 +103,10 @@ def tile_attend_complexscores_kernel(tc, hre, him, rre, rim, tre_words, tre_scal
             queries = slice(first, first + count)
             nc.vector.tensor_tensor(terms[c, t // 2][:, t % 2, :, queries], rel[t][:, :, queries], head[c, t][:, :, queries].to_broadcast([P, PARTS, count]), MULT)
 
-        def multiply_each(c, t):
+        def multiply_each(c, t, first, count):
+            queries = slice(first, first + count)
             for r in (1, 0):
-                nc.vector.tensor_tensor(terms[c, t // 2][:, t % 2, r, :], rel[t][:, r, :], head[c, t][:, 0, :], MULT)
+                nc.vector.tensor_tensor(terms[c, t // 2][:, t % 2, r, queries], rel[t][:, r, queries], head[c, t][:, 0, queries], MULT)
 
         def add_pair(engine, s, u, words, queries):
             engine.tensor_tensor(
@@ -113,6 +119,9 @@ def tile_attend_complexscores_kernel(tc, hre, him, rre, rim, tre_words, tre_scal
         def add_last_x(e, first, count):
             queries = slice(first, first + count)
             nc.vector.tensor_tensor(last_x[:, e, queries], terms[0, 1][:, e, 0, queries], terms[1, 1][:, e, 1, queries], COMBINE[0])
+
+        def add_term(e, c):
+            nc.tensor.matmul(sums[:, e, :], lhsT=terms[c, 1][:, e, 1 - c, 0:P], rhs=ident[:], is_transpose=True, start=(c == 0), stop=(c == PARTS - 1))
 
         for c in range(PARTS):
             gather_rel(c, 0)
@@ -133,16 +142,27 @@ def tile_attend_complexscores_kernel(tc, hre, him, rre, rim, tre_words, tre_scal
         for c in range(PARTS):
             gather_head(c, 2, 0, Q)
         multiply_both(0, 2, 0, Q)
-        multiply_each(1, 2)
+        multiply_each(1, 2, 0, Q)
         add_last_x(0, 0, Q)
+        for c in range(PARTS):
+            add_term(0, c)
         for c in range(PARTS):
             for b in range(BLOCKS):
                 gather_head(c, LAST, b * P, P)
-                multiply_both(c, LAST, b * P, P)
+                if (c, b) == (1, 1):
+                    multiply_each(c, LAST, b * P, P)
+                else:
+                    multiply_both(c, LAST, b * P, P)
+            add_term(1, c)
         for b in range(BLOCKS):
             add_last_x(1, b * P, P)
             nc.scalar.copy(grouped_x[b][:, :, 2:PACK], last_x[:, :, b * P : (b + 1) * P].rearrange("p e q -> p q e"))
-        add_pair(nc.gpsimd, 1, 1, grouped_z[:], slice(0, Q))
+        pairs = keep.tile([P, P, 2], BF16, name="pairs")
+        nc.scalar.copy(pairs[:], sums[:].rearrange("q e p -> q p e"))
+        nc.tensor.transpose(turned[:], pairs[:].rearrange("q p e -> q (p e)").bitcast(F32), ident[:])
+        words = grouped_z[:, 0:P, :].rearrange("p q t -> p (q t)").bitcast(F32).rearrange("p (q u) -> p q u", u=2)
+        nc.scalar.copy(words[:, :, 1], turned[:])
+        add_pair(nc.gpsimd, 1, 1, grouped_z[:, P:Q, :], slice(P, Q))
 
         def gather_words(tile, c, first, count):
             nc.vector.tensor_copy(tile[:], word_table[c][:].indirect(tail_list[:, first // LIST_GROUP : (first + count) // LIST_GROUP]))

@@ -50,7 +50,7 @@ def tile_attend_complexscores_kernel(tc, hre, him, rre, rim, tre_words, tre_scal
         ident = keep.tile([P, P], F32, name="ident")
         make_identity(nc, ident[:])
 
-        word_table = [keep.tile([P, V], U16, name="word_table%d" % c, tag="word_table%d" % c, align_bytes=MX_ALIGN) for c in range(PARTS)]
+        word_table = [keep.tile([P, V], U16, name="word_table%d" % c, align_bytes=MX_ALIGN) for c in range(PARTS)]
         rel_table, head_table = {}, {}
 
         def load_planes(windows, table, c, first, count):
@@ -80,8 +80,8 @@ def tile_attend_complexscores_kernel(tc, hre, him, rre, rim, tre_words, tre_scal
         for c, table in enumerate((tre_words, tim_words)):
             nc.sync.dma_start(word_table[c][:].bitcast(I32), table[0].bitcast(I32))
 
-        grouped_x = [keep.tile([P, P, PACK], BF16, name="grouped_x%d" % b, tag="grouped_x%d" % b, align_bytes=MX_ALIGN) for b in range(BLOCKS)]
-        grouped_z = keep.tile([P, Q, PACK], BF16, name="grouped_z", tag="grouped_z", align_bytes=MX_ALIGN)
+        grouped_x = [keep.tile([P, P, PACK], BF16, name="grouped_x%d" % b, align_bytes=MX_ALIGN) for b in range(BLOCKS)]
+        grouped_z = keep.tile([P, Q, PACK], BF16, name="grouped_z", align_bytes=MX_ALIGN)
         sums = psum.tile([P, 2, P], F32, name="sums")
         turned = psum.tile([P, P], F32, name="turned")
         picked_scales = keep.tile([P, PARTS * I], U8, name="picked_scales")
@@ -188,18 +188,18 @@ def tile_attend_complexscores_kernel(tc, hre, him, rre, rim, tre_words, tre_scal
 
         real_words = keep.tile([P, I], U16, name="real_words", align_bytes=MX_ALIGN)
         gather_words(real_words, 0, 0, I)
-        codes = [keep.tile([P, Q], U32, name="codes_x", tag="word_table0", align_bytes=MX_ALIGN)]
+        codes = [keep.tile([P, Q], U32, name="codes_x", align_bytes=MX_ALIGN)]
         query_scales = [keep.tile([P, Q], U8, name="query_scales%d" % s, align_bytes=MX_ALIGN) for s in range(PARTS)]
         for b in range(BLOCKS):
             quantise(0, grouped_x[b][:], slice(b * P, (b + 1) * P))
             for piece in pieces:
                 if piece[2] == b:
                     multiply(piece, 0, real_words, 0)
-        imag_words = [keep.tile([P, HALF], U16, name="imag_words0", tag="grouped_x1", align_bytes=MX_ALIGN)]
+        imag_words = [keep.tile([P, HALF], U16, name="imag_words0", align_bytes=MX_ALIGN)]
         gather_words(imag_words[0], 1, 0, HALF)
-        codes.append(keep.tile([P, Q], U32, name="codes_z", tag="grouped_x0", align_bytes=MX_ALIGN))
+        codes.append(keep.tile([P, Q], U32, name="codes_z", align_bytes=MX_ALIGN))
         quantise(1, grouped_z[:], slice(0, Q))
-        imag_words.append(keep.tile([P, HALF], U16, name="imag_words1", tag="grouped_z", align_bytes=MX_ALIGN))
+        imag_words.append(keep.tile([P, HALF], U16, name="imag_words1", align_bytes=MX_ALIGN))
         gather_words(imag_words[1], 1, HALF, HALF)
         results = {(h, b): keep.tile([P, HALF], F32, name="result%d_%d" % (h, b)) for h in range(2) for b in range(BLOCKS)}
         for piece in pieces:

@@ -55,7 +55,8 @@ def tile_attend_complexscores_kernel(tc, hre, him, rre, rim, tre_words, tre_scal
 
         def load_planes(windows, table, c, first, count):
             width = table.shape[1]
-            tile = keep.tile([P, count, width], F32, name="table%d_%d_%d" % (width, c, first))
+            name = "table%d_%d_%d" % (width, c, first)
+            tile = keep.tile([P, count, width], F32, name=name, tag=name, align_bytes=MX_ALIGN)
             nc.sync.dma_start(tile[:], table.rearrange("(p t) w -> p t w", t=PACK)[:, first : first + count, :])
             for n in range(count):
                 windows[c, first + n] = tile[:, n, :]
@@ -80,7 +81,6 @@ def tile_attend_complexscores_kernel(tc, hre, him, rre, rim, tre_words, tre_scal
         for c, table in enumerate((tre_words, tim_words)):
             nc.sync.dma_start(word_table[c][:].bitcast(I32), table[0].bitcast(I32))
 
-        grouped_x = [keep.tile([P, P, PACK], BF16, name="grouped_x%d" % b, align_bytes=MX_ALIGN) for b in range(BLOCKS)]
         grouped_z = keep.tile([P, Q, PACK], BF16, name="grouped_z", align_bytes=MX_ALIGN)
         sums = psum.tile([P, 2, P], F32, name="sums")
         turned = psum.tile([P, P], F32, name="turned")
@@ -130,19 +130,21 @@ def tile_attend_complexscores_kernel(tc, hre, him, rre, rim, tre_words, tre_scal
             for c in range(PARTS):
                 gather_head(c, t, 0, Q)
                 multiply_both(c, t, 0, Q)
-        for b in range(BLOCKS):
-            add_pair(nc.vector, 0, 0, grouped_x[b][:], slice(b * P, (b + 1) * P))
-        add_pair(nc.vector, 1, 0, grouped_z[:], slice(0, Q))
+        add_pair(nc.gpsimd, 1, 0, grouped_z[:], slice(0, Q))
         for c in range(PARTS):
             gather_rel(c, 1)
+        grouped_x = keep.tile([P, Q, PACK], BF16, name="grouped_x", tag="table%d_1_2" % U, align_bytes=MX_ALIGN)
+        add_pair(nc.vector, 0, 0, grouped_x[:], slice(0, Q))
 
         for r in range(QUADRANT // SPREAD):
             nc.sync.dma_start(tail_scales[r:P:QUADRANT, :].bitcast(I32), picked_scales[SPREAD * r : P : QUADRANT, :].bitcast(I32))
 
-        for c in range(PARTS):
-            gather_head(c, 2, 0, Q)
+        gather_head(0, 2, 0, Q)
         multiply_both(0, 2, 0, Q)
-        multiply_each(1, 2, 0, Q)
+        for b in range(BLOCKS):
+            gather_head(1, 2, b * P, P)
+        multiply_both(1, 2, 0, P)
+        multiply_each(1, 2, P, P)
         add_last_x(0, 0, Q)
         for c in range(PARTS):
             add_term(0, c)
@@ -156,7 +158,7 @@ def tile_attend_complexscores_kernel(tc, hre, him, rre, rim, tre_words, tre_scal
             add_term(1, c)
         for b in range(BLOCKS):
             add_last_x(1, b * P, P)
-            nc.scalar.copy(grouped_x[b][:, :, 2:PACK], last_x[:, :, b * P : (b + 1) * P].rearrange("p e q -> p q e"))
+            nc.scalar.copy(grouped_x[:, b * P : (b + 1) * P, 2:PACK], last_x[:, :, b * P : (b + 1) * P].rearrange("p e q -> p q e"))
         pairs = keep.tile([P, P, 2], BF16, name="pairs")
         nc.scalar.copy(pairs[:], sums[:].rearrange("q e p -> q p e"))
         nc.tensor.transpose(turned[:], pairs[:].rearrange("q p e -> q (p e)").bitcast(F32), ident[:])
@@ -191,7 +193,7 @@ def tile_attend_complexscores_kernel(tc, hre, him, rre, rim, tre_words, tre_scal
         codes = [keep.tile([P, Q], U32, name="codes_x", align_bytes=MX_ALIGN)]
         query_scales = [keep.tile([P, Q], U8, name="query_scales%d" % s, align_bytes=MX_ALIGN) for s in range(PARTS)]
         for b in range(BLOCKS):
-            quantise(0, grouped_x[b][:], slice(b * P, (b + 1) * P))
+            quantise(0, grouped_x[:, b * P : (b + 1) * P, :], slice(b * P, (b + 1) * P))
             for piece in pieces:
                 if piece[2] == b:
                     multiply(piece, 0, real_words, 0)

@@ -29,6 +29,7 @@ SCALE_ROWS = D // 32
 SPREAD = P // SCALE_ROWS
 MX_ALIGN = 64
 HALF = I // 2
+VECTOR_SHARE = 64
 
 
 def tile_attend_complexscores_kernel(tc, hre, him, rre, rim, tre_words, tre_scales, tim_words, tim_scales, offs, offs2, offs3, out):
@@ -150,7 +151,10 @@ def tile_attend_complexscores_kernel(tc, hre, him, rre, rim, tre_words, tre_scal
             add_term(0, c)
         for c in range(PARTS):
             for b in range(BLOCKS):
-                gather_head(c, LAST, b * P, P)
+                shared = VECTOR_SHARE if (c, b) == (1, 1) else 0
+                gather_head(c, LAST, b * P, P - shared)
+                if shared:
+                    nc.vector.tensor_copy(head[c, LAST][:, 0, Q - shared : Q], head_table[c, LAST].indirect(head_list[:, (Q - shared) // LIST_GROUP :]))
                 if (c, b) == (1, 1):
                     multiply_each(c, LAST, b * P, P)
                 else:
@@ -172,7 +176,7 @@ def tile_attend_complexscores_kernel(tc, hre, him, rre, rim, tre_words, tre_scal
         def quantise(s, words, queries):
             nc.vector.quantize_mx(out=codes[s][:, queries].bitcast(FP8X4), scales=query_scales[s][:, queries], in_=words.rearrange("p q t -> p (q t)"))
 
-        pieces = [(0, HALF, 0), (0, HALF, 1), (HALF, HALF, 0), (HALF, P, 1), (HALF + P, P, 1)]
+        pieces = [(0, HALF, b) for b in range(BLOCKS)] + [(first, P, b) for b in range(BLOCKS) for first in (HALF, HALF + P)]
         scores = {piece: psum.tile([P, piece[1]], F32, name="scores%d" % n) for n, piece in enumerate(pieces)}
 
         def multiply(piece, s, words, words_first):

@@ -89,7 +89,7 @@ def tile_attend_complexscores_kernel(tc, hre, him, rre, rim, tre_words, tre_scal
 
         rel = [keep.tile([P, PARTS, Q], F32, name="rel%d" % t) for t in range(PACK)]
         head = {(c, t): keep.tile([P, 1, Q], F32, name="head%d_%d" % (c, t)) for c in range(PARTS) for t in range(PACK)}
-        terms = {(c, u): keep.tile([P, 2, PARTS, Q], F32, name="terms%d_%d" % (c, u)) for c in range(PARTS) for u in range(2)}
+        terms = {(c, u): keep.tile([P, 2, PARTS, Q], F32, name="terms%d_%d" % (c, u), tag="terms%d_%d" % (c, u), align_bytes=MX_ALIGN) for c in range(PARTS) for u in range(2)}
         last_x = keep.tile([P, 2, Q], BF16, name="last_x")
 
         def gather_rel(c, u):
@@ -104,9 +104,9 @@ def tile_attend_complexscores_kernel(tc, hre, him, rre, rim, tre_words, tre_scal
             queries = slice(first, first + count)
             nc.vector.tensor_tensor(terms[c, t // 2][:, t % 2, :, queries], rel[t][:, :, queries], head[c, t][:, :, queries].to_broadcast([P, PARTS, count]), MULT)
 
-        def multiply_each(c, t, first, count):
+        def multiply_each(c, t, first, count, order=(1, 0)):
             queries = slice(first, first + count)
-            for r in (1, 0):
+            for r in order:
                 nc.vector.tensor_tensor(terms[c, t // 2][:, t % 2, r, queries], rel[t][:, r, queries], head[c, t][:, 0, queries], MULT)
 
         def add_pair(engine, s, u, words, queries):
@@ -155,8 +155,8 @@ def tile_attend_complexscores_kernel(tc, hre, him, rre, rim, tre_words, tre_scal
                 gather_head(c, LAST, b * P, P - shared)
                 if shared:
                     nc.vector.tensor_copy(head[c, LAST][:, 0, Q - shared : Q], head_table[c, LAST].indirect(head_list[:, (Q - shared) // LIST_GROUP :]))
-                if (c, b) == (1, 1):
-                    multiply_each(c, LAST, b * P, P)
+                if c == 1:
+                    multiply_each(c, LAST, b * P, P, (b, 1 - b))
                 else:
                     multiply_both(c, LAST, b * P, P)
             add_term(1, c)
@@ -176,7 +176,8 @@ def tile_attend_complexscores_kernel(tc, hre, him, rre, rim, tre_words, tre_scal
         def quantise(s, words, queries):
             nc.vector.quantize_mx(out=codes[s][:, queries].bitcast(FP8X4), scales=query_scales[s][:, queries], in_=words.rearrange("p q t -> p (q t)"))
 
-        pieces = [(0, HALF, b) for b in range(BLOCKS)] + [(first, P, b) for b in range(BLOCKS) for first in (HALF, HALF + P)]
+        pieces = [(0, HALF, 1), (0, HALF, 0), (HALF, HALF, 0), (HALF, P, 1), (HALF + P, P, 1)]
+        late = pieces[3:]
         scores = {piece: psum.tile([P, piece[1]], F32, name="scores%d" % n) for n, piece in enumerate(pieces)}
 
         def multiply(piece, s, words, words_first):
@@ -188,8 +189,8 @@ def tile_attend_complexscores_kernel(tc, hre, him, rre, rim, tre_words, tre_scal
                 lhsT_scale=query_scales[s][:, queries],
                 rhs=words[:, first - words_first : first - words_first + width].bitcast(FP4X4),
                 rhs_scale=tail_scales[:, s * I + first : s * I + first + width],
-                start=(s == 0),
-                stop=(s == PARTS - 1),
+                start=(s == (piece in late)),
+                stop=(s != (piece in late)),
             )
 
         real_words = keep.tile([P, I], U16, name="real_words", align_bytes=MX_ALIGN)
@@ -199,20 +200,22 @@ def tile_attend_complexscores_kernel(tc, hre, him, rre, rim, tre_words, tre_scal
         for b in range(BLOCKS):
             quantise(0, grouped_x[:, b * P : (b + 1) * P, :], slice(b * P, (b + 1) * P))
             for piece in pieces:
-                if piece[2] == b:
+                if piece[2] == b and piece not in late:
                     multiply(piece, 0, real_words, 0)
-        imag_words = [keep.tile([P, HALF], U16, name="imag_words0", align_bytes=MX_ALIGN)]
-        gather_words(imag_words[0], 1, 0, HALF)
         codes.append(keep.tile([P, Q], U32, name="codes_z", align_bytes=MX_ALIGN))
-        quantise(1, grouped_z[:], slice(0, Q))
-        imag_words.append(keep.tile([P, HALF], U16, name="imag_words1", align_bytes=MX_ALIGN))
-        gather_words(imag_words[1], 1, HALF, HALF)
+        imag_words = [keep.tile([P, HALF], U16, name="imag_words%d" % h, tag="terms%d_1" % h, align_bytes=MX_ALIGN) for h in range(2)]
+        for h in range(2):
+            queries = slice((1 - h) * P, (2 - h) * P)
+            quantise(1, grouped_z[:, queries, :], queries)
+            gather_words(imag_words[h], 1, h * HALF, HALF)
         results = {(h, b): keep.tile([P, HALF], F32, name="result%d_%d" % (h, b)) for h in range(2) for b in range(BLOCKS)}
         for piece in pieces:
             first, width, b = piece
             h, offset = divmod(first, HALF)
             multiply(piece, 1, imag_words[h], h * HALF)
-            copy = nc.vector.tensor_copy if b else nc.scalar.copy
+            if piece in late:
+                multiply(piece, 0, real_words, 0)
+            copy = nc.scalar.copy if h != b else nc.vector.tensor_copy
             copy(results[h, b][:, offset : offset + width], scores[piece][:])
             if offset + width == HALF:
                 nc.sync.dma_start(out[b * P : (b + 1) * P, h * HALF : (h + 1) * HALF], results[h, b][:])

@@ -104,9 +104,9 @@ def tile_attend_complexscores_kernel(tc, hre, him, rre, rim, tre_words, tre_scal
             queries = slice(first, first + count)
             nc.vector.tensor_tensor(terms[c, t // 2][:, t % 2, :, queries], rel[t][:, :, queries], head[c, t][:, :, queries].to_broadcast([P, PARTS, count]), MULT)
 
-        def multiply_each(c, t, first, count, order=(1, 0)):
+        def multiply_each(c, t, first, count):
             queries = slice(first, first + count)
-            for r in order:
+            for r in (1, 0):
                 nc.vector.tensor_tensor(terms[c, t // 2][:, t % 2, r, queries], rel[t][:, r, queries], head[c, t][:, 0, queries], MULT)
 
         def add_pair(engine, s, u, words, queries):
@@ -155,8 +155,8 @@ def tile_attend_complexscores_kernel(tc, hre, him, rre, rim, tre_words, tre_scal
                 gather_head(c, LAST, b * P, P - shared)
                 if shared:
                     nc.vector.tensor_copy(head[c, LAST][:, 0, Q - shared : Q], head_table[c, LAST].indirect(head_list[:, (Q - shared) // LIST_GROUP :]))
-                if c == 1:
-                    multiply_each(c, LAST, b * P, P, (b, 1 - b))
+                if (c, b) == (1, 1):
+                    multiply_each(c, LAST, b * P, P)
                 else:
                     multiply_both(c, LAST, b * P, P)
             add_term(1, c)

@@ -22,7 +22,6 @@ P = 128
 BLOCKS = Q // P
 PARTS = 2
 PACK = 4
-LAST = PACK - 1
 LIST_GROUP = 16
 QUADRANT = 32
 SCALE_ROWS = D // 32
@@ -45,13 +44,14 @@ def tile_attend_complexscores_kernel(tc, hre, him, rre, rim, tre_words, tre_scal
 
         scale_table = [keep.tile([P, V], U8, name="scale_table%d" % c) for c in range(PARTS)]
         for c in range(PARTS):
-            nc.gpsimd.memset(scale_table[c][:].bitcast(I32), 0)
+            nc.vector.memset(scale_table[c][:].bitcast(I32), 0)
         tail_scales = keep.tile([P, PARTS * I], U8, name="tail_scales", align_bytes=MX_ALIGN)
-        nc.gpsimd.memset(tail_scales[:].bitcast(I32), 0)
+        nc.vector.memset(tail_scales[:].bitcast(I32), 0)
         ident = keep.tile([P, P], F32, name="ident")
         make_identity(nc, ident[:])
 
         word_table = [keep.tile([P, V], U16, name="word_table%d" % c, align_bytes=MX_ALIGN) for c in range(PARTS)]
+        picked_scales = keep.tile([P, PARTS * I], U8, name="picked_scales")
         rel_table, head_table = {}, {}
 
         def load_planes(windows, table, c, first, count):
@@ -61,10 +61,14 @@ def tile_attend_complexscores_kernel(tc, hre, him, rre, rim, tre_words, tre_scal
             nc.sync.dma_start(tile[:], table.rearrange("(p t) w -> p t w", t=PACK)[:, first : first + count, :])
             for n in range(count):
                 windows[c, first + n] = tile[:, n, :]
-            windows[c, first] = tile[:].rearrange("p t w -> p (t w)")
+            if table.shape[1] == U:
+                windows[c, first] = tile[:].rearrange("p t w -> p (t w)")
 
         def load_scales(c, table):
             nc.sync.dma_start(scale_table[c][0:P:SPREAD, :].bitcast(I32), table[0].bitcast(I32))
+
+        def load_words(c, table):
+            nc.sync.dma_start(word_table[c][:].bitcast(I32), table[0].bitcast(I32))
 
         load_planes(rel_table, rre, 0, 0, 2)
         nc.sync.dma_start(rel_list[:], offs2)
@@ -73,102 +77,115 @@ def tile_attend_complexscores_kernel(tc, hre, him, rre, rim, tre_words, tre_scal
         load_planes(rel_table, rim, 1, 0, 2)
         load_scales(1, tim_scales)
         nc.sync.dma_start(head_list[:], offs)
-        for t in range(PACK):
-            if t == 2:
-                load_planes(rel_table, rre, 0, 2, 2)
-                load_planes(rel_table, rim, 1, 2, 2)
-            load_planes(head_table, hre, 0, t, 1)
-            load_planes(head_table, him, 1, t, 1)
-        for c, table in enumerate((tre_words, tim_words)):
-            nc.sync.dma_start(word_table[c][:].bitcast(I32), table[0].bitcast(I32))
+        load_planes(head_table, hre, 0, 0, 3)
+        load_planes(head_table, him, 1, 0, 1)
+        load_planes(head_table, him, 1, 1, 1)
+        load_planes(rel_table, rre, 0, 2, 2)
+        load_planes(rel_table, rim, 1, 2, 2)
+        load_planes(head_table, him, 1, 2, 1)
+        load_planes(head_table, hre, 0, 3, 1)
+        load_planes(head_table, him, 1, 3, 1)
+        load_words(0, tre_words)
 
-        grouped_z = keep.tile([P, Q, PACK], BF16, name="grouped_z", align_bytes=MX_ALIGN)
+        rel = [keep.tile([P, PARTS, 2, Q], F32, name="rel%d" % u) for u in range(2)]
+        head = {(c, u): keep.tile([P, 2, Q], F32, name="head%d_%d" % (c, u)) for c in range(PARTS) for u in range(2)}
+        terms = {(c, u): keep.tile([P, PARTS, 2, Q], F32, name="terms%d_%d" % (c, u), tag="terms%d_%d" % (c, u), align_bytes=MX_ALIGN) for c in range(PARTS) for u in range(2)}
+        grouped = {1: keep.tile([P, Q, PACK], BF16, name="grouped1", align_bytes=MX_ALIGN)}
         sums = psum.tile([P, 2, P], F32, name="sums")
         turned = psum.tile([P, P], F32, name="turned")
-        picked_scales = keep.tile([P, PARTS * I], U8, name="picked_scales")
-
-        rel = [keep.tile([P, PARTS, Q], F32, name="rel%d" % t) for t in range(PACK)]
-        head = {(c, t): keep.tile([P, 1, Q], F32, name="head%d_%d" % (c, t)) for c in range(PARTS) for t in range(PACK)}
-        terms = {(c, u): keep.tile([P, 2, PARTS, Q], F32, name="terms%d_%d" % (c, u), tag="terms%d_%d" % (c, u), align_bytes=MX_ALIGN) for c in range(PARTS) for u in range(2)}
         last_x = keep.tile([P, 2, Q], BF16, name="last_x")
 
-        def gather_rel(c, u):
-            nc.scalar.activation(rel[2 * u][:, c, :], rel_table[c, 2 * u].indirect(rel_list[:]), COPY)
-            nc.vector.tensor_copy(rel[2 * u + 1][:, c, :], rel_table[c, 2 * u + 1].indirect(rel_list[:]))
+        def gather(on_vector, dest, window, offsets):
+            if on_vector:
+                nc.vector.tensor_copy(dest, window.indirect(offsets))
+            else:
+                nc.scalar.activation(dest, window.indirect(offsets), COPY)
 
-        def gather_head(c, t, first, count):
-            window = head_table[c, t].indirect(head_list[:, first // LIST_GROUP : (first + count) // LIST_GROUP])
-            nc.scalar.activation(head[c, t][:, 0, first : first + count], window, COPY)
+        def gather_rel(r, u):
+            for e in range(2):
+                gather(e == 1, rel[u][:, r, e, :], rel_table[r, 2 * u + e], rel_list[:])
 
-        def multiply_both(c, t, first, count):
+        def gather_head(on_vector, c, t, first, count):
+            gather(on_vector, head[c, t // 2][:, t % 2, first : first + count], head_table[c, t], head_list[:, first // LIST_GROUP : (first + count) // LIST_GROUP])
+
+        def multiply_pair(c, u, r):
+            nc.vector.tensor_tensor(terms[c, u][:, r], rel[u][:, r], head[c, u][:], MULT)
+
+        def multiply_plane(c, t, first, count):
+            u, e = divmod(t, 2)
             queries = slice(first, first + count)
-            nc.vector.tensor_tensor(terms[c, t // 2][:, t % 2, :, queries], rel[t][:, :, queries], head[c, t][:, :, queries].to_broadcast([P, PARTS, count]), MULT)
+            nc.vector.tensor_tensor(terms[c, u][:, :, e, queries], rel[u][:, :, e, queries], head[c, u][:, e : e + 1, queries].to_broadcast([P, PARTS, count]), MULT)
 
-        def multiply_each(c, t, first, count):
-            queries = slice(first, first + count)
-            for r in (1, 0):
-                nc.vector.tensor_tensor(terms[c, t // 2][:, t % 2, r, queries], rel[t][:, r, queries], head[c, t][:, 0, queries], MULT)
+        def multiply_part(c, t, r, queries):
+            u, e = divmod(t, 2)
+            nc.vector.tensor_tensor(terms[c, u][:, r, e, queries], rel[u][:, r, e, queries], head[c, u][:, e, queries], MULT)
 
-        def add_pair(engine, s, u, words, queries):
+        def add_pair(engine, s, u, queries):
             engine.tensor_tensor(
-                words.rearrange("p (n i) t -> p n t i", i=2)[:, :, 2 * u : 2 * u + 2, :],
-                terms[0, u][:, :, s, queries].rearrange("p t (n i) -> p n t i", i=2),
-                terms[1, u][:, :, 1 - s, queries].rearrange("p t (n i) -> p n t i", i=2),
+                grouped[s][:, queries, :].rearrange("p (n i) t -> p n t i", i=2)[:, :, 2 * u : 2 * u + 2, :],
+                terms[0, u][:, s, :, queries].rearrange("p t (n i) -> p n t i", i=2),
+                terms[1, u][:, 1 - s, :, queries].rearrange("p t (n i) -> p n t i", i=2),
                 COMBINE[s],
             )
 
-        def add_last_x(e, first, count):
-            queries = slice(first, first + count)
-            nc.vector.tensor_tensor(last_x[:, e, queries], terms[0, 1][:, e, 0, queries], terms[1, 1][:, e, 1, queries], COMBINE[0])
+        def add_last_x(e, queries):
+            nc.vector.tensor_tensor(last_x[:, e, queries], terms[0, 1][:, 0, e, queries], terms[1, 1][:, 1, e, queries], COMBINE[0])
 
         def add_term(e, c):
-            nc.tensor.matmul(sums[:, e, :], lhsT=terms[c, 1][:, e, 1 - c, 0:P], rhs=ident[:], is_transpose=True, start=(c == 0), stop=(c == PARTS - 1))
+            nc.tensor.matmul(sums[:, e, :], lhsT=terms[c, 1][:, 1 - c, e, 0:P], rhs=ident[:], is_transpose=True, start=(c == 0), stop=(c == PARTS - 1))
 
-        for c in range(PARTS):
-            gather_rel(c, 0)
-            nc.vector.tensor_copy(picked_scales[:, c * I : (c + 1) * I], scale_table[c][:].indirect(tail_list[:]))
-        for t in range(2):
-            for c in range(PARTS):
-                gather_head(c, t, 0, Q)
-                multiply_both(c, t, 0, Q)
-        add_pair(nc.gpsimd, 1, 0, grouped_z[:], slice(0, Q))
-        for c in range(PARTS):
-            gather_rel(c, 1)
-        grouped_x = keep.tile([P, Q, PACK], BF16, name="grouped_x", tag="table%d_1_2" % U, align_bytes=MX_ALIGN)
-        add_pair(nc.vector, 0, 0, grouped_x[:], slice(0, Q))
-
+        for r in range(PARTS):
+            gather_rel(r, 0)
+            nc.vector.tensor_copy(picked_scales[:, r * I : (r + 1) * I], scale_table[r][:].indirect(tail_list[:]))
         for r in range(QUADRANT // SPREAD):
             nc.sync.dma_start(tail_scales[r:P:QUADRANT, :].bitcast(I32), picked_scales[SPREAD * r : P : QUADRANT, :].bitcast(I32))
+        load_words(1, tim_words)
 
-        gather_head(0, 2, 0, Q)
-        multiply_both(0, 2, 0, Q)
+        for t in range(3):
+            gather_head(t > 0, 0, t, 0, Q)
+        for r in range(PARTS):
+            multiply_pair(0, 0, r)
+        gather_head(False, 1, 0, 0, Q)
+        multiply_plane(1, 0, 0, Q)
+        gather_head(False, 1, 1, 0, Q)
+        for r in (1, 0):
+            multiply_part(1, 1, r, slice(0, Q))
+        add_pair(nc.gpsimd, 1, 0, slice(0, Q))
+        for r in range(PARTS):
+            gather_rel(r, 1)
+        grouped[0] = keep.tile([P, Q, PACK], BF16, name="grouped0", tag="table%d_1_2" % U, align_bytes=MX_ALIGN)
+        add_pair(nc.vector, 0, 0, slice(0, Q))
+
+        multiply_plane(0, 2, 0, Q)
         for b in range(BLOCKS):
-            gather_head(1, 2, b * P, P)
-        multiply_both(1, 2, 0, P)
-        multiply_each(1, 2, P, P)
-        add_last_x(0, 0, Q)
+            gather_head(False, 1, 2, b * P, P)
+        multiply_plane(1, 2, 0, P)
+        for r in (1, 0):
+            multiply_part(1, 2, r, slice(P, Q))
+        add_last_x(0, slice(0, Q))
         for c in range(PARTS):
             add_term(0, c)
-        for c in range(PARTS):
-            for b in range(BLOCKS):
-                shared = VECTOR_SHARE if (c, b) == (1, 1) else 0
-                gather_head(c, LAST, b * P, P - shared)
-                if shared:
-                    nc.vector.tensor_copy(head[c, LAST][:, 0, Q - shared : Q], head_table[c, LAST].indirect(head_list[:, (Q - shared) // LIST_GROUP :]))
-                if (c, b) == (1, 1):
-                    multiply_each(c, LAST, b * P, P)
-                else:
-                    multiply_both(c, LAST, b * P, P)
-            add_term(1, c)
         for b in range(BLOCKS):
-            add_last_x(1, b * P, P)
-            nc.scalar.copy(grouped_x[:, b * P : (b + 1) * P, 2:PACK], last_x[:, :, b * P : (b + 1) * P].rearrange("p e q -> p q e"))
+            gather_head(False, 0, 3, b * P, P)
+            multiply_plane(0, 3, b * P, P)
+        add_term(1, 0)
+        gather_head(False, 1, 3, 0, P)
+        multiply_plane(1, 3, 0, P)
+        gather_head(False, 1, 3, P, P - VECTOR_SHARE)
+        gather_head(True, 1, 3, Q - VECTOR_SHARE, VECTOR_SHARE)
+        for r in (1, 0):
+            multiply_part(1, 3, r, slice(P, Q))
+        add_term(1, 1)
+        for b in range(BLOCKS):
+            queries = slice(b * P, (b + 1) * P)
+            add_last_x(1, queries)
+            nc.scalar.copy(grouped[0][:, queries, 2:PACK], last_x[:, :, queries].rearrange("p e q -> p q e"))
         pairs = keep.tile([P, P, 2], BF16, name="pairs")
         nc.scalar.copy(pairs[:], sums[:].rearrange("q e p -> q p e"))
         nc.tensor.transpose(turned[:], pairs[:].rearrange("q p e -> q (p e)").bitcast(F32), ident[:])
-        words = grouped_z[:, 0:P, :].rearrange("p q t -> p (q t)").bitcast(F32).rearrange("p (q u) -> p q u", u=2)
+        words = grouped[1][:, 0:P, :].rearrange("p q t -> p (q t)").bitcast(F32).rearrange("p (q u) -> p q u", u=2)
         nc.scalar.copy(words[:, :, 1], turned[:])
-        add_pair(nc.gpsimd, 1, 1, grouped_z[:, P:Q, :], slice(P, Q))
+        add_pair(nc.gpsimd, 1, 1, slice(P, Q))
 
         def gather_words(tile, c, first, count):
             nc.vector.tensor_copy(tile[:], word_table[c][:].indirect(tail_list[:, first // LIST_GROUP : (first + count) // LIST_GROUP]))
@@ -198,7 +215,7 @@ def tile_attend_complexscores_kernel(tc, hre, him, rre, rim, tre_words, tre_scal
         codes = [keep.tile([P, Q], U32, name="codes_x", align_bytes=MX_ALIGN)]
         query_scales = [keep.tile([P, Q], U8, name="query_scales%d" % s, align_bytes=MX_ALIGN) for s in range(PARTS)]
         for b in range(BLOCKS):
-            quantise(0, grouped_x[:, b * P : (b + 1) * P, :], slice(b * P, (b + 1) * P))
+            quantise(0, grouped[0][:, b * P : (b + 1) * P, :], slice(b * P, (b + 1) * P))
             for piece in pieces:
                 if piece[2] == b and piece not in late:
                     multiply(piece, 0, real_words, 0)
@@ -206,7 +223,7 @@ def tile_attend_complexscores_kernel(tc, hre, him, rre, rim, tre_words, tre_scal
         imag_words = [keep.tile([P, HALF], U16, name="imag_words%d" % h, tag="terms%d_1" % h, align_bytes=MX_ALIGN) for h in range(2)]
         for h in range(2):
             queries = slice((1 - h) * P, (2 - h) * P)
-            quantise(1, grouped_z[:, queries, :], queries)
+            quantise(1, grouped[1][:, queries, :], queries)
             gather_words(imag_words[h], 1, h * HALF, HALF)
         results = {(h, b): keep.tile([P, HALF], F32, name="result%d_%d" % (h, b)) for h in range(2) for b in range(BLOCKS)}
         for piece in pieces:

@@ -36,6 +36,7 @@ def tile_attend_complexscores_kernel(tc, hre, him, rre, rim, tre_words, tre_scal
     with ExitStack() as ctx:
         lists = ctx.enter_context(tc.tile_pool(name="lists", bufs=1))
         keep = ctx.enter_context(tc.tile_pool(name="keep", bufs=1))
+        shared = ctx.enter_context(tc.tile_pool(name="shared", bufs=1))
         psum = ctx.enter_context(tc.psum_pool(name="psum", bufs=1))
 
         head_list = lists.tile([P, Q // LIST_GROUP], U16, name="head_list")
@@ -51,7 +52,7 @@ def tile_attend_complexscores_kernel(tc, hre, him, rre, rim, tre_words, tre_scal
         make_identity(nc, ident[:])
 
         word_table = [keep.tile([P, V], U16, name="word_table%d" % c, align_bytes=MX_ALIGN) for c in range(PARTS)]
-        picked_scales = keep.tile([P, PARTS * I], U8, name="picked_scales")
+        picked_scales = shared.tile([P, PARTS * I], U8, name="picked_scales", align_bytes=MX_ALIGN, offset=I)
         rel_table, head_table = {}, {}
 
         def load_planes(windows, table, c, first, count):
@@ -77,23 +78,24 @@ def tile_attend_complexscores_kernel(tc, hre, him, rre, rim, tre_words, tre_scal
         load_planes(rel_table, rim, 1, 0, 2)
         load_scales(1, tim_scales)
         nc.sync.dma_start(head_list[:], offs)
-        load_planes(head_table, hre, 0, 0, 3)
+        load_planes(head_table, hre, 0, 0, 2)
         load_planes(head_table, him, 1, 0, 1)
         load_planes(head_table, him, 1, 1, 1)
         load_planes(rel_table, rre, 0, 2, 2)
         load_planes(rel_table, rim, 1, 2, 2)
+        load_planes(head_table, hre, 0, 2, 1)
         load_planes(head_table, him, 1, 2, 1)
         load_planes(head_table, hre, 0, 3, 1)
         load_planes(head_table, him, 1, 3, 1)
         load_words(0, tre_words)
+        load_words(1, tim_words)
 
         rel = [keep.tile([P, PARTS, 2, Q], F32, name="rel%d" % u) for u in range(2)]
         head = {(c, u): keep.tile([P, 2, Q], F32, name="head%d_%d" % (c, u)) for c in range(PARTS) for u in range(2)}
         terms = {(c, u): keep.tile([P, PARTS, 2, Q], F32, name="terms%d_%d" % (c, u), tag="terms%d_%d" % (c, u), align_bytes=MX_ALIGN) for c in range(PARTS) for u in range(2)}
         grouped = {1: keep.tile([P, Q, PACK], BF16, name="grouped1", align_bytes=MX_ALIGN)}
-        sums = psum.tile([P, 2, P], F32, name="sums")
-        turned = psum.tile([P, P], F32, name="turned")
-        last_x = keep.tile([P, 2, Q], BF16, name="last_x")
+        sums = [psum.tile([P, 3, P], F32, name="sums%d" % b) for b in range(BLOCKS)]
+        last_x = keep.tile([P, 2, P], BF16, name="last_x")
 
         def gather(on_vector, dest, window, offsets):
             if on_vector:
@@ -128,20 +130,19 @@ def tile_attend_complexscores_kernel(tc, hre, him, rre, rim, tre_words, tre_scal
                 COMBINE[s],
             )
 
-        def add_last_x(e, queries):
-            nc.vector.tensor_tensor(last_x[:, e, queries], terms[0, 1][:, 0, e, queries], terms[1, 1][:, 1, e, queries], COMBINE[0])
+        def add_last_x(e):
+            nc.vector.tensor_tensor(last_x[:, e, :], terms[0, 1][:, 0, e, 0:P], terms[1, 1][:, 1, e, 0:P], COMBINE[0])
 
-        def add_term(e, c):
-            nc.tensor.matmul(sums[:, e, :], lhsT=terms[c, 1][:, 1 - c, e, 0:P], rhs=ident[:], is_transpose=True, start=(c == 0), stop=(c == PARTS - 1))
+        def add_term(b, e, c):
+            nc.tensor.matmul(sums[b][:, e, :], lhsT=terms[c, 1][:, 1 - c, e, b * P : (b + 1) * P], rhs=ident[:], is_transpose=True, start=(c == 0), stop=(c == PARTS - 1))
 
         for r in range(PARTS):
             gather_rel(r, 0)
             nc.vector.tensor_copy(picked_scales[:, r * I : (r + 1) * I], scale_table[r][:].indirect(tail_list[:]))
         for r in range(QUADRANT // SPREAD):
             nc.sync.dma_start(tail_scales[r:P:QUADRANT, :].bitcast(I32), picked_scales[SPREAD * r : P : QUADRANT, :].bitcast(I32))
-        load_words(1, tim_words)
 
-        for t in range(3):
+        for t in range(2):
             gather_head(t > 0, 0, t, 0, Q)
         for r in range(PARTS):
             multiply_pair(0, 0, r)
@@ -156,45 +157,47 @@ def tile_attend_complexscores_kernel(tc, hre, him, rre, rim, tre_words, tre_scal
         grouped[0] = keep.tile([P, Q, PACK], BF16, name="grouped0", tag="table%d_1_2" % U, align_bytes=MX_ALIGN)
         add_pair(nc.vector, 0, 0, slice(0, Q))
 
+        gather_head(False, 0, 2, 0, Q)
         multiply_plane(0, 2, 0, Q)
         for b in range(BLOCKS):
             gather_head(False, 1, 2, b * P, P)
-        multiply_plane(1, 2, 0, P)
-        for r in (1, 0):
-            multiply_part(1, 2, r, slice(P, Q))
-        add_last_x(0, slice(0, Q))
-        for c in range(PARTS):
-            add_term(0, c)
+        for b in range(BLOCKS):
+            multiply_plane(1, 2, b * P, P)
+        add_last_x(0)
+        for b in range(BLOCKS):
+            for c in range(PARTS):
+                add_term(b, 0, c)
         for b in range(BLOCKS):
             gather_head(False, 0, 3, b * P, P)
             multiply_plane(0, 3, b * P, P)
-        add_term(1, 0)
+            add_term(b, 1, 0)
         gather_head(False, 1, 3, 0, P)
         multiply_plane(1, 3, 0, P)
         gather_head(False, 1, 3, P, P - VECTOR_SHARE)
         gather_head(True, 1, 3, Q - VECTOR_SHARE, VECTOR_SHARE)
-        for r in (1, 0):
+        for r in range(PARTS):
             multiply_part(1, 3, r, slice(P, Q))
-        add_term(1, 1)
+        add_last_x(1)
+        add_pair(nc.gpsimd, 0, 1, slice(P, Q))
         for b in range(BLOCKS):
-            queries = slice(b * P, (b + 1) * P)
-            add_last_x(1, queries)
-            nc.scalar.copy(grouped[0][:, queries, 2:PACK], last_x[:, :, queries].rearrange("p e q -> p q e"))
-        pairs = keep.tile([P, P, 2], BF16, name="pairs")
-        nc.scalar.copy(pairs[:], sums[:].rearrange("q e p -> q p e"))
-        nc.tensor.transpose(turned[:], pairs[:].rearrange("q p e -> q (p e)").bitcast(F32), ident[:])
-        words = grouped[1][:, 0:P, :].rearrange("p q t -> p (q t)").bitcast(F32).rearrange("p (q u) -> p q u", u=2)
-        nc.scalar.copy(words[:, :, 1], turned[:])
-        add_pair(nc.gpsimd, 1, 1, slice(P, Q))
+            add_term(b, 1, 1)
+        for b in range(BLOCKS):
+            pairs = keep.tile([P, P, 2], BF16, name="pairs%d" % b)
+            nc.scalar.copy(pairs[:], sums[b][:, 0:2, :].rearrange("q e p -> q p e"))
+            nc.tensor.transpose(sums[b][:, 2, :], pairs[:].rearrange("q p e -> q (p e)").bitcast(F32), ident[:])
+        nc.scalar.copy(grouped[0][:, 0:P, 2:PACK], last_x[:].rearrange("p e q -> p q e"))
+        for b in range(BLOCKS):
+            words = grouped[1][:, b * P : (b + 1) * P, :].rearrange("p q t -> p (q t)").bitcast(F32).rearrange("p (q u) -> p q u", u=2)
+            nc.scalar.copy(words[:, :, 1], sums[b][:, 2, :])
 
         def gather_words(tile, c, first, count):
             nc.vector.tensor_copy(tile[:], word_table[c][:].indirect(tail_list[:, first // LIST_GROUP : (first + count) // LIST_GROUP]))
 
-        def quantise(s, words, queries):
-            nc.vector.quantize_mx(out=codes[s][:, queries].bitcast(FP8X4), scales=query_scales[s][:, queries], in_=words.rearrange("p q t -> p (q t)"))
+        def quantise(s, b):
+            queries = slice(b * P, (b + 1) * P)
+            nc.vector.quantize_mx(out=codes[s][:, b, :].bitcast(FP8X4), scales=query_scales[s][:, queries], in_=grouped[s][:, queries, :].rearrange("p q t -> p (q t)"))
 
-        pieces = [(0, HALF, 1), (0, HALF, 0), (HALF, HALF, 0), (HALF, P, 1), (HALF + P, P, 1)]
-        late = pieces[3:]
+        pieces = [(0, HALF, 1), (0, HALF, 0), (HALF, P, 0), (HALF + P, P, 0), (HALF, P, 1), (HALF + P, P, 1)]
         scores = {piece: psum.tile([P, piece[1]], F32, name="scores%d" % n) for n, piece in enumerate(pieces)}
 
         def multiply(piece, s, words, words_first):
@@ -202,37 +205,44 @@ def tile_attend_complexscores_kernel(tc, hre, him, rre, rim, tre_words, tre_scal
             queries = slice(b * P, (b + 1) * P)
             nc.tensor.matmul_mx(
                 out=scores[piece][:],
-                lhsT=codes[s][:, queries].bitcast(FP8X4),
+                lhsT=codes[s][:, b, :].bitcast(FP8X4),
                 lhsT_scale=query_scales[s][:, queries],
                 rhs=words[:, first - words_first : first - words_first + width].bitcast(FP4X4),
                 rhs_scale=tail_scales[:, s * I + first : s * I + first + width],
-                start=(s == (piece in late)),
-                stop=(s != (piece in late)),
+                start=(s == 0),
+                stop=(s == PARTS - 1),
             )
 
         real_words = keep.tile([P, I], U16, name="real_words", align_bytes=MX_ALIGN)
-        gather_words(real_words, 0, 0, I)
-        codes = [keep.tile([P, Q], U32, name="codes_x", align_bytes=MX_ALIGN)]
+        imag_words = [keep.tile([P, HALF], U16, name="imag_words0", align_bytes=MX_ALIGN)]
+        codes = [
+            keep.tile([P, BLOCKS, P], U32, name="codes0", align_bytes=MX_ALIGN),
+            shared.tile([P, BLOCKS, P], U32, name="codes1", align_bytes=MX_ALIGN, offset=0),
+        ]
         query_scales = [keep.tile([P, Q], U8, name="query_scales%d" % s, align_bytes=MX_ALIGN) for s in range(PARTS)]
-        for b in range(BLOCKS):
-            quantise(0, grouped[0][:, b * P : (b + 1) * P, :], slice(b * P, (b + 1) * P))
-            for piece in pieces:
-                if piece[2] == b and piece not in late:
-                    multiply(piece, 0, real_words, 0)
-        codes.append(keep.tile([P, Q], U32, name="codes_z", align_bytes=MX_ALIGN))
-        imag_words = [keep.tile([P, HALF], U16, name="imag_words%d" % h, tag="terms%d_1" % h, align_bytes=MX_ALIGN) for h in range(2)]
-        for h in range(2):
-            queries = slice((1 - h) * P, (2 - h) * P)
-            quantise(1, grouped[1][:, queries, :], queries)
-            gather_words(imag_words[h], 1, h * HALF, HALF)
         results = {(h, b): keep.tile([P, HALF], F32, name="result%d_%d" % (h, b)) for h in range(2) for b in range(BLOCKS)}
-        for piece in pieces:
+
+        def finish(piece):
             first, width, b = piece
             h, offset = divmod(first, HALF)
             multiply(piece, 1, imag_words[h], h * HALF)
-            if piece in late:
-                multiply(piece, 0, real_words, 0)
-            copy = nc.scalar.copy if h != b else nc.vector.tensor_copy
+            copy = nc.vector.tensor_copy if offset else nc.scalar.copy
             copy(results[h, b][:, offset : offset + width], scores[piece][:])
             if offset + width == HALF:
                 nc.sync.dma_start(out[b * P : (b + 1) * P, h * HALF : (h + 1) * HALF], results[h, b][:])
+
+        gather_words(real_words, 0, 0, I)
+        for b in (1, 0):
+            quantise(0, b)
+            for piece in pieces:
+                if piece[2] == b:
+                    multiply(piece, 0, real_words, 0)
+        gather_words(imag_words[0], 1, 0, HALF)
+        for b in range(BLOCKS):
+            quantise(1, b)
+            finish((0, HALF, b))
+        imag_words.append(shared.tile([P, HALF], U16, name="imag_words1", align_bytes=MX_ALIGN, offset=PARTS * I))
+        gather_words(imag_words[1], 1, HALF, HALF)
+        for b in range(BLOCKS):
+            for first in (HALF, HALF + P):
+                finish((first, P, b))

@@ -52,7 +52,10 @@ def tile_attend_complexscores_kernel(tc, hre, him, rre, rim, tre_words, tre_scal
         make_identity(nc, ident[:])
 
         word_table = [keep.tile([P, V], U16, name="word_table%d" % c, align_bytes=MX_ALIGN) for c in range(PARTS)]
-        picked_scales = shared.tile([P, PARTS * I], U8, name="picked_scales", align_bytes=MX_ALIGN, offset=I)
+        picked_scales = [
+            keep.tile([P, I], U8, name="picked_scales0"),
+            shared.tile([P, I], U8, name="picked_scales1", align_bytes=MX_ALIGN, offset=PARTS * I - I // 2),
+        ]
         rel_table, head_table = {}, {}
 
         def load_planes(windows, table, c, first, count):
@@ -87,8 +90,6 @@ def tile_attend_complexscores_kernel(tc, hre, him, rre, rim, tre_words, tre_scal
         load_planes(head_table, him, 1, 2, 1)
         load_planes(head_table, hre, 0, 3, 1)
         load_planes(head_table, him, 1, 3, 1)
-        load_words(0, tre_words)
-        load_words(1, tim_words)
 
         rel = [keep.tile([P, PARTS, 2, Q], F32, name="rel%d" % u) for u in range(2)]
         head = {(c, u): keep.tile([P, 2, Q], F32, name="head%d_%d" % (c, u)) for c in range(PARTS) for u in range(2)}
@@ -138,9 +139,11 @@ def tile_attend_complexscores_kernel(tc, hre, him, rre, rim, tre_words, tre_scal
 
         for r in range(PARTS):
             gather_rel(r, 0)
-            nc.vector.tensor_copy(picked_scales[:, r * I : (r + 1) * I], scale_table[r][:].indirect(tail_list[:]))
-        for r in range(QUADRANT // SPREAD):
-            nc.sync.dma_start(tail_scales[r:P:QUADRANT, :].bitcast(I32), picked_scales[SPREAD * r : P : QUADRANT, :].bitcast(I32))
+            nc.vector.tensor_copy(picked_scales[r][:], scale_table[r][:].indirect(tail_list[:]))
+        for c, table in enumerate((tre_words, tim_words)):
+            load_words(c, table)
+            for r in range(QUADRANT // SPREAD):
+                nc.sync.dma_start(tail_scales[r:P:QUADRANT, c * I : (c + 1) * I].bitcast(I32), picked_scales[c][SPREAD * r : P : QUADRANT, :].bitcast(I32))
 
         for t in range(2):
             gather_head(t > 0, 0, t, 0, Q)

@@ -29,6 +29,7 @@ SPREAD = P // SCALE_ROWS
 MX_ALIGN = 64
 HALF = I // 2
 VECTOR_SHARE = 64
+PLACED = 128
 
 
 def tile_attend_complexscores_kernel(tc, hre, him, rre, rim, tre_words, tre_scales, tim_words, tim_scales, offs, offs2, offs3, out):
@@ -94,9 +95,9 @@ def tile_attend_complexscores_kernel(tc, hre, him, rre, rim, tre_words, tre_scal
         rel = [keep.tile([P, PARTS, 2, Q], F32, name="rel%d" % u) for u in range(2)]
         head = {(c, u): keep.tile([P, 2, Q], F32, name="head%d_%d" % (c, u)) for c in range(PARTS) for u in range(2)}
         terms = {(c, u): keep.tile([P, PARTS, 2, Q], F32, name="terms%d_%d" % (c, u), tag="terms%d_%d" % (c, u), align_bytes=MX_ALIGN) for c in range(PARTS) for u in range(2)}
-        grouped = {1: keep.tile([P, Q, PACK], BF16, name="grouped1", align_bytes=MX_ALIGN)}
-        sums = [psum.tile([P, 3, P], F32, name="sums%d" % b) for b in range(BLOCKS)]
-        last_x = keep.tile([P, 2, P], BF16, name="last_x")
+        grouped = [keep.tile([P, Q, PACK], BF16, name="grouped%d" % s, align_bytes=MX_ALIGN) for s in range(PARTS)]
+        sums = [psum.tile([P, PACK, P], F32, name="sums%d" % b) for b in range(BLOCKS)]
+        last_x = keep.tile([P, 2, PLACED], BF16, name="last_x")
 
         def gather(on_vector, dest, window, offsets):
             if on_vector:
@@ -132,10 +133,14 @@ def tile_attend_complexscores_kernel(tc, hre, him, rre, rim, tre_words, tre_scal
             )
 
         def add_last_x(e):
-            nc.vector.tensor_tensor(last_x[:, e, :], terms[0, 1][:, 0, e, 0:P], terms[1, 1][:, 1, e, 0:P], COMBINE[0])
+            nc.vector.tensor_tensor(last_x[:, e, :], terms[0, 1][:, 0, e, 0:PLACED], terms[1, 1][:, 1, e, 0:PLACED], COMBINE[0])
 
-        def add_term(b, e, c):
-            nc.tensor.matmul(sums[b][:, e, :], lhsT=terms[c, 1][:, 1 - c, e, b * P : (b + 1) * P], rhs=ident[:], is_transpose=True, start=(c == 0), stop=(c == PARTS - 1))
+        def add_term(b, u, e, c, start, stop):
+            nc.tensor.matmul(sums[b][:, e, :], lhsT=terms[c, u][:, 1 - c, e, b * P : (b + 1) * P], rhs=ident[:], is_transpose=True, start=start, stop=stop)
+
+        def turn_back(copy, u, b, pairs):
+            copy(pairs, sums[b][:, 0:2, :].rearrange("q e p -> q p e"))
+            nc.tensor.transpose(sums[b][:, 2 + u, :], pairs.rearrange("q p e -> q (p e)").bitcast(F32), ident[:])
 
         for r in range(PARTS):
             gather_rel(r, 0)
@@ -154,13 +159,17 @@ def tile_attend_complexscores_kernel(tc, hre, him, rre, rim, tre_words, tre_scal
         gather_head(False, 1, 1, 0, Q)
         for r in (1, 0):
             multiply_part(1, 1, r, slice(0, Q))
-        add_pair(nc.gpsimd, 1, 0, slice(0, Q))
+        for c in range(PARTS):
+            for e in range(2):
+                for b in range(BLOCKS):
+                    add_term(b, 0, e, c, (c, e) == (0, 0), (c, e) == (1, 1))
+        add_pair(nc.vector, 0, 0, slice(0, Q))
         for r in range(PARTS):
             gather_rel(r, 1)
-        grouped[0] = keep.tile([P, Q, PACK], BF16, name="grouped0", tag="table%d_1_2" % U, align_bytes=MX_ALIGN)
-        add_pair(nc.vector, 0, 0, slice(0, Q))
 
         gather_head(False, 0, 2, 0, Q)
+        turn_back(nc.vector.tensor_copy, 0, 0, keep.tile([P, P, 2], BF16, name="first_pairs0")[:])
+        turn_back(nc.scalar.copy, 0, 1, keep.tile([P, P, 2], BF16, name="first_pairs1", tag="table%d_0_2" % T, align_bytes=MX_ALIGN)[:])
         multiply_plane(0, 2, 0, Q)
         for b in range(BLOCKS):
             gather_head(False, 1, 2, b * P, P)
@@ -169,11 +178,11 @@ def tile_attend_complexscores_kernel(tc, hre, him, rre, rim, tre_words, tre_scal
         add_last_x(0)
         for b in range(BLOCKS):
             for c in range(PARTS):
-                add_term(b, 0, c)
+                add_term(b, 1, 0, c, c == 0, c == 1)
         for b in range(BLOCKS):
             gather_head(False, 0, 3, b * P, P)
             multiply_plane(0, 3, b * P, P)
-            add_term(b, 1, 0)
+            add_term(b, 1, 1, 0, True, False)
         gather_head(False, 1, 3, 0, P)
         multiply_plane(1, 3, 0, P)
         gather_head(False, 1, 3, P, P - VECTOR_SHARE)
@@ -181,17 +190,15 @@ def tile_attend_complexscores_kernel(tc, hre, him, rre, rim, tre_words, tre_scal
         for r in range(PARTS):
             multiply_part(1, 3, r, slice(P, Q))
         add_last_x(1)
-        add_pair(nc.gpsimd, 0, 1, slice(P, Q))
+        add_pair(nc.gpsimd, 0, 1, slice(PLACED, Q))
         for b in range(BLOCKS):
-            add_term(b, 1, 1)
+            add_term(b, 1, 1, 1, False, True)
         for b in range(BLOCKS):
-            pairs = keep.tile([P, P, 2], BF16, name="pairs%d" % b)
-            nc.scalar.copy(pairs[:], sums[b][:, 0:2, :].rearrange("q e p -> q p e"))
-            nc.tensor.transpose(sums[b][:, 2, :], pairs[:].rearrange("q p e -> q (p e)").bitcast(F32), ident[:])
-        nc.scalar.copy(grouped[0][:, 0:P, 2:PACK], last_x[:].rearrange("p e q -> p q e"))
+            turn_back(nc.scalar.copy, 1, b, keep.tile([P, P, 2], BF16, name="last_pairs%d" % b)[:])
+        nc.scalar.copy(grouped[0][:, 0:PLACED, 2:PACK], last_x[:].rearrange("p e q -> p q e"))
         for b in range(BLOCKS):
             words = grouped[1][:, b * P : (b + 1) * P, :].rearrange("p q t -> p (q t)").bitcast(F32).rearrange("p (q u) -> p q u", u=2)
-            nc.scalar.copy(words[:, :, 1], sums[b][:, 2, :])
+            nc.scalar.copy(words, sums[b][:, 2:PACK, :].rearrange("p u q -> p q u"))
 
         def gather_words(tile, c, first, count):
             nc.vector.tensor_copy(tile[:], word_table[c][:].indirect(tail_list[:, first // LIST_GROUP : (first + count) // LIST_GROUP]))

@@ -24,8 +24,8 @@ PARTS = 2
 PACK = 4
 LIST_GROUP = 16
 QUADRANT = 32
-SCALE_ROWS = D // 32
-SPREAD = P // SCALE_ROWS
+QUADRANT_ROWS = 4
+PORT_ROWS = 4
 MX_ALIGN = 64
 HALF = I // 2
 VECTOR_SHARE = 64
@@ -59,32 +59,31 @@ def tile_attend_complexscores_kernel(tc, hre, him, rre, rim, tre_words, tre_scal
         ]
         rel_table, head_table = {}, {}
 
-        def load_planes(windows, table, c, first, count):
+        def load_planes(windows, table, c, first, count, queue=nc.sync):
             width = table.shape[1]
             name = "table%d_%d_%d" % (width, c, first)
             tile = keep.tile([P, count, width], F32, name=name, tag=name, align_bytes=MX_ALIGN)
-            nc.sync.dma_start(tile[:], table.rearrange("(p t) w -> p t w", t=PACK)[:, first : first + count, :])
+            queue.dma_start(tile[:], table.rearrange("(p t) w -> p t w", t=PACK)[:, first : first + count, :])
             for n in range(count):
                 windows[c, first + n] = tile[:, n, :]
             if table.shape[1] == U:
                 windows[c, first] = tile[:].rearrange("p t w -> p (t w)")
 
         def load_scales(c, table):
-            nc.sync.dma_start(scale_table[c][0:P:SPREAD, :].bitcast(I32), table[0].bitcast(I32))
+            nc.sync.dma_start(scale_table[c][QUADRANT : P - QUADRANT : PORT_ROWS, :].bitcast(I32), table[0].bitcast(I32))
 
         def load_words(c, table):
             nc.sync.dma_start(word_table[c][:].bitcast(I32), table[0].bitcast(I32))
 
-        load_planes(rel_table, rre, 0, 0, 2)
         nc.sync.dma_start(rel_list[:], offs2)
         nc.sync.dma_start(tail_list[:], offs3)
+        nc.sync.dma_start(head_list[:], offs)
+        load_planes(rel_table, rre, 0, 0, 2, nc.scalar)
         load_scales(0, tre_scales)
         load_planes(rel_table, rim, 1, 0, 2)
         load_scales(1, tim_scales)
-        nc.sync.dma_start(head_list[:], offs)
         load_planes(head_table, hre, 0, 0, 2)
-        load_planes(head_table, him, 1, 0, 1)
-        load_planes(head_table, him, 1, 1, 1)
+        load_planes(head_table, him, 1, 0, 2)
         load_planes(rel_table, rre, 0, 2, 2)
         load_planes(rel_table, rim, 1, 2, 2)
         load_planes(head_table, hre, 0, 2, 1)
@@ -147,22 +146,21 @@ def tile_attend_complexscores_kernel(tc, hre, him, rre, rim, tre_words, tre_scal
             nc.vector.tensor_copy(picked_scales[r][:], scale_table[r][:].indirect(tail_list[:]))
         for c, table in enumerate((tre_words, tim_words)):
             load_words(c, table)
-            for r in range(QUADRANT // SPREAD):
-                nc.sync.dma_start(tail_scales[r:P:QUADRANT, c * I : (c + 1) * I].bitcast(I32), picked_scales[c][SPREAD * r : P : QUADRANT, :].bitcast(I32))
+            for r in range(QUADRANT_ROWS):
+                nc.sync.dma_start(tail_scales[r:P:QUADRANT, c * I : (c + 1) * I].bitcast(I32), picked_scales[c][QUADRANT + PORT_ROWS * r : P - QUADRANT : PORT_ROWS * QUADRANT_ROWS, :].bitcast(I32))
 
         for t in range(2):
             gather_head(t > 0, 0, t, 0, Q)
         for r in range(PARTS):
             multiply_pair(0, 0, r)
-        gather_head(False, 1, 0, 0, Q)
-        multiply_plane(1, 0, 0, Q)
-        gather_head(False, 1, 1, 0, Q)
-        for r in (1, 0):
-            multiply_part(1, 1, r, slice(0, Q))
+        for t in range(2):
+            gather_head(t > 0, 1, t, 0, Q)
+        for t in (1, 0):
+            multiply_plane(1, t, 0, Q)
         for c in range(PARTS):
-            for e in range(2):
+            for e in (1, 0):
                 for b in range(BLOCKS):
-                    add_term(b, 0, e, c, (c, e) == (0, 0), (c, e) == (1, 1))
+                    add_term(b, 0, e, c, (c, e) == (0, 1), (c, e) == (1, 0))
         add_pair(nc.vector, 0, 0, slice(0, Q))
         for r in range(PARTS):
             gather_rel(r, 1)

@@ -24,8 +24,8 @@ PARTS = 2
 PACK = 4
 LIST_GROUP = 16
 QUADRANT = 32
-QUADRANT_ROWS = 4
-PORT_ROWS = 4
+SCALE_ROWS = D // 32
+SPREAD = P // SCALE_ROWS
 MX_ALIGN = 64
 HALF = I // 2
 VECTOR_SHARE = 64
@@ -48,15 +48,11 @@ def tile_attend_complexscores_kernel(tc, hre, him, rre, rim, tre_words, tre_scal
         for c in range(PARTS):
             nc.vector.memset(scale_table[c][:].bitcast(I32), 0)
         tail_scales = keep.tile([P, PARTS * I], U8, name="tail_scales", align_bytes=MX_ALIGN)
-        nc.vector.memset(tail_scales[:].bitcast(I32), 0)
         ident = keep.tile([P, P], F32, name="ident")
         make_identity(nc, ident[:])
 
         word_table = [keep.tile([P, V], U16, name="word_table%d" % c, align_bytes=MX_ALIGN) for c in range(PARTS)]
-        picked_scales = [
-            keep.tile([P, I], U8, name="picked_scales0"),
-            shared.tile([P, I], U8, name="picked_scales1", align_bytes=MX_ALIGN, offset=PARTS * I - I // 2),
-        ]
+        picked_scales = shared.tile([P, PARTS * I], U8, name="picked_scales", align_bytes=MX_ALIGN, offset=PARTS * I // 2)
         rel_table, head_table = {}, {}
 
         def load_planes(windows, table, c, first, count, queue=nc.sync):
@@ -70,7 +66,7 @@ def tile_attend_complexscores_kernel(tc, hre, him, rre, rim, tre_words, tre_scal
                 windows[c, first] = tile[:].rearrange("p t w -> p (t w)")
 
         def load_scales(c, table):
-            nc.sync.dma_start(scale_table[c][QUADRANT : P - QUADRANT : PORT_ROWS, :].bitcast(I32), table[0].bitcast(I32))
+            nc.sync.dma_start(scale_table[c][0:P:SPREAD, :].bitcast(I32), table[0].bitcast(I32))
 
         def load_words(c, table):
             nc.sync.dma_start(word_table[c][:].bitcast(I32), table[0].bitcast(I32))
@@ -143,11 +139,12 @@ def tile_attend_complexscores_kernel(tc, hre, him, rre, rim, tre_words, tre_scal
 
         for r in range(PARTS):
             gather_rel(r, 0)
-            nc.vector.tensor_copy(picked_scales[r][:], scale_table[r][:].indirect(tail_list[:]))
+            nc.vector.tensor_copy(picked_scales[:, r * I : (r + 1) * I], scale_table[r][:].indirect(tail_list[:]))
+        nc.vector.tensor_copy(tail_scales[:].bitcast(I32), picked_scales[:].bitcast(I32))
         for c, table in enumerate((tre_words, tim_words)):
             load_words(c, table)
-            for r in range(QUADRANT_ROWS):
-                nc.sync.dma_start(tail_scales[r:P:QUADRANT, c * I : (c + 1) * I].bitcast(I32), picked_scales[c][QUADRANT + PORT_ROWS * r : P - QUADRANT : PORT_ROWS * QUADRANT_ROWS, :].bitcast(I32))
+        for r in range(1, QUADRANT // SPREAD):
+            nc.sync.dma_start(tail_scales[r:P:QUADRANT, :].bitcast(I32), picked_scales[SPREAD * r : P : QUADRANT, :].bitcast(I32))
 
         for t in range(2):
             gather_head(t > 0, 0, t, 0, Q)

@@ -15,13 +15,14 @@ U8 = mybir.dt.uint8
 FP8X4 = mybir.dt.float8_e4m3fn_x4
 FP4X4 = mybir.dt.float4_e2m1fn_x4
 MULT = mybir.AluOpType.mult
-COMBINE = (mybir.AluOpType.subtract, mybir.AluOpType.add)
+SUBTRACT = mybir.AluOpType.subtract
 COPY = mybir.ActivationFunctionType.Copy
 
 P = 128
 BLOCKS = Q // P
 PARTS = 2
 PACK = 4
+LAST = PACK - 1
 LIST_GROUP = 16
 QUADRANT = 32
 SCALE_ROWS = D // 32
@@ -29,7 +30,6 @@ SPREAD = P // SCALE_ROWS
 MX_ALIGN = 64
 HALF = I // 2
 VECTOR_SHARE = 64
-PLACED = 128
 
 
 def tile_attend_complexscores_kernel(tc, hre, him, rre, rim, tre_words, tre_scales, tim_words, tim_scales, offs, offs2, offs3, out):
@@ -62,14 +62,11 @@ def tile_attend_complexscores_kernel(tc, hre, him, rre, rim, tre_words, tre_scal
             queue.dma_start(tile[:], table.rearrange("(p t) w -> p t w", t=PACK)[:, first : first + count, :])
             for n in range(count):
                 windows[c, first + n] = tile[:, n, :]
-            if table.shape[1] == U:
+            if width == U:
                 windows[c, first] = tile[:].rearrange("p t w -> p (t w)")
 
         def load_scales(c, table):
             nc.sync.dma_start(scale_table[c][0:P:SPREAD, :].bitcast(I32), table[0].bitcast(I32))
-
-        def load_words(c, table):
-            nc.sync.dma_start(word_table[c][:].bitcast(I32), table[0].bitcast(I32))
 
         nc.sync.dma_start(rel_list[:], offs2)
         nc.sync.dma_start(tail_list[:], offs3)
@@ -82,17 +79,19 @@ def tile_attend_complexscores_kernel(tc, hre, him, rre, rim, tre_words, tre_scal
         load_planes(head_table, him, 1, 0, 2)
         load_planes(rel_table, rre, 0, 2, 2)
         load_planes(rel_table, rim, 1, 2, 2)
-        load_planes(head_table, hre, 0, 2, 1)
-        load_planes(head_table, him, 1, 2, 1)
-        load_planes(head_table, hre, 0, 3, 1)
-        load_planes(head_table, him, 1, 3, 1)
+        for t in (2, LAST):
+            load_planes(head_table, hre, 0, t, 1)
+            load_planes(head_table, him, 1, t, 1)
 
-        rel = [keep.tile([P, PARTS, 2, Q], F32, name="rel%d" % u) for u in range(2)]
-        head = {(c, u): keep.tile([P, 2, Q], F32, name="head%d_%d" % (c, u)) for c in range(PARTS) for u in range(2)}
-        terms = {(c, u): keep.tile([P, PARTS, 2, Q], F32, name="terms%d_%d" % (c, u), tag="terms%d_%d" % (c, u), align_bytes=MX_ALIGN) for c in range(PARTS) for u in range(2)}
+        relp = [keep.tile([P, PARTS, 2, Q], F32, name="relp%d" % u) for u in range(2)]
+        head = {(c, t): keep.tile([P, Q], F32, name="head%d_%d" % (c, t)) for c in range(PARTS) for t in range(PACK)}
+        early = [keep.tile([P, PARTS, LAST, Q], F32, name="early%d" % c, align_bytes=MX_ALIGN) for c in range(PARTS)]
+        last = [keep.tile([P, PARTS, Q], F32, name="last%d" % c, align_bytes=MX_ALIGN) for c in range(PARTS)]
         grouped = [keep.tile([P, Q, PACK], BF16, name="grouped%d" % s, align_bytes=MX_ALIGN) for s in range(PARTS)]
         sums = [psum.tile([P, PACK, P], F32, name="sums%d" % b) for b in range(BLOCKS)]
-        last_x = keep.tile([P, 2, PLACED], BF16, name="last_x")
+
+        def term(c, r, t, queries):
+            return last[c][:, r, queries] if t == LAST else early[c][:, r, t, queries]
 
         def gather(on_vector, dest, window, offsets):
             if on_vector:
@@ -102,36 +101,24 @@ def tile_attend_complexscores_kernel(tc, hre, him, rre, rim, tre_words, tre_scal
 
         def gather_rel(r, u):
             for e in range(2):
-                gather(e == 1, rel[u][:, r, e, :], rel_table[r, 2 * u + e], rel_list[:])
+                gather(e == 1, relp[u][:, r, e, :], rel_table[r, 2 * u + e], rel_list[:])
 
         def gather_head(on_vector, c, t, first, count):
-            gather(on_vector, head[c, t // 2][:, t % 2, first : first + count], head_table[c, t], head_list[:, first // LIST_GROUP : (first + count) // LIST_GROUP])
-
-        def multiply_pair(c, u, r):
-            nc.vector.tensor_tensor(terms[c, u][:, r], rel[u][:, r], head[c, u][:], MULT)
+            gather(on_vector, head[c, t][:, first : first + count], head_table[c, t], head_list[:, first // LIST_GROUP : (first + count) // LIST_GROUP])
 
         def multiply_plane(c, t, first, count):
             u, e = divmod(t, 2)
             queries = slice(first, first + count)
-            nc.vector.tensor_tensor(terms[c, u][:, :, e, queries], rel[u][:, :, e, queries], head[c, u][:, e : e + 1, queries].to_broadcast([P, PARTS, count]), MULT)
+            both = last[c][:, :, queries] if t == LAST else early[c][:, :, t, queries]
+            nc.vector.tensor_tensor(both, relp[u][:, :, e, queries], head[c, t][:, queries].unsqueeze(1).to_broadcast([P, PARTS, count]), MULT)
 
-        def multiply_part(c, t, r, queries):
+        def multiply_part(c, t, r, first, count):
             u, e = divmod(t, 2)
-            nc.vector.tensor_tensor(terms[c, u][:, r, e, queries], rel[u][:, r, e, queries], head[c, u][:, e, queries], MULT)
+            queries = slice(first, first + count)
+            nc.vector.tensor_tensor(term(c, r, t, queries), relp[u][:, r, e, queries], head[c, t][:, queries], MULT)
 
-        def add_pair(engine, s, u, queries):
-            engine.tensor_tensor(
-                grouped[s][:, queries, :].rearrange("p (n i) t -> p n t i", i=2)[:, :, 2 * u : 2 * u + 2, :],
-                terms[0, u][:, s, :, queries].rearrange("p t (n i) -> p n t i", i=2),
-                terms[1, u][:, 1 - s, :, queries].rearrange("p t (n i) -> p n t i", i=2),
-                COMBINE[s],
-            )
-
-        def add_last_x(e):
-            nc.vector.tensor_tensor(last_x[:, e, :], terms[0, 1][:, 0, e, 0:PLACED], terms[1, 1][:, 1, e, 0:PLACED], COMBINE[0])
-
-        def add_term(b, u, e, c, start, stop):
-            nc.tensor.matmul(sums[b][:, e, :], lhsT=terms[c, u][:, 1 - c, e, b * P : (b + 1) * P], rhs=ident[:], is_transpose=True, start=start, stop=stop)
+        def add_term(b, t, c, start, stop):
+            nc.tensor.matmul(sums[b][:, t % 2, :], lhsT=term(c, 1 - c, t, slice(b * P, (b + 1) * P)), rhs=ident[:], is_transpose=True, start=start, stop=stop)
 
         def turn_back(copy, u, b, pairs):
             copy(pairs, sums[b][:, 0:2, :].rearrange("q e p -> q p e"))
@@ -142,55 +129,57 @@ def tile_attend_complexscores_kernel(tc, hre, him, rre, rim, tre_words, tre_scal
             nc.vector.tensor_copy(picked_scales[:, r * I : (r + 1) * I], scale_table[r][:].indirect(tail_list[:]))
         nc.vector.tensor_copy(tail_scales[:].bitcast(I32), picked_scales[:].bitcast(I32))
         for c, table in enumerate((tre_words, tim_words)):
-            load_words(c, table)
+            nc.sync.dma_start(word_table[c][:].bitcast(I32), table[0].bitcast(I32))
         for r in range(1, QUADRANT // SPREAD):
             nc.sync.dma_start(tail_scales[r:P:QUADRANT, :].bitcast(I32), picked_scales[SPREAD * r : P : QUADRANT, :].bitcast(I32))
 
-        for t in range(2):
-            gather_head(t > 0, 0, t, 0, Q)
-        for r in range(PARTS):
-            multiply_pair(0, 0, r)
-        for t in range(2):
-            gather_head(t > 0, 1, t, 0, Q)
-        for t in (1, 0):
-            multiply_plane(1, t, 0, Q)
         for c in range(PARTS):
-            for e in (1, 0):
+            for t in range(2):
+                gather_head(t > 0, c, t, 0, Q)
+            for t in range(2):
+                multiply_plane(c, t, 0, Q)
+        for c in range(PARTS):
+            for t in range(2):
                 for b in range(BLOCKS):
-                    add_term(b, 0, e, c, (c, e) == (0, 1), (c, e) == (1, 0))
-        add_pair(nc.vector, 0, 0, slice(0, Q))
+                    add_term(b, t, c, (c, t) == (0, 0), (c, t) == (1, 1))
         for r in range(PARTS):
             gather_rel(r, 1)
 
         gather_head(False, 0, 2, 0, Q)
-        turn_back(nc.vector.tensor_copy, 0, 0, keep.tile([P, P, 2], BF16, name="first_pairs0")[:])
-        turn_back(nc.scalar.copy, 0, 1, keep.tile([P, P, 2], BF16, name="first_pairs1", tag="table%d_0_2" % T, align_bytes=MX_ALIGN)[:])
+        turn_back(nc.scalar.copy, 0, 0, keep.tile([P, P, 2], BF16, name="first_pairs0", tag="table%d_0_2" % T, align_bytes=MX_ALIGN)[:])
         multiply_plane(0, 2, 0, Q)
         for b in range(BLOCKS):
             gather_head(False, 1, 2, b * P, P)
+        turn_back(nc.scalar.copy, 0, 1, keep.tile([P, P, 2], BF16, name="first_pairs1", tag="table%d_1_2" % T, align_bytes=MX_ALIGN)[:])
         for b in range(BLOCKS):
             multiply_plane(1, 2, b * P, P)
-        add_last_x(0)
+        for b in range(BLOCKS):
+            queries = slice(b * P, (b + 1) * P)
+            nc.vector.tensor_tensor(
+                grouped[0][:, queries, :].rearrange("p (n i) t -> p n t i", i=2)[:, :, 0:LAST, :],
+                early[0][:, 0, :, queries].rearrange("p t (n i) -> p n t i", i=2),
+                early[1][:, 1, :, queries].rearrange("p t (n i) -> p n t i", i=2),
+                SUBTRACT,
+            )
         for b in range(BLOCKS):
             for c in range(PARTS):
-                add_term(b, 1, 0, c, c == 0, c == 1)
+                add_term(b, 2, c, c == 0, c == 1)
         for b in range(BLOCKS):
-            gather_head(False, 0, 3, b * P, P)
-            multiply_plane(0, 3, b * P, P)
-            add_term(b, 1, 1, 0, True, False)
-        gather_head(False, 1, 3, 0, P)
-        multiply_plane(1, 3, 0, P)
-        gather_head(False, 1, 3, P, P - VECTOR_SHARE)
-        gather_head(True, 1, 3, Q - VECTOR_SHARE, VECTOR_SHARE)
-        for r in range(PARTS):
-            multiply_part(1, 3, r, slice(P, Q))
-        add_last_x(1)
-        add_pair(nc.gpsimd, 0, 1, slice(PLACED, Q))
-        for b in range(BLOCKS):
-            add_term(b, 1, 1, 1, False, True)
+            gather_head(False, 0, LAST, b * P, P)
+            multiply_plane(0, LAST, b * P, P)
+            add_term(b, LAST, 0, True, False)
+
+        gather_head(False, 1, LAST, 0, P)
+        multiply_plane(1, LAST, 0, P)
+        add_term(0, LAST, 1, False, True)
+        gather_head(False, 1, LAST, P, P - VECTOR_SHARE)
+        gather_head(True, 1, LAST, Q - VECTOR_SHARE, VECTOR_SHARE)
+        for r in (1, 0):
+            multiply_part(1, LAST, r, P, P)
+        add_term(1, LAST, 1, False, True)
+        nc.gpsimd.tensor_tensor(grouped[0][:, :, LAST], last[0][:, 0, :], last[1][:, 1, :], SUBTRACT)
         for b in range(BLOCKS):
             turn_back(nc.scalar.copy, 1, b, keep.tile([P, P, 2], BF16, name="last_pairs%d" % b)[:])
-        nc.scalar.copy(grouped[0][:, 0:PLACED, 2:PACK], last_x[:].rearrange("p e q -> p q e"))
         for b in range(BLOCKS):
             words = grouped[1][:, b * P : (b + 1) * P, :].rearrange("p q t -> p (q t)").bitcast(F32).rearrange("p (q u) -> p q u", u=2)
             nc.scalar.copy(words, sums[b][:, 2:PACK, :].rearrange("p u q -> p q u"))
@@ -202,7 +191,7 @@ def tile_attend_complexscores_kernel(tc, hre, him, rre, rim, tre_words, tre_scal
             queries = slice(b * P, (b + 1) * P)
             nc.vector.quantize_mx(out=codes[s][:, b, :].bitcast(FP8X4), scales=query_scales[s][:, queries], in_=grouped[s][:, queries, :].rearrange("p q t -> p (q t)"))
 
-        pieces = [(0, HALF, 1), (0, HALF, 0), (HALF, P, 0), (HALF + P, P, 0), (HALF, P, 1), (HALF + P, P, 1)]
+        pieces = [(0, HALF, 0), (0, HALF, 1), (HALF, P, 0), (HALF + P, P, 0), (HALF, P, 1), (HALF + P, P, 1)]
         scores = {piece: psum.tile([P, piece[1]], F32, name="scores%d" % n) for n, piece in enumerate(pieces)}
 
         def multiply(piece, s, words, words_first):
@@ -237,7 +226,7 @@ def tile_attend_complexscores_kernel(tc, hre, him, rre, rim, tre_words, tre_scal
                 nc.sync.dma_start(out[b * P : (b + 1) * P, h * HALF : (h + 1) * HALF], results[h, b][:])
 
         gather_words(real_words, 0, 0, I)
-        for b in (1, 0):
+        for b in range(BLOCKS):
             quantise(0, b)
             for piece in pieces:
                 if piece[2] == b:

@@ -45,8 +45,8 @@ def tile_attend_complexscores_kernel(tc, hre, him, rre, rim, tre_words, tre_scal
         tail_list = lists.tile([P, I // LIST_GROUP], U16, name="tail_list")
 
         scale_table = [keep.tile([P, V], U8, name="scale_table%d" % c) for c in range(PARTS)]
-        for c in range(PARTS):
-            nc.vector.memset(scale_table[c][:].bitcast(I32), 0)
+        for c, engine in enumerate((nc.gpsimd, nc.vector)):
+            engine.memset(scale_table[c][:].bitcast(I32), 0)
         tail_scales = keep.tile([P, PARTS * I], U8, name="tail_scales", align_bytes=MX_ALIGN)
         ident = keep.tile([P, P], F32, name="ident")
         make_identity(nc, ident[:])
@@ -71,20 +71,20 @@ def tile_attend_complexscores_kernel(tc, hre, him, rre, rim, tre_words, tre_scal
         nc.sync.dma_start(rel_list[:], offs2)
         nc.sync.dma_start(tail_list[:], offs3)
         nc.sync.dma_start(head_list[:], offs)
-        load_planes(rel_table, rre, 0, 0, 2, nc.scalar)
+        load_planes(rel_table, rre, 0, 0, LAST, nc.scalar)
         load_scales(0, tre_scales)
-        load_planes(rel_table, rim, 1, 0, 2)
         load_scales(1, tim_scales)
-        load_planes(head_table, hre, 0, 0, 2)
-        load_planes(head_table, him, 1, 0, 2)
-        load_planes(rel_table, rre, 0, 2, 2)
-        load_planes(rel_table, rim, 1, 2, 2)
-        for t in (2, LAST):
-            load_planes(head_table, hre, 0, t, 1)
-            load_planes(head_table, him, 1, t, 1)
+        load_planes(rel_table, rim, 1, 0, LAST)
+        for first, count in ((0, 2), (2, 1)):
+            load_planes(head_table, hre, 0, first, count)
+            load_planes(head_table, him, 1, first, count)
+        load_planes(rel_table, rre, 0, LAST, 1)
+        load_planes(rel_table, rim, 1, LAST, 1)
+        load_planes(head_table, hre, 0, LAST, 1)
+        load_planes(head_table, him, 1, LAST, 1)
 
-        relp = [keep.tile([P, PARTS, 2, Q], F32, name="relp%d" % u) for u in range(2)]
-        head = {(c, t): keep.tile([P, Q], F32, name="head%d_%d" % (c, t)) for c in range(PARTS) for t in range(PACK)}
+        rel = [keep.tile([P, PARTS, Q], F32, name="rel%d" % t) for t in range(PACK)]
+        head = {(c, t): keep.tile([P, Q], F32, name="head%d_%d" % (c, t), tag="head%d_%d" % (c, t)) for c in range(PARTS) for t in range(PACK)}
         early = [keep.tile([P, PARTS, LAST, Q], F32, name="early%d" % c, align_bytes=MX_ALIGN) for c in range(PARTS)]
         last = [keep.tile([P, PARTS, Q], F32, name="last%d" % c, align_bytes=MX_ALIGN) for c in range(PARTS)]
         grouped = [keep.tile([P, Q, PACK], BF16, name="grouped%d" % s, align_bytes=MX_ALIGN) for s in range(PARTS)]
@@ -99,23 +99,21 @@ def tile_attend_complexscores_kernel(tc, hre, him, rre, rim, tre_words, tre_scal
             else:
                 nc.scalar.activation(dest, window.indirect(offsets), COPY)
 
-        def gather_rel(r, u):
-            for e in range(2):
-                gather(e == 1, relp[u][:, r, e, :], rel_table[r, 2 * u + e], rel_list[:])
+        def gather_rel(r, planes):
+            for t in planes:
+                gather(t > 0 and (r, t) != (0, LAST), rel[t][:, r, :], rel_table[r, t], rel_list[:])
 
         def gather_head(on_vector, c, t, first, count):
             gather(on_vector, head[c, t][:, first : first + count], head_table[c, t], head_list[:, first // LIST_GROUP : (first + count) // LIST_GROUP])
 
         def multiply_plane(c, t, first, count):
-            u, e = divmod(t, 2)
             queries = slice(first, first + count)
             both = last[c][:, :, queries] if t == LAST else early[c][:, :, t, queries]
-            nc.vector.tensor_tensor(both, relp[u][:, :, e, queries], head[c, t][:, queries].unsqueeze(1).to_broadcast([P, PARTS, count]), MULT)
+            nc.vector.tensor_tensor(both, rel[t][:, :, queries], head[c, t][:, queries].unsqueeze(1).to_broadcast([P, PARTS, count]), MULT)
 
         def multiply_part(c, t, r, first, count):
-            u, e = divmod(t, 2)
             queries = slice(first, first + count)
-            nc.vector.tensor_tensor(term(c, r, t, queries), relp[u][:, r, e, queries], head[c, t][:, queries], MULT)
+            nc.vector.tensor_tensor(term(c, r, t, queries), rel[t][:, r, queries], head[c, t][:, queries], MULT)
 
         def add_term(b, t, c, start, stop):
             nc.tensor.matmul(sums[b][:, t % 2, :], lhsT=term(c, 1 - c, t, slice(b * P, (b + 1) * P)), rhs=ident[:], is_transpose=True, start=start, stop=stop)
@@ -125,9 +123,10 @@ def tile_attend_complexscores_kernel(tc, hre, him, rre, rim, tre_words, tre_scal
             nc.tensor.transpose(sums[b][:, 2 + u, :], pairs.rearrange("q p e -> q (p e)").bitcast(F32), ident[:])
 
         for r in range(PARTS):
-            gather_rel(r, 0)
             nc.vector.tensor_copy(picked_scales[:, r * I : (r + 1) * I], scale_table[r][:].indirect(tail_list[:]))
+        gather_rel(0, range(LAST))
         nc.vector.tensor_copy(tail_scales[:].bitcast(I32), picked_scales[:].bitcast(I32))
+        gather_rel(1, range(LAST))
         for c, table in enumerate((tre_words, tim_words)):
             nc.sync.dma_start(word_table[c][:].bitcast(I32), table[0].bitcast(I32))
         for r in range(1, QUADRANT // SPREAD):
@@ -135,24 +134,24 @@ def tile_attend_complexscores_kernel(tc, hre, him, rre, rim, tre_words, tre_scal
 
         for c in range(PARTS):
             for t in range(2):
-                gather_head(t > 0, c, t, 0, Q)
+                gather_head((c, t) == (1, 1), c, t, 0, Q)
             for t in range(2):
                 multiply_plane(c, t, 0, Q)
         for c in range(PARTS):
             for t in range(2):
                 for b in range(BLOCKS):
                     add_term(b, t, c, (c, t) == (0, 0), (c, t) == (1, 1))
-        for r in range(PARTS):
-            gather_rel(r, 1)
 
         gather_head(False, 0, 2, 0, Q)
-        turn_back(nc.scalar.copy, 0, 0, keep.tile([P, P, 2], BF16, name="first_pairs0", tag="table%d_0_2" % T, align_bytes=MX_ALIGN)[:])
         multiply_plane(0, 2, 0, Q)
         for b in range(BLOCKS):
             gather_head(False, 1, 2, b * P, P)
-        turn_back(nc.scalar.copy, 0, 1, keep.tile([P, P, 2], BF16, name="first_pairs1", tag="table%d_1_2" % T, align_bytes=MX_ALIGN)[:])
+        gather_rel(0, [LAST])
+        turn_back(nc.scalar.copy, 0, 1, keep.tile([P, P, 2], BF16, name="first_pairs1", tag="table%d_0_%d" % (U, LAST), align_bytes=MX_ALIGN)[:])
         for b in range(BLOCKS):
             multiply_plane(1, 2, b * P, P)
+        turn_back(nc.vector.tensor_copy, 0, 0, keep.tile([P, P, 2], BF16, name="first_pairs0", tag="head1_2")[:])
+        gather_rel(1, [LAST])
         for b in range(BLOCKS):
             queries = slice(b * P, (b + 1) * P)
             nc.vector.tensor_tensor(

@@ -45,8 +45,8 @@ def tile_attend_complexscores_kernel(tc, hre, him, rre, rim, tre_words, tre_scal
         tail_list = lists.tile([P, I // LIST_GROUP], U16, name="tail_list")
 
         scale_table = [keep.tile([P, V], U8, name="scale_table%d" % c) for c in range(PARTS)]
-        for c, engine in enumerate((nc.gpsimd, nc.vector)):
-            engine.memset(scale_table[c][:].bitcast(I32), 0)
+        for c in range(PARTS):
+            nc.vector.memset(scale_table[c][:].bitcast(I32), 0)
         tail_scales = keep.tile([P, PARTS * I], U8, name="tail_scales", align_bytes=MX_ALIGN)
         ident = keep.tile([P, P], F32, name="ident")
         make_identity(nc, ident[:])
@@ -73,8 +73,8 @@ def tile_attend_complexscores_kernel(tc, hre, him, rre, rim, tre_words, tre_scal
         nc.sync.dma_start(head_list[:], offs)
         load_planes(rel_table, rre, 0, 0, LAST, nc.scalar)
         load_scales(0, tre_scales)
-        load_scales(1, tim_scales)
         load_planes(rel_table, rim, 1, 0, LAST)
+        load_scales(1, tim_scales)
         for first, count in ((0, 2), (2, 1)):
             load_planes(head_table, hre, 0, first, count)
             load_planes(head_table, him, 1, first, count)
@@ -123,10 +123,9 @@ def tile_attend_complexscores_kernel(tc, hre, him, rre, rim, tre_words, tre_scal
             nc.tensor.transpose(sums[b][:, 2 + u, :], pairs.rearrange("q p e -> q (p e)").bitcast(F32), ident[:])
 
         for r in range(PARTS):
+            gather_rel(r, range(LAST))
             nc.vector.tensor_copy(picked_scales[:, r * I : (r + 1) * I], scale_table[r][:].indirect(tail_list[:]))
-        gather_rel(0, range(LAST))
         nc.vector.tensor_copy(tail_scales[:].bitcast(I32), picked_scales[:].bitcast(I32))
-        gather_rel(1, range(LAST))
         for c, table in enumerate((tre_words, tim_words)):
             nc.sync.dma_start(word_table[c][:].bitcast(I32), table[0].bitcast(I32))
         for r in range(1, QUADRANT // SPREAD):

from contextlib import ExitStack

import concourse.mybir as mybir
from concourse.masks import make_identity

D, T, U, Q, V, I = 512, 1024, 512, 256, 2048, 512
FLOPS = 2 * 2 * D * Q * I

F32 = mybir.dt.float32
BF16 = mybir.dt.bfloat16
I32 = mybir.dt.int32
U32 = mybir.dt.uint32
U16 = mybir.dt.uint16
U8 = mybir.dt.uint8
FP8X4 = mybir.dt.float8_e4m3fn_x4
FP4X4 = mybir.dt.float4_e2m1fn_x4
MULT = mybir.AluOpType.mult
SUBTRACT = mybir.AluOpType.subtract
COPY = mybir.ActivationFunctionType.Copy

P = 128
BLOCKS = Q // P
PARTS = 2
PACK = 4
LAST = PACK - 1
LIST_GROUP = 16
QUADRANT = 32
SCALE_ROWS = D // 32
SPREAD = P // SCALE_ROWS
MX_ALIGN = 64
HALF = I // 2
VECTOR_SHARE = 64


def tile_attend_complexscores_kernel(tc, hre, him, rre, rim, tre_words, tre_scales, tim_words, tim_scales, offs, offs2, offs3, out):
    nc = tc.nc
    with ExitStack() as ctx:
        lists = ctx.enter_context(tc.tile_pool(name="lists", bufs=1))
        keep = ctx.enter_context(tc.tile_pool(name="keep", bufs=1))
        shared = ctx.enter_context(tc.tile_pool(name="shared", bufs=1))
        psum = ctx.enter_context(tc.psum_pool(name="psum", bufs=1))

        head_list = lists.tile([P, Q // LIST_GROUP], U16, name="head_list")
        rel_list = lists.tile([P, Q // LIST_GROUP], U16, name="rel_list")
        tail_list = lists.tile([P, I // LIST_GROUP], U16, name="tail_list")

        scale_table = [keep.tile([P, V], U8, name="scale_table%d" % c) for c in range(PARTS)]
        for c in range(PARTS):
            nc.vector.memset(scale_table[c][:].bitcast(I32), 0)
        tail_scales = keep.tile([P, PARTS * I], U8, name="tail_scales", align_bytes=MX_ALIGN)
        ident = keep.tile([P, P], F32, name="ident")
        make_identity(nc, ident[:])

        word_table = [keep.tile([P, V], U16, name="word_table%d" % c, align_bytes=MX_ALIGN) for c in range(PARTS)]
        picked_scales = shared.tile([P, PARTS * I], U8, name="picked_scales", align_bytes=MX_ALIGN, offset=PARTS * I // 2)
        rel_table, head_table = {}, {}

        def load_planes(windows, table, c, first, count, queue=nc.sync):
            width = table.shape[1]
            name = "table%d_%d_%d" % (width, c, first)
            tile = keep.tile([P, count, width], F32, name=name, tag=name, align_bytes=MX_ALIGN)
            queue.dma_start(tile[:], table.rearrange("(p t) w -> p t w", t=PACK)[:, first : first + count, :])
            for n in range(count):
                windows[c, first + n] = tile[:, n, :]
            if width == U:
                windows[c, first] = tile[:].rearrange("p t w -> p (t w)")

        def load_scales(c, table):
            nc.sync.dma_start(scale_table[c][0:P:SPREAD, :].bitcast(I32), table[0].bitcast(I32))

        nc.sync.dma_start(rel_list[:], offs2)
        nc.sync.dma_start(tail_list[:], offs3)
        nc.sync.dma_start(head_list[:], offs)
        load_planes(rel_table, rre, 0, 0, LAST, nc.scalar)
        load_scales(0, tre_scales)
        load_planes(rel_table, rim, 1, 0, LAST)
        load_scales(1, tim_scales)
        for first, count in ((0, 2), (2, 1)):
            load_planes(head_table, hre, 0, first, count)
            load_planes(head_table, him, 1, first, count)
        load_planes(rel_table, rre, 0, LAST, 1)
        load_planes(rel_table, rim, 1, LAST, 1)
        load_planes(head_table, hre, 0, LAST, 1)
        load_planes(head_table, him, 1, LAST, 1)

        rel = [keep.tile([P, PARTS, Q], F32, name="rel%d" % t) for t in range(PACK)]
        head = {(c, t): keep.tile([P, Q], F32, name="head%d_%d" % (c, t), tag="head%d_%d" % (c, t)) for c in range(PARTS) for t in range(PACK)}
        early = [keep.tile([P, PARTS, LAST, Q], F32, name="early%d" % c, align_bytes=MX_ALIGN) for c in range(PARTS)]
        last = [keep.tile([P, PARTS, Q], F32, name="last%d" % c, align_bytes=MX_ALIGN) for c in range(PARTS)]
        grouped = [keep.tile([P, Q, PACK], BF16, name="grouped%d" % s, align_bytes=MX_ALIGN) for s in range(PARTS)]
        sums = [psum.tile([P, PACK, P], F32, name="sums%d" % b) for b in range(BLOCKS)]

        def term(c, r, t, queries):
            return last[c][:, r, queries] if t == LAST else early[c][:, r, t, queries]

        def gather(on_vector, dest, window, offsets):
            if on_vector:
                nc.vector.tensor_copy(dest, window.indirect(offsets))
            else:
                nc.scalar.activation(dest, window.indirect(offsets), COPY)

        def gather_rel(r, planes):
            for t in planes:
                gather(t > 0 and (r, t) != (0, LAST), rel[t][:, r, :], rel_table[r, t], rel_list[:])

        def gather_head(on_vector, c, t, first, count):
            gather(on_vector, head[c, t][:, first : first + count], head_table[c, t], head_list[:, first // LIST_GROUP : (first + count) // LIST_GROUP])

        def multiply_plane(c, t, first, count):
            queries = slice(first, first + count)
            both = last[c][:, :, queries] if t == LAST else early[c][:, :, t, queries]
            nc.vector.tensor_tensor(both, rel[t][:, :, queries], head[c, t][:, queries].unsqueeze(1).to_broadcast([P, PARTS, count]), MULT)

        def multiply_part(c, t, r, first, count):
            queries = slice(first, first + count)
            nc.vector.tensor_tensor(term(c, r, t, queries), rel[t][:, r, queries], head[c, t][:, queries], MULT)

        def add_term(b, t, c, start, stop):
            nc.tensor.matmul(sums[b][:, t % 2, :], lhsT=term(c, 1 - c, t, slice(b * P, (b + 1) * P)), rhs=ident[:], is_transpose=True, start=start, stop=stop)

        def turn_back(copy, u, b, pairs):
            copy(pairs, sums[b][:, 0:2, :].rearrange("q e p -> q p e"))
            nc.tensor.transpose(sums[b][:, 2 + u, :], pairs.rearrange("q p e -> q (p e)").bitcast(F32), ident[:])

        for r in range(PARTS):
            gather_rel(r, range(LAST))
            nc.vector.tensor_copy(picked_scales[:, r * I : (r + 1) * I], scale_table[r][:].indirect(tail_list[:]))
        nc.vector.tensor_copy(tail_scales[:].bitcast(I32), picked_scales[:].bitcast(I32))
        for c, table in enumerate((tre_words, tim_words)):
            nc.sync.dma_start(word_table[c][:].bitcast(I32), table[0].bitcast(I32))
        for r in range(1, QUADRANT // SPREAD):
            nc.sync.dma_start(tail_scales[r:P:QUADRANT, :].bitcast(I32), picked_scales[SPREAD * r : P : QUADRANT, :].bitcast(I32))

        for c in range(PARTS):
            for t in range(2):
                gather_head((c, t) == (1, 1), c, t, 0, Q)
            for t in range(2):
                multiply_plane(c, t, 0, Q)
        for c in range(PARTS):
            for t in range(2):
                for b in range(BLOCKS):
                    add_term(b, t, c, (c, t) == (0, 0), (c, t) == (1, 1))

        gather_head(False, 0, 2, 0, Q)
        multiply_plane(0, 2, 0, Q)
        for b in range(BLOCKS):
            gather_head(False, 1, 2, b * P, P)
        gather_rel(0, [LAST])
        turn_back(nc.scalar.copy, 0, 1, keep.tile([P, P, 2], BF16, name="first_pairs1", tag="table%d_0_%d" % (U, LAST), align_bytes=MX_ALIGN)[:])
        for b in range(BLOCKS):
            multiply_plane(1, 2, b * P, P)
        turn_back(nc.vector.tensor_copy, 0, 0, keep.tile([P, P, 2], BF16, name="first_pairs0", tag="head1_2")[:])
        gather_rel(1, [LAST])
        for b in range(BLOCKS):
            queries = slice(b * P, (b + 1) * P)
            nc.vector.tensor_tensor(
                grouped[0][:, queries, :].rearrange("p (n i) t -> p n t i", i=2)[:, :, 0:LAST, :],
                early[0][:, 0, :, queries].rearrange("p t (n i) -> p n t i", i=2),
                early[1][:, 1, :, queries].rearrange("p t (n i) -> p n t i", i=2),
                SUBTRACT,
            )
        for b in range(BLOCKS):
            for c in range(PARTS):
                add_term(b, 2, c, c == 0, c == 1)
        for b in range(BLOCKS):
            gather_head(False, 0, LAST, b * P, P)
            multiply_plane(0, LAST, b * P, P)
            add_term(b, LAST, 0, True, False)

        gather_head(False, 1, LAST, 0, P)
        multiply_plane(1, LAST, 0, P)
        add_term(0, LAST, 1, False, True)
        gather_head(False, 1, LAST, P, P - VECTOR_SHARE)
        gather_head(True, 1, LAST, Q - VECTOR_SHARE, VECTOR_SHARE)
        for r in (1, 0):
            multiply_part(1, LAST, r, P, P)
        add_term(1, LAST, 1, False, True)
        nc.gpsimd.tensor_tensor(grouped[0][:, :, LAST], last[0][:, 0, :], last[1][:, 1, :], SUBTRACT)
        for b in range(BLOCKS):
            turn_back(nc.scalar.copy, 1, b, keep.tile([P, P, 2], BF16, name="last_pairs%d" % b)[:])
        for b in range(BLOCKS):
            words = grouped[1][:, b * P : (b + 1) * P, :].rearrange("p q t -> p (q t)").bitcast(F32).rearrange("p (q u) -> p q u", u=2)
            nc.scalar.copy(words, sums[b][:, 2:PACK, :].rearrange("p u q -> p q u"))

        def gather_words(tile, c, first, count):
            nc.vector.tensor_copy(tile[:], word_table[c][:].indirect(tail_list[:, first // LIST_GROUP : (first + count) // LIST_GROUP]))

        def quantise(s, b):
            queries = slice(b * P, (b + 1) * P)
            nc.vector.quantize_mx(out=codes[s][:, b, :].bitcast(FP8X4), scales=query_scales[s][:, queries], in_=grouped[s][:, queries, :].rearrange("p q t -> p (q t)"))

        pieces = [(0, HALF, 0), (0, HALF, 1), (HALF, P, 0), (HALF + P, P, 0), (HALF, P, 1), (HALF + P, P, 1)]
        scores = {piece: psum.tile([P, piece[1]], F32, name="scores%d" % n) for n, piece in enumerate(pieces)}

        def multiply(piece, s, words, words_first):
            first, width, b = piece
            queries = slice(b * P, (b + 1) * P)
            nc.tensor.matmul_mx(
                out=scores[piece][:],
                lhsT=codes[s][:, b, :].bitcast(FP8X4),
                lhsT_scale=query_scales[s][:, queries],
                rhs=words[:, first - words_first : first - words_first + width].bitcast(FP4X4),
                rhs_scale=tail_scales[:, s * I + first : s * I + first + width],
                start=(s == 0),
                stop=(s == PARTS - 1),
            )

        real_words = keep.tile([P, I], U16, name="real_words", align_bytes=MX_ALIGN)
        imag_words = [keep.tile([P, HALF], U16, name="imag_words0", align_bytes=MX_ALIGN)]
        codes = [
            keep.tile([P, BLOCKS, P], U32, name="codes0", align_bytes=MX_ALIGN),
            shared.tile([P, BLOCKS, P], U32, name="codes1", align_bytes=MX_ALIGN, offset=0),
        ]
        query_scales = [keep.tile([P, Q], U8, name="query_scales%d" % s, align_bytes=MX_ALIGN) for s in range(PARTS)]
        results = {(h, b): keep.tile([P, HALF], F32, name="result%d_%d" % (h, b)) for h in range(2) for b in range(BLOCKS)}

        def finish(piece):
            first, width, b = piece
            h, offset = divmod(first, HALF)
            multiply(piece, 1, imag_words[h], h * HALF)
            copy = nc.vector.tensor_copy if offset else nc.scalar.copy
            copy(results[h, b][:, offset : offset + width], scores[piece][:])
            if offset + width == HALF:
                nc.sync.dma_start(out[b * P : (b + 1) * P, h * HALF : (h + 1) * HALF], results[h, b][:])

        gather_words(real_words, 0, 0, I)
        for b in range(BLOCKS):
            quantise(0, b)
            for piece in pieces:
                if piece[2] == b:
                    multiply(piece, 0, real_words, 0)
        gather_words(imag_words[0], 1, 0, HALF)
        for b in range(BLOCKS):
            quantise(1, b)
            finish((0, HALF, b))
        imag_words.append(shared.tile([P, HALF], U16, name="imag_words1", align_bytes=MX_ALIGN, offset=PARTS * I))
        gather_words(imag_words[1], 1, HALF, HALF)
        for b in range(BLOCKS):
            for first in (HALF, HALF + P):
                finish((first, P, b))
